import numpy as np, ml_dtypes
CORES = [25,29,65,69,153,157,193,197]
N = 8
import mx_ref
BF = ml_dtypes.bfloat16
def gentries(a):
    return np.ascontiguousarray(a.reshape(8, 16, -1).transpose(0, 2, 1)).reshape(8, -1)
def gtable(e):
    e = np.asarray(e); return np.ascontiguousarray(e.reshape(8, -1, 16).transpose(0, 2, 1)).reshape(128, -1).astype(np.int32)
def gcols(t, e):
    v = np.concatenate([t.reshape(8, 16, -1, 4), np.zeros((8, 16, 1, 4), BF)], axis=2)
    return np.ascontiguousarray(np.stack([v[g][:, e[g]] for g in range(8)])).reshape(128, -1)
def tile(rs):
    return np.stack(rs, axis=2).reshape(128, -1).astype(BF)
def pick(q, e):
    c = np.concatenate([q[0].reshape(128, -1, 4), np.zeros((128, 1, 4), np.uint8)], axis=1); s = np.concatenate([q[1], np.ones((16, 1), np.uint8)], axis=1)
    return (np.ascontiguousarray(c[:, e].reshape(128, -1)), np.ascontiguousarray(s[:, e]))
def join(*qs):
    return (np.concatenate([q[0] for q in qs], axis=1), np.concatenate([q[1] for q in qs], axis=1))
def put(q, e, v):
    c, s = q[0].reshape(128, -1, 4).copy(), q[1].copy(); c[:, e] = v[0].reshape(128, -1, 4); s[:, e] = v[1]
    return (c.reshape(128, -1), s)
def pk(c, s):
    return (np.ascontiguousarray(c), mx_ref.live(s))
def emit(q):
    return q[0], q[1]
def packed(v, rng):
    q = [mx_ref.quantize(np.ascontiguousarray(v[r])) for r in range(N)]
    return np.stack([a for a, b in q]), np.stack([mx_ref.plane(b, rng) for a, b in q])
def values_of_codes():
    e, c = np.zeros((128, 128, 4), np.float32), np.zeros((128, 2, 4), np.uint8)
    e[np.arange(128), np.arange(128), 0] = 1
    c[:127, :, 0] = np.arange(256).reshape(2, 128).T[:127]
    return mx_ref.matmul(mx_ref.quantize(e.reshape(128, 512).astype(BF)), (c.reshape(128, 8), np.full((16, 2), 127, np.uint8))).T.reshape(-1).astype(np.float64)
CODE_VALUE, SCALE_VALUE = values_of_codes(), 2.0 ** (np.arange(256) - 127.0)
def decode(q):
    return (CODE_VALUE[q[0]].reshape(16, 8, -1, 4) * SCALE_VALUE[q[1]][:, None, :, None] + 0.0).reshape(128, -1).astype(np.float32)
def f(rng, *shape):
    return mx_ref.flush((rng.standard_normal(shape, dtype=np.float32) * np.exp2(rng.integers(-2, 3, shape[:-1] + (1,)))).astype(BF))
def wide(rng, *shape, cols=0):
    v = rng.standard_normal(shape, dtype=np.float32) * np.exp2(rng.integers(-12, 13, shape)).astype(np.float32)
    if cols: v *= np.repeat(np.exp2(rng.integers(-cols, cols + 1, shape[:-2] + (1, shape[-1] // 4))) * (rng.random(shape[:-2] + (1, shape[-1] // 4)) > 0.0625), 4, axis=-1).astype(np.float32)
    return mx_ref.flush(v.astype(BF))
C, H = 352, 176
STEP = [4, 1, 2]
PLACES = np.arange(C)
def numbers_of(rng):
    return {"x": np.array(f(rng, N, 128, 4 * C)), "u": np.array(f(rng, N, 128, 512)), "v": np.array(f(rng, N, 128, 512))}
def drawn(rng):
    o = rng.permuted(np.tile(PLACES, (N, 8, 3, 1)), axis=3)
    k = np.zeros_like(o)
    np.put_along_axis(k, o, o.reshape(N, 8, 3, H, 2)[..., ::-1].reshape(N, 8, 3, C), axis=3)
    e = np.tile(PLACES, (N, 8, 1))
    return rng.permuted(e, axis=2), rng.permuted(e, axis=2), k
def stored(p, e, k):
    return {"pp": np.stack([gtable(p[r]) for r in range(N)]), "rf": np.stack([gtable(e[r]) for r in range(N)]), "pr": np.stack([gtable(k[r].reshape(8, 3 * C)) for r in range(N)])}
def layers(rng, still=[]):
    w = np.array(f(rng, N, 128, 2048)).reshape(N, 8, 16, 4, 8, 16, 4)
    for i in still:
        w[:, :, i] = 0
        w[:, :, :, :, :, i] = 0
    return w
def weights(rng, w):
    c, s = packed(np.ascontiguousarray(w).reshape(N, 128, 2048), rng)
    return {"wc": c, "ws": s}
def scoring(d):
    u = d["u"].reshape(N, 128, 128, 4)
    u[:, :, ::16] = 0
    u[:, :, 1::16] = 0
    return u
def setup_inputs(rng):
    return {**numbers_of(rng), **stored(*drawn(rng)), **weights(rng, layers(rng))}
def setup_inputs_ties(rng):
    d = numbers_of(rng)
    p, e, k = drawn(rng)
    o = rng.permutation(N)
    k[o[3], :4] = k[o[3], :4, :1]
    a, b = rng.integers(-1, 2, (2, N, 8, C))
    a[o[0]] = 0
    a[o[1]] = 1
    b[o[1], :4] = 1
    b[o[1], 4:] = 0
    for g in range(4): a[o[3], g, p[o[3], g]] = np.where(PLACES < k[o[3], g, 0], 1, -rng.integers(0, 2, C))
    x = d["x"].reshape(N, 8, 16, C, 4)
    x[:, :, 0] = 0
    x[:, :, 0, :, 0] = a.astype(np.float32).astype(BF)
    x[:, :, 0, :, 1] = b.astype(np.float32).astype(BF)
    u = scoring(d)
    for h in range(0, 128, 16):
        u[:, h, h, 0] = 1
        u[:, h, h + 1, 1] = 1
    return {"x": x.reshape(N, 128, 4 * C), "u": u.reshape(N, 128, 512), "v": d["v"], **stored(p, rng.integers(0, C, (N, 8, C)), k), **weights(rng, layers(rng, [0]))}
def setup_inputs_near(rng):
    d = numbers_of(rng)
    o = rng.permutation(N)
    z = int(np.argmax(o))
    k = np.where(o % 2 == 0, 2.0 ** -30, 1.0)
    x = np.zeros((N, 8, 16, C, 4))
    for i in (0, 2):
        s = rng.integers(-1, 2, (N, 8, C)) * k[:, None, None]
        x[:, :, i, :, 0] = 1.125 * s
        x[:, :, i + 1, :, 0] = -1.25 * s
    for r in range(N):
        at_ = [0, C - 1, int(rng.integers(C)), int(rng.integers(C))]
        for g, j in zip(rng.permutation(8)[:4], at_): x[r, g, 0, j, 0] = 2.0 ** 30 * rng.choice([-1.0, 1.0])
    x[:, :, 8:] = rng.choice([-1.0, 1.0], (N, 8, 8, C, 4)) * (1 + 0.125 * rng.integers(0, 8, (N, 8, 8, C, 4))) * 2.0 ** -30
    x[z, :, :8] = 0
    x[:, :, 7, :, 0] = 2.0 ** -30
    x[:, :, 8, :, 3] = 2.0 ** -30
    u = scoring(d)
    w = layers(rng)
    w[:, :, :8] = 0
    w[:, :, :, :, :, :9] = 0
    for h in range(0, 128, 16):
        for i in (0, 1):
            u[:, h + 2 * i, h + i, 0] = (1.125 * k).astype(np.float32).astype(BF)
            u[:, h + 2 * i + 1, h + i, 0] = k.astype(np.float32).astype(BF)
            u[z, :, h + i] = 0
            u[z, h + 5 + i, h + i, 0] = 2.0 ** -30
            w[z, h // 16, 8, 0, h // 16, 5 + i, i] = 2.0 ** -8
    return {"x": x.astype(np.float32).reshape(N, 128, 4 * C).astype(BF), "u": u.reshape(N, 128, 512), "v": d["v"], **stored(*drawn(rng)), **weights(rng, w)}
def setup_inputs_odd(rng):
    d = numbers_of(rng)
    x = (2 * rng.integers(0, 8, (N, 16, 8, C, 4)) + 1) * 2.0 ** -8 * rng.choice([-1.0, 1.0], (N, 16, 8, C, 4))
    x[:, :, 0, :, 0] = 2.0 ** 8 * np.where(rng.random((N, 16, C)) < 0.5, 1.96875, 1.875)
    u = scoring(d)
    for i in (0, 1):
        x[:, ::2, 1 + 2 * i, :, 0] = (8 + rng.integers(0, 2, (N, 8, C))) * 2.0 ** -8
        x[:, ::2, 2 + 2 * i, :, 0] = 8 * 2.0 ** -8
        for h in range(0, 128, 16):
            u[:, h + 1 + 2 * i, h + i, 0] = 1
            u[:, h + 2 + 2 * i, h + i, 0] = -1
    return {"x": x.astype(np.float32).reshape(N, 128, 4 * C).astype(BF), "u": u.reshape(N, 128, 512), "v": d["v"], **stored(*drawn(rng)), **weights(rng, layers(rng, [0, 1, 2, 3, 4, 8]))}
def setup_inputs_ends(rng):
    d = numbers_of(rng)
    p, q, k = drawn(rng)
    o, e = rng.permutation(N) % 4, rng.permutation(N) % 4
    s = rng.choice([-1.0, 1.0], (N, 128, C, 4))
    s[o == 0] = -1
    s[o == 1] = rng.choice([-1.0, 1.0], (N, 1, C, 1))[o == 1]
    x = s * (0.87 + 0.07 * rng.random((N, 128, C, 4))) * 2.0 ** 30
    x[:, 15::16] = 0
    x[o == 3] = 2.0 ** -30
    size = np.where(o == 3, 2.0 ** -30, 2.0 ** 30)
    u = scoring(d)
    for i in (0, 1):
        a = np.stack([rng.permutation(8) % 2 * 2.0 - 1.0 for r in range(N)]) * size[:, None]
        u[:, :, i::16] = a.astype(np.float32).astype(BF)[:, None, :, None]
    v = rng.choice([-1.0, 1.0], (N, 128, 512)) * np.where(o % 2 == 1, 2.0 ** -30, 2.0 ** 30)[:, None, None]
    p[e == 0] = PLACES
    p[e == 1] = PLACES[::-1]
    q[e == 0] = np.where(np.arange(8) % 2 == 0, C - 1, 0)[:, None]
    q[e == 1] = (rng.integers(0, 2, (N, 8, C)) * (C - 1))[e == 1]
    q[e == 2] = PLACES
    q[e == 3] = rng.integers(0, C, (N, 8, C))[e == 3]
    k[e == 0] = PLACES
    k[e == 1] = PLACES[::-1]
    k[e == 2] = PLACES ^ 1
    w = np.zeros((N, 128, 4, 128, 4), np.float32)
    i = np.arange(128)
    for b in range(4): w[:, i, b, i, b] = np.where(o[:, None] == 3, np.where(i % 16 == 15, 2.0 ** 8, 2.0 ** -8), -0.25)
    return {"x": x.astype(np.float32).reshape(N, 128, 4 * C).astype(BF), "u": u.reshape(N, 128, 512), "v": v.astype(np.float32).astype(BF), **stored(p, q, k), **weights(rng, w.astype(BF))}
def setup_inputs_spread(rng):
    d = setup_inputs(rng)
    d["x"] = wide(rng, N, 128, 4 * C, cols=6)
    return d
def check_inputs(d):
    b = []
    for k in ("x", "u", "v"):
        a = np.abs(d[k].astype(np.float32))
        if not (np.isfinite(a).all() and ((a == 0) | (a >= 2.0 ** -30) & (a <= 2.0 ** 30)).all()): b.append("a value of " + k)
    for k in ("pp", "rf", "pr"):
        if not ((d[k] >= 0) & (d[k] < C)).all(): b.append("an entry of " + k)
    none, least, most = [emit(mx_ref.quantize(np.full((128, 16), k, np.float32).astype(BF)))[1][0, 0] for k in (0.0, 2.0 ** -8, 2.0 ** 8)]
    for r in range(N):
        if not (np.sort(gentries(d["pp"][r]), axis=1) == PLACES).all(): b.append("pp: a column not once in a group")
        k = gentries(d["pr"][r]).reshape(8, 3, C)
        if ((k >= 0) & (k < C)).all() and not (np.take_along_axis(k, k, axis=2) == PLACES).all(): b.append("pr: a place that isn't the pair of its pair")
        if ((d["wc"][r] == 0x7F) | (d["wc"][r] == 0xFF)).any(): b.append("wc: a code that is no number")
        s = mx_ref.live(d["ws"][r])
        if ((s != none) & ((s < least) | (s > most))).any(): b.append("ws: a scale out of range")
        if (((d["wc"][r].reshape(16, 8, 512, 4) & 0x7F) != 0) & (s == none)[:, None, :, None]).any(): b.append("wc: a code other than zero under the scale of zeros")
    return b
def at(a, e):
    return np.take_along_axis(a, e, axis=1)
def layer(w, q):
    return tile([mx_ref.matmul(pick(w, np.arange(128 * b, 128 * b + 128)), q) * np.float32(0.03125) for b in range(4)])
def reference(x, u, v, pp, rf, pr, wc, ws):
    qu = [mx_ref.quantize(u[r]) for r in range(N)]
    lay = [pk(wc[r], ws[r]) for r in range(N)]
    place, refs = [gentries(pp[r]) for r in range(N)], [gentries(rf[r]) for r in range(N)]
    pair = [gentries(pr[r]).reshape(8, 3, C) for r in range(N)]
    now = [x[r] for r in range(N)]
    for t, step in enumerate(STEP):
        held, mix = [], []
        for r in range(N):
            q = mx_ref.quantize(now[r])
            s = mx_ref.matmul(qu[r], q)
            sign, mode = s[::16] > 0, s[1::16] > 0
            held.append(decode(q))
            k, here = pair[r][:, t], at(sign, place[r])
            swap = np.where(here == at(here, k), k, PLACES)
            place[r] = at(place[r], swap)
            old = at(refs[r], swap)
            refs[r] = np.where(at(mode, place[r]), at(swap, old), (old + PLACES - swap) % C)
            g = held[r].astype(BF)
            z = gcols(g, place[r]).astype(np.float32) + gcols(g, at(place[r], refs[r])).astype(np.float32)
            mix.append(mx_ref.quantize((z * np.float32(0.5)).astype(BF)))
        for r in range(N):
            h = layer(lay[r], join(pick(mix[r], np.arange(H)), pick(mix[r ^ step], np.arange(H, C))))
            inverse = np.argsort(place[r], axis=1)
            now[r] = (held[r] + gcols(h, at(refs[r ^ step], at(refs[r], inverse))).astype(np.float32)).astype(BF)
    y, pf = np.zeros((N, 128, C), np.float32), np.zeros((N, 8, 2 * C), np.float32)
    oc, osc = np.zeros((N, 128, 4 * C), np.uint8), np.zeros((N, 16, C), np.uint8)
    for r in range(N):
        q = mx_ref.quantize(now[r])
        y[r] = mx_ref.matmul(mx_ref.quantize(v[r]), q)
        pf[r] = np.concatenate([place[r], refs[r]], axis=1)
        oc[r], osc[r] = emit(q)
    return {"y": y, "pf": pf, "oc": oc, "osc": osc}

@@ -1,0 +1,506 @@
+from concourse.bass import DstId, RemoteDMATransfer
+from concourse.mybir import dt, AluOpType, ActivationFunctionType
+
+A, F = AluOpType, ActivationFunctionType
+N, C, H = 8, 352, 176
+STEP = [4, 1, 2]
+CH = [(0, 224), (224, 352)]
+SEQ = [("PFbpfTHOKh", "", "r"), ("PbpTHOh", "FK", "fr"), ("iOCcTEve", "", "")]
+CUT = ((0, 11), (11, 22))
+EARLY = ()
+POOL = ()
+EV = ()
+XS = [1, 1, 1]
+BIG = 16384.0
+
+SCRATCH = {
+    "xin": ("sbuf", [128, 4 * C], "bfloat16"), "xt": ("sbuf", [128, 4 * C], "bfloat16"),
+    "ut": ("sbuf", [128, 512], "bfloat16"), "vt": ("sbuf", [128, 512], "bfloat16"),
+    "uq": ("sbuf", [128, 128], "float8_e4m3fn_x4"), "us": ("sbuf", [128, 128], "uint8"),
+    "ua": ("sbuf", [128, 256], "float8_e4m3fn_x4"), "uas": ("sbuf", [128, 256], "uint8"),
+    "vq": ("sbuf", [128, 128], "float8_e4m3fn_x4"), "vs": ("sbuf", [128, 128], "uint8"),
+    "wq": ("sbuf", [128, 512], "float8_e4m3fn_x4"), "wsp": ("sbuf", [128, 512], "uint8"),
+    "one": ("sbuf", [128, 128], "bfloat16"), "gb": ("sbuf", [128, C], "bfloat16"), "gsb": ("sbuf", [128, C], "bfloat16"), "c0b": ("sbuf", [128, C], "bfloat16"),
+    "bg": ("sbuf", [128, 4 * C], "bfloat16"), "et": ("sbuf", [128, 2048], "bfloat16"),
+    "eq": ("sbuf", [128, 512], "float8_e4m3fn_x4"), "es": ("sbuf", [128, 512], "uint8"),
+    "ppi": ("sbuf", [128, 22], "int32"), "rfi": ("sbuf", [128, 22], "int32"), "pri": ("sbuf", [128, 66], "int32"),
+    "pp16": ("sbuf", [128, 22], "uint16"), "rf16": ("sbuf", [128, 22], "uint16"), "pr16": ("sbuf", [128, 66], "uint16"),
+    "idx": ("sbuf", [128, C], "float32"), "jm": ("sbuf", [128, C], "float32"), "mk": ("sbuf", [128, 2 * C], "float32"),
+    "ck": ("sbuf", [128, C], "float32"), "c01": ("sbuf", [128, C], "float32"),
+    "wt": ("sbuf", [128, 8], "float32"), "uo": ("sbuf", [128, 16], "uint16"),
+    "pm": ("sbuf", [128, 66], "int32"), "q16": ("sbuf", [128, 82], "int32"),
+    "qq": ("sbuf", [128, 66], "int32"), "qk": ("sbuf", [128, 66], "float32"),
+    "sa": ("sbuf", [128, C], "bfloat16"), "bw": ("sbuf", [128, 864], "float32"), "am": ("sbuf", [128, C], "float32"),
+    "sE": ("sbuf", [128, C], "float32"), "e3": ("sbuf", [128, 66], "float32"), "sm": ("sbuf", [128, 66], "float32"),
+    "gm": ("sbuf", [128, 2 * C], "float32"), "gs": ("sbuf", [128, 2 * C], "float32"),
+    "tt": ("sbuf", [128, 44], "float32"), "t3": ("sbuf", [128, 22], "int32"),
+    "pkf": ("sbuf", [128, 2 * C], "float32"), "sp": ("sbuf", [128, 2 * C], "float32"),
+    "x1": ("sbuf", [128, 66], "int32"), "xx": ("sbuf", [128, 22], "float32"), "nn": ("sbuf", [128, 22], "int32"),
+    "fsr": ("sbuf", [128, C], "float32"), "hr": ("sbuf", [128, C], "float32"), "ew": ("sbuf", [128, C], "float32"),
+    "esc": ("sbuf", [128, C], "float32"), "ei": ("sbuf", [128, 22], "int32"),
+    "fp": ("sbuf", [128, 4 * C], "bfloat16"), "gp": ("sbuf", [128, 4 * C], "bfloat16"), "bp": ("sbuf", [128, 4 * C], "bfloat16"),
+    "ztu": ("sbuf", [128, 4 * H], "bfloat16"), "ztl": ("sbuf", [128, 4 * H], "bfloat16"),
+    "yt": ("sbuf", [128, C], "float32"), "g2": ("sbuf", [128, 4 * C], "bfloat16"),
+}
+for k in range(8):
+    SCRATCH["b%d" % k] = ("psum", [128, 512], "float32")
+for k in range(4):
+    SCRATCH["xq%d" % k] = ("sbuf", [128, C], "float8_e4m3fn_x4")
+    SCRATCH["xs%d" % k] = ("sbuf", [128, C], "uint8")
+for k in range(3):
+    for nm in ("zu", "zl", "zr"):
+        SCRATCH["%sq%d" % (nm, k)] = ("sbuf", [128, H], "float8_e4m3fn_x4")
+        SCRATCH["%ss%d" % (nm, k)] = ("sbuf", [128, H], "uint8")
+    SCRATCH["oc%d" % k] = ("sbuf", [128, 44], "uint16")
+    SCRATCH["f16%d" % k] = ("sbuf", [128, 22], "uint16")
+    SCRATCH["fs%d" % k] = ("sbuf", [128, 22], "uint16")
+    SCRATCH["sel%d" % k] = ("sbuf", [128, 66], "float32")
+    SCRATCH["ba%d" % k] = ("sbuf", [128, 66], "float32")
+    SCRATCH["di%d" % k] = ("sbuf", [128, 66], "float32")
+    SCRATCH["rep%d" % k] = ("sbuf", [128, 2 * C], "float32")
+SCRATCH["fia"] = ("sbuf", [128, 66], "int32")
+SCRATCH["pka"] = ("sbuf", [128, 66], "uint16")
+SCRATCH["e16a"] = ("sbuf", [128, 66], "uint16")
+SCRATCH["fua"] = ("sbuf", [128, 36], "uint16")
+SCRATCH["mra"] = ("sbuf", [128, 3 * C], "float32")
+SCRATCH["rep3"] = ("sbuf", [128, 2 * C], "float32")
+SCRATCH["hq"] = ("sbuf", [128, H], "float8_e4m3fn_x4")
+SCRATCH["hs"] = ("sbuf", [128, H], "uint8")
+SCRATCH["hl"] = ("sbuf", [128, 22], "uint16")
+
+ENG = {"V": "sv", "S": "ss", "P": "st", "G": "sg"}
+SEMAPHORES = ["sv", "ss", "st", "sg", "rl", "hla", "hca", "hsa"] + ["la%d" % k for k in range(3)] + ["za%d" % k for k in range(3)] + ["d%d" % k for k in range(40)]
+
+
+def machine(g, T):
+    queues = {"V": g.vector, "S": g.scalar, "P": g.tensor, "G": g, "Y": g.sync}
+    know = {q: {} for q in queues}
+    cnt, hist, behind, ndma = {}, {}, {}, [0]
+
+    def need(q, tok):
+        sem, val = tok
+        k = know[q]
+        if k.get(sem, 0) >= val:
+            return
+        queues[q].wait_ge(T.sem[sem], val)
+        k[sem] = val
+        for s, v in behind.get(tok, {}).items():
+            k[s] = max(k.get(s, 0), v)
+
+    def norm(rs):
+        return [(r, 0, 1 << 30) if isinstance(r, str) else r for r in rs]
+
+    def before(q, rd, wr):
+        toks = []
+        for key, lo, hi in rd:
+            toks += [tok for (l, h, tok, w) in hist.get(key, []) if w and l < hi and lo < h]
+        for key, lo, hi in wr:
+            toks += [tok for (l, h, tok, w) in hist.get(key, []) if l < hi and lo < h]
+        best = {}
+        for s, v in toks:
+            best[s] = max(best.get(s, 0), v)
+        own = ENG.get(q)
+        for s in sorted(best, key=lambda s: s == own):
+            need(q, (s, best[s]))
+
+    def after(tok, rd, wr):
+        for key, lo, hi in wr:
+            hist[key] = [e for e in hist.get(key, []) if not (lo <= e[0] and e[1] <= hi)] + [(lo, hi, tok, True)]
+        for key, lo, hi in rd:
+            hist.setdefault(key, []).append((lo, hi, tok, False))
+
+    def op(q, call, rd, wr):
+        rd, wr = norm(rd), norm(wr)
+        before(q, rd, wr)
+        sem = ENG[q]
+        cnt[sem] = cnt.get(sem, 0) + 1
+        tok = (sem, cnt[sem])
+        call(queues[q]).then_inc(T.sem[sem], 1)
+        behind[tok] = dict(know[q])
+        after(tok, rd, wr)
+
+    def dma(q, out, in_, rd, wr):
+        rd, wr = norm(rd), norm(wr)
+        before(q, rd, wr)
+        sem = "d%d" % ndma[0]
+        ndma[0] += 1
+        cnt[sem] = 16
+        queues[q].dma_start(out, in_).then_inc(T.sem[sem], 16)
+        behind[(sem, 16)] = dict(know[q])
+        after((sem, 16), rd, wr)
+
+    def lands(key, sem, val):
+        after((sem, val), [], norm([key]))
+
+    def sends(rd, n, call):
+        before("G", norm(rd), [])
+        call()
+        cnt["rl"] = cnt.get("rl", 0) + n
+
+    def finish():
+        for s in sorted(cnt, key=lambda s: s[0] == "d"):
+            need("Y", (s, cnt[s]))
+    return op, dma, lands, sends, finish
+
+
+def bits(topo, src, dst, n=16, skip=0):
+    e = topo.engines(src, dst)[skip:skip + n]
+    return sum(1 << i for i in e), len(e)
+
+
+def helpers(T, topo, src, dst):
+    if topo.may_write(src, dst):
+        return []
+    return [c for c in topo.cores_of(src) if c not in T.cores and topo.die(c) == topo.die(src) and topo.may_write(c, dst)][:2]
+
+
+def send(g, T, topo, src, dst, out, in_, rsem, n=16):
+    rid, pid = topo.addr(dst, src)
+    m, k = bits(topo, src, dst, n)
+    g.remote_dma(out_ap=out, in_ap=in_, remote_sem=T.sem[rsem], local_sem=T.sem.rl, pid=pid, routing_id=rid, dma_engine_mask=m)
+    return k
+
+
+def hand_on(g, core, T, topo):
+    n = [0]
+    for r, src in enumerate(T.cores):
+        for s in STEP:
+            dst = T.cores[r ^ s]
+            hp = helpers(T, topo, src, dst)
+            if core not in hp:
+                continue
+            t, k = STEP.index(s), bits(topo, src, core)[1]
+            mine = [ab for c, ab in zip((hp[0], hp[-1]), CUT) if c == core]
+            g.wait_ge(T.sem.hla, 8 * len(mine))
+            for a, b in mine:
+                n[0] += send(g, T, topo, core, dst, T["fs%d" % t][:, a:b], T.hl[:, a:b], "la%d" % t)
+            if core == hp[0]:
+                g.wait_ge(T.sem.hca, k)
+                n[0] += send(g, T, topo, core, dst, T["zrq%d" % t][:, 0:H].bitcast(dt.uint8), T.hq[:, 0:H].bitcast(dt.uint8), "za%d" % t)
+            if core == hp[-1]:
+                g.wait_ge(T.sem.hsa, k)
+                n[0] += send(g, T, topo, core, dst, T["zrs%d" % t][:, 0:H], T.hs[:, 0:H], "za%d" % t)
+    if n[0]:
+        g.wait_ge(T.sem.rl, n[0])
+
+
+def rank_program(g, core, T, topo):
+    rank = T.rank_of(core)
+    if rank is None:
+        return hand_on(g, core, T, topo)
+    op, dma, lands, sends, finish = machine(g, T)
+    copy, sign = F.Copy, F.Sign
+
+    for t in range(3):
+        src = T.cores[rank ^ STEP[t]]
+        hp = helpers(T, topo, src, core)
+        if hp:
+            lands("fs%d" % t, "la%d" % t, bits(topo, hp[0], core)[1] + bits(topo, hp[-1], core)[1])
+            lands("zr%d" % t, "za%d" % t, bits(topo, hp[0], core)[1] + bits(topo, hp[-1], core)[1])
+        else:
+            lands("fs%d" % t, "la%d" % t, bits(topo, src, core)[1])
+            lands("zr%d" % t, "za%d" % t, 2 * bits(topo, src, core)[1])
+
+    for i, (a, b) in enumerate(CH):
+        dma("Y", T.xin[:, 4 * a:4 * b], T.x[:, 4 * a:4 * b], [], ["xin%d" % i])
+    dma("S", T.ppi[:, :], T.pp[:, :], [], ["ppi"])
+    dma("S", T.pri[:, :], T.pr[:, :], [], ["pri"])
+    dma("S", T.ut[:, :], T.u[:, :], [], ["ut"])
+    dma("S", T.rfi[:, :], T.rf[:, :], [], ["rfi"])
+    dma("Y", T.wq[:, 0:512].bitcast(dt.uint8), T.wc[:, :], [], ["wq"])
+    dma("Y", T.wsp[:, 0:512], T.ws[:, :], [], ["wsp"])
+    dma("Y", T.vt[:, :], T.v[:, :], [], ["vt"])
+
+    op("V", lambda q: q.memset(T.one[:, :], 1.0), [], ["one"])
+    op("V", lambda q: q.memset(T.et[:, :], 0.0), [], ["et"])
+    for nm, a, b, v in (("c01", 0, C, 1.0), ("bw", 352, 512, 0.0)):
+        op("V", lambda q: q.memset(T[nm][:, a:b], v), [], [(nm, a, b)])
+    op("G", lambda q: q.iota(T.pm[:, :], [[0, 66]], 0, 1), [], ["pm"])
+    op("G", lambda q: q.iota(T.gs[:, 0:16], [[1, 16]], 0, 0, allow_small_or_imprecise_dtypes=True), [], ["gs"])
+    op("G", lambda q: q.iota(T.idx[:, :], [[1, C]], 0, 0, allow_small_or_imprecise_dtypes=True), [], ["idx"])
+    op("G", lambda q: q.iota(T.q16[:, 66:82], [[1, 2], [16, 8]], 0, 0), [], ["uoi"])
+    for p in range(4):
+        op("G", lambda q: q.affine_select(T.et[:, 512 * p + p:512 * p + 512:4], T.one[:, :], [[-1, 128]], A.is_equal, 0.0, 0, 1), ["one", "et"], [("et_%d" % p)])
+    op("G", lambda q: q.iota(T.q16[:, 0:66], [[0, 3], [16, 22]], 352 - 512, 0), [], ["q16"])
+    op("G", lambda q: q.iota(T.jm[:, :], [[0, 22], [1, 16]], 0, 0, allow_small_or_imprecise_dtypes=True), [], ["jm"])
+    op("G", lambda q: q.affine_select(T.c01[:, :], T.c01[:, :], [[0, 22], [1, 16]], A.is_gt, 0.0, 0, 0), ["c01"], ["c01"])
+    op("V", lambda q: q.tensor_scalar(T.pm[:, :], T.pm[:, :], 15, None, A.bitwise_and), ["pm"], ["pm"])
+    op("V", lambda q: q.tensor_scalar(T.wt[:, 3:4], T.pm[:, 0:1], 1.0, None, A.add), ["pm"], ["wt3"])
+    op("V", lambda q: q.tensor_scalar(T.wt[:, 2:3], T.pm[:, 0:1], -1.0, None, A.mult), ["pm"], ["wt2"])
+    op("V", lambda q: q.tensor_copy(T.wt[:, 4:5], T.pm[:, 0:1]), ["pm"], ["wt4"])
+    op("V", lambda q: q.tensor_scalar(T.gm[:, 0:16], T.gs[:, 0:16], T.wt[:, 3:4], BIG - 1.0, A.is_equal, A.mult), ["gs", "wt3"], [("gm", 0, 16)])
+    op("V", lambda q: q.tensor_copy(T.e16a[:, 0:22], T.pm[:, 0:22]), ["pm"], ["e160"])
+    op("V", lambda q: q.tensor_scalar(T.gm[:, 16:32], T.gs[:, 0:16], T.wt[:, 4:5], None, A.not_equal), ["gs", "wt4"], [("gm", 16, 32)])
+    op("V", lambda q: q.tensor_scalar(T.wt[:, 1:2], T.pm[:, 0:1], 15.0, 1.0 - 1.0 / BIG, A.is_equal, A.mult), ["pm"], ["wt1"])
+    op("V", lambda q: q.tensor_tensor(T.gm[:, 32:48], T.gm[:, 0:16], T.gm[:, 16:32], A.add), [("gm", 0, 32)], [("gm", 32, 48)])
+    op("S", lambda q: q.activation(T.ck[:, :], T.gm[:, 32:48].indirect(T.e16a[:, 0:22]), copy), [("gm", 32, 48), "e160"], ["ck"])
+    op("V", lambda q: q.tensor_scalar(T.gm[:, 48:64], T.gs[:, 0:16], T.wt[:, 3:4], 15.0, A.is_equal, A.mult), ["gs", "wt3"], [("gm", 48, 64)])
+    op("V", lambda q: q.tensor_scalar(T.wt[:, 0:1], T.wt[:, 1:2], 1.0 / BIG, None, A.add), ["wt1"], ["wt0"])
+    op("V", lambda q: q.tensor_tensor(T.gm[:, 64:80], T.gm[:, 48:64], T.gm[:, 16:32], A.add), [("gm", 16, 64)], [("gm", 64, 80)])
+
+    op("V", lambda q: q.tensor_copy(T.pp16[:, :], T.ppi[:, :]), ["ppi"], ["pp16"])
+    op("V", lambda q: q.tensor_copy(T.pr16[:, :], T.pri[:, :]), ["pri"], ["pr16"])
+    op("S", lambda q: q.activation(T.rep0[:, 0:C], T.idx[:, :].indirect(T.pp16[:, 0:22]), copy), ["pp16", "idx"], [("rep0", 0, C)])
+    op("V", lambda q: q.tensor_copy(T.rf16[:, :], T.rfi[:, :]), ["rfi"], ["rf16"])
+    op("V", lambda q: q.tensor_copy(T.uo[:, :], T.q16[:, 66:82]), ["uoi"], ["uo"])
+    op("V", lambda q: q.quantize_mx(T.uq[:, :], T.us[:, :], T.ut[:, :]), ["ut"], ["uq"])
+    op("V", lambda q: q.tensor_copy(T.ua[:, 0:256].bitcast(dt.uint32), T.uq[:, 0:128].bitcast(dt.uint32).indirect(T.uo[:, 0:16])), ["uq", "uo"], ["ua"])
+    op("S", lambda q: q.activation(T.uas[:, 0:256], T.us[:, 0:128].indirect(T.uo[:, 0:16]), copy), ["uq", "uo"], ["uas"])
+
+    def quant(t, i, buf, keys):
+        a, b = CH[i]
+        op("V", lambda q: q.quantize_mx(T["xq%d" % t][:, a:b], T["xs%d" % t][:, a:b], T[buf][:, 4 * a:4 * b]), keys, [("xq%d" % t, a, b)])
+
+    def mm(bank, side, scale, c0, rq, rs, a, b, rd):
+        op("P", lambda q: q.matmul_mx(T["b%d" % bank][:, 0:b - a], T[side][:, c0:c0 + 128], T[scale][:, c0:c0 + 128],
+                                      T[rq][:, a:b], T[rs][:, a:b], True, True), rd, ["b%d" % bank])
+
+    def unpack(t, p, a, b):
+        mm(4 + p, "eq", "es", 128 * p, "xq%d" % t, "xs%d" % t, a, b, ["eq", ("xq%d" % t, a, b)])
+
+    def evac(p, a, b):
+        op("S", lambda q: q.activation(T.fp[:, C * p + a:C * p + b], T["b%d" % (4 + p)][:, 0:b - a], copy), [], ["b%d" % (4 + p), ("fp%d" % p, a, b)])
+
+    def signs(t, i):
+        a, b = CH[i]
+        for n in range(2):
+            mm(2 * i + n, "ua", "uas", 128 * n, "xq%d" % t, "xs%d" % t, a, b, ["ua", "uas", ("xq%d" % t, a, b)])
+        tiny = -(2.0 ** -100)
+        op("S", lambda q: q.activation(T.sa[:, a:b], T["b%d" % (2 * i)][:, 0:b - a], sign, bias=tiny), [], ["b%d" % (2 * i), ("sa", a, b)])
+        op("S", lambda q: q.activation(T.bw[:, a:b], T["b%d" % (2 * i + 1)][:, 0:b - a], sign, bias=tiny), [], ["b%d" % (2 * i + 1), ("bw", a, b)])
+
+    def head(t, i):
+        signs(t, i)
+        for p in range(4):
+            if i == 0 and p in EARLY:
+                unpack(t, p, *CH[0])
+            elif i == 1 and p in EARLY:
+                evac(p, *CH[0])
+        for p in range(4):
+            if i == 1 and p not in EARLY:
+                unpack(t, p, 0, C)
+                evac(p, 0, C)
+        for p in range(4):
+            if i == 1 and p in EARLY:
+                unpack(t, p, *CH[1])
+                evac(p, *CH[1])
+
+    def compose(t, rep, n):
+        k, a, b = T.pr16[:, 22 * t:22 * t + 22], C * n, C * n + C
+        op("S", lambda q: q.activation(T.pkf[:, a:b], T[rep][:, a:b].indirect(k), copy), ["pr16", (rep, a, b)], [("pkf", a, b)])
+
+    def kplus(t, q0):
+        k = T.pr16[:, 22 * t:22 * t + 22]
+        if q0 == "V":
+            op("V", lambda q: q.tensor_scalar(T.mra[:, C * t:C * t + C], T.idx[:, :].indirect(k), 1024.0, None, A.add), ["pr16", "idx"], ["mr%d" % t])
+        else:
+            op("S", lambda q: q.activation(T.mra[:, C * t:C * t + C], T.idx[:, :].indirect(k), F.Identity, bias=1024.0), ["pr16", "idx"], ["mr%d" % t])
+
+    def scan(out, okey, lo, fac, data, dkey):
+        op("V", lambda q: q.tensor_tensor_scan(T[out][:, lo:lo + C], T[fac][:, :], data, 0.0, A.mult, A.add), [fac, dkey], [(okey, lo, lo + C)])
+
+    def lists_base(t, psrc, pkey, fsrc, fkey):
+        ba = "ba%d" % t
+        for n, (s, key) in enumerate(((psrc, pkey), (fsrc, fkey), (fsrc, fkey))):
+            op("V", lambda q: q.tensor_scalar(T[ba][:, 22 * n:22 * n + 22], s, 512.0 if n == 1 else 0.0, None, A.add), [key], [(ba, 22 * n, 22 * n + 22)])
+
+    def lists_scan(t, n):
+        a, b = C * n, C * n + C
+        scan("sp", "sp", a, "ck", T.pkf[:, a:b], ("pkf", a, b))
+        op("V", lambda q: q.tensor_scalar(T.x1[:, 22 * n:22 * n + 22], T.sp[:, a + 15:b:16], T.wt[:, 0:1], 512.0 * n, A.mult, A.add), [("sp", a, b), "wt0"], [("x1", 22 * n, 22 * n + 22)])
+        if n == 0:
+            op("V", lambda q: q.tensor_scalar(T.pka[:, 22 * t:22 * t + 22], T.sp[:, a + 15:b:16], T.wt[:, 0:1], None, A.mult), [("sp", a, b), "wt0"], ["pk16%d" % t])
+
+    def rest(t, n):
+        ba, di = "ba%d" % t, "di%d" % t
+        if n == 0:
+            op("V", lambda q: q.tensor_tensor(T.xx[:, :], T.x1[:, 22:44], T.qk[:, 22 * t:22 * t + 22], A.add), [("x1", 22, 44), "qk"], ["xx"])
+        if n == 1:
+            op("V", lambda q: q.tensor_scalar(T.nn[:, :], T.xx[:, :], 1.0 / 352, 0.4986, A.mult, A.subtract), ["xx"], ["nn"])
+        if n == 2:
+            op("V", lambda q: q.tensor_scalar(T.nn[:, :], T.nn[:, :], -352.0, None, A.mult), ["nn"], ["nn"])
+        if n == 3:
+            op("V", lambda q: q.tensor_tensor(T.x1[:, 44:66], T.xx[:, :], T.nn[:, :], A.add), ["xx", "nn"], [("x1", 44, 66)])
+        if n == 4:
+            op("V", lambda q: q.tensor_tensor(T[di][:, :], T.x1[:, :], T[ba][:, :], A.subtract), ["x1", ba], [di])
+
+    def lists_rest(t):
+        rest(t, 0)
+        rest(t, 1)
+
+    quant(0, 0, "xin", ["xin0"])
+    quant(0, 1, "xin", ["xin1"])
+    op("V", lambda q: q.tensor_copy(T.rep0[:, C:2 * C], T.idx[:, :].indirect(T.rf16[:, 0:22])), ["rf16", "idx"], [("rep0", C, 2 * C)])
+    kplus(0, "V")
+    compose(0, "rep0", 0)
+    compose(0, "rep0", 1)
+    op("V", lambda q: q.quantize_mx(T.eq[:, :], T.es[:, :], T.et[:, :]), ["et"] + ["et_%d" % p for p in range(4)], ["eq"])
+    head(0, 0)
+    head(0, 1)
+    op("S", lambda q: q.activation(T.hr[:, :], T.jm[:, :], F.Abs, bias=T.wt[:, 2:3]), ["jm", "wt2"], ["hr"])
+    op("S", lambda q: q.activation(T.mk[:, C:2 * C], T.hr[:, :], F.Relu, bias=1.0, scale=-1.0), ["hr"], [("mk", C, 2 * C)])
+    op("S", lambda q: q.activation(T.c0b[:, :], T.gm[:, 64:80].indirect(T.e16a[:, 0:22]), copy), [("gm", 64, 80), "e160"], ["c0b"])
+
+    op("V", lambda q: q.tensor_tensor(T.qq[:, :], T.pm[:, :], T.q16[:, 0:66], A.add), ["pm", "q16"], ["qq"])
+    op("V", lambda q: q.tensor_tensor(T.qk[:, :], T.qq[:, :], T.pri[:, :], A.subtract), ["qq", "pri"], ["qk"])
+    lists_base(0, T.ppi[:, :], "ppi", T.rfi[:, :], "rfi")
+    lists_scan(0, 0)
+    lists_scan(0, 1)
+    lists_rest(0)
+
+    p16, p16key = T.pp16[:, 0:22], "pp16"
+    for t in range(3):
+        fi_, fu_, e_ = T.fia[:, 22 * t:22 * t + 22], T.fua[:, 12 * t:12 * t + 11], T.e16a[:, 22 * t:22 * t + 22]
+        ba, di, oc, sel, f16, fu, fi = [n + str(t) for n in ("ba", "di", "oc", "sel", "f16", "fu", "fi")]
+        op("V", lambda q: q.tensor_tensor(T.am[:, :], T.sa[:, :].indirect(p16), T.mra[:, C * t:C * t + C], A.mult), ["sa", p16key, "mr%d" % t], ["am"])
+        rest(t, 2)
+        op("V", lambda q: q.tensor_tensor(T.bw[:, 512:864], T.sa[:, :].indirect(T.pka[:, 22 * t:22 * t + 22]), T.am[:, :], A.mult), ["sa", "pk16%d" % t, "am"], [("bw", 512, 864)])
+        rest(t, 3)
+        scan("sE", "sE", 0, "ck", T.bw[:, 512:864], ("bw", 512, 864))
+        rest(t, 4)
+
+        def eqs(n):
+            op("V", lambda q: q.tensor_scalar(T.e3[:, 22 * n:22 * n + 22], T.sE[:, 15:C:16], 0.0, None, A.is_gt), ["sE"], [("e3", 22 * n, 22 * n + 22)])
+
+        def choose(a, b):
+            op("V", lambda q: q.tensor_tensor(T.sm[:, a:b], T.e3[:, a:b], T[di][:, a:b], A.mult), [("e3", a, b), di], [("sm", a, b)])
+            op("V", lambda q: q.tensor_tensor(T[sel][:, a:b], T.sm[:, a:b], T[ba][:, a:b], A.add), [("sm", a, b), ba], [(sel, a, b)])
+        eqs(0)
+        eqs(1)
+        choose(0, 44)
+        op("V", lambda q: q.tensor_copy(T[oc][:, :], T[sel][:, 0:44]), [(sel, 0, 44)], [oc])
+        op("S", lambda q: q.activation(T.gb[:, :], T.bw[:, 0:C].indirect(T[oc][:, 0:22]), copy, scale=4096.0), [("bw", 0, C), oc], ["gb"])
+        for p in range(4):
+            op("S", lambda q: q.activation(T.gp[:, C * p:C * p + C], T.fp[:, C * p:C * p + C].indirect(T[oc][:, 0:22]), copy, scale=0.5), ["fp%d" % p, oc], ["gp%d" % p])
+        op("V", lambda q: q.tensor_tensor(T.gm[:, C:2 * C], T.bw[:, :].indirect(T[oc][:, 22:44]), T.mk[:, C:2 * C], A.mult), ["bw", oc, "mk"], ["gm"])
+        eqs(2)
+        scan("gs", "gs", C, "c01", T.gm[:, C:2 * C], "gm")
+        op("V", lambda q: q.tensor_tensor(T.sm[:, 44:66], T.e3[:, 44:66], T[di][:, 44:66], A.mult), [("e3", 44, 66), di], [("sm", 44, 66)])
+        scan("gsb", "gsb", 0, "c0b", T.gb[:, :], "gb")
+        op("V", lambda q: q.tensor_tensor(T[sel][:, 44:66], T.sm[:, 44:66], T[ba][:, 44:66], A.add), [("sm", 44, 66), ba], [(sel, 44, 66)])
+        op("V", lambda q: q.tensor_tensor(T.tt[:, 0:22], T.gs[:, C + 15:2 * C:16], T[sel][:, 22:44], A.max), ["gs", sel], ["t1"])
+        op("V", lambda q: q.tensor_tensor(T.tt[:, 22:44], T.gsb[:, 15:C:16], T.tt[:, 0:22], A.min), ["gsb", "t1"], ["t2"])
+        op("V", lambda q: q.tensor_tensor(T.t3[:, :], T.tt[:, 22:44], T[sel][:, 44:66], A.max), ["t2", sel], ["t3"])
+        op("V", lambda q: q.tensor_scalar(fi_, T.t3[:, :], 511, None, A.bitwise_and), ["t3"], [fi])
+        op("V", lambda q: q.tensor_copy(fu_, T.fia[:, 22 * t + 11:22 * t + 22]), [fi], [fu])
+        op("V", lambda q: q.tensor_copy(T[f16][:, :], fi_), [fi], [f16])
+        dst = T.cores[rank ^ STEP[t]]
+        hp = helpers(T, topo, core, dst)
+        if hp:
+            halves = []
+            for n, (c, (a, b)) in enumerate(zip((hp[0], hp[-1]), CUT)):
+                rid, pid = topo.addr(c, core)
+                halves.append(RemoteDMATransfer(dst_ids=[DstId(rid=rid, pnc=pid)], dma_engine_mask=bits(topo, core, c, 8, 8 * n)[0],
+                                                remote_sem=T.sem.hla, src=T[f16][:, a:b], dst=T.hl[:, a:b]))
+            sends([f16], 16, lambda: g.remote_dma_fused(halves, local_sem=T.sem.rl))
+        else:
+            sends([f16], bits(topo, core, dst)[1], lambda: send(g, T, topo, core, dst, T["fs%d" % t][:, 0:22], T[f16][:, 0:22], "la%d" % t))
+        for p in POOL:
+            a, b = C * p, C * p + H
+            op("G", lambda q: q.affine_select(T.g2[:, a:b], T.gp[:, a:b], [[0, H]], A.is_ge, 0.0, 1, 0), ["gp%d" % p], [("g2", a, b)])
+        for half, (buf, off, o, nm) in enumerate((("ztu", fu_, H, "zu"), ("ztl", T[f16][:, 0:11], 0, "zl"))):
+            zq, zs = "%sq%d" % (nm, t), "%ss%d" % (nm, t)
+            for p in range(4):
+                a, b = C * p + o, C * p + o + H
+                if half == 1 and p not in POOL:
+                    op("S", lambda q: q.activation(T.g2[:, a:b], T.gp[:, a:b], copy), ["gp%d" % p], [("g2", a, b)])
+            for p in range(4):
+                for n in ((0, 1), (2,), (3,), ())[p] if half == 0 else ():
+                    a, b = C * n + o, C * n + o + H
+                    op("V", lambda q: q.tensor_copy(T.g2[:, a:b], T.gp[:, a:b]), ["gp%d" % n], [("g2", a, b)])
+                a, b = C * p + o, C * p + o + H
+                op("V", lambda q: q.tensor_tensor(T[buf][:, p:4 * H:4], T.gp[:, C * p:C * p + C].indirect(off), T.g2[:, a:b], A.add), ["gp%d" % p, ("g2", a, b), f16, fu], ["%s_%d" % (buf, p)])
+            op("V", lambda q: q.quantize_mx(T[zq][:, :], T[zs][:, :], T[buf][:, :]), ["%s_%d" % (buf, p) for p in range(4)], [zq])
+            if half == 0 and not hp:
+                k = bits(topo, core, dst)[1]
+                sends([zq], k, lambda: send(g, T, topo, core, dst, T["zrq%d" % t][:, 0:H].bitcast(dt.uint8), T[zq][:, 0:H].bitcast(dt.uint8), "za%d" % t))
+                sends([zq], k, lambda: send(g, T, topo, core, dst, T["zrs%d" % t][:, 0:H], T[zs][:, 0:H], "za%d" % t))
+            elif half == 0:
+                sends([zq], bits(topo, core, hp[0])[1], lambda: send(g, T, topo, core, hp[0], T.hq[:, 0:H].bitcast(dt.uint8), T[zq][:, 0:H].bitcast(dt.uint8), "hca"))
+                sends([zq], bits(topo, core, hp[-1])[1], lambda: send(g, T, topo, core, hp[-1], T.hs[:, 0:H], T[zs][:, 0:H], "hsa"))
+        rep = "rep%d" % (t + 1)
+        op("S", lambda q: q.activation(T[rep][:, 0:C], T.idx[:, :].indirect(T[oc][:, 0:22]), copy), [oc, "idx"], [(rep, 0, C)])
+        op("S", lambda q: q.activation(T[rep][:, C:2 * C], T.idx[:, :].indirect(T[f16][:, 0:22]), copy), [f16, "idx"], [(rep, C, 2 * C)])
+        for p in range(4):
+            mm(4 + p, "wq", "wsp", 128 * p, "zlq%d" % t, "zls%d" % t, 0, H, ["wq", "wsp", "zlq%d" % t])
+        def own_half():
+            for p in range(4):
+                op("S", lambda q: q.activation(T.bp[:, C * p:C * p + H], T["b%d" % (4 + p)][:, 0:H], copy, scale=0.03125), [], ["b%d" % (4 + p), ("bp%d" % p, 0, H)])
+
+        def theirs():
+            op("S", lambda q: q.activation(T.fsr[:, :], T.idx[:, :].indirect(T["fs%d" % t][:, 0:22]), copy), ["fs%d" % t, "idx"], ["fsr"])
+
+        def wrapped(src, key, out, okey):
+            scan("esc", "esc", 0, "ck", src, key)
+            op("V", lambda q: q.tensor_scalar(out, T.esc[:, 15:C:16], T.wt[:, 0:1], None, A.mult), ["esc", "wt0"], [okey])
+
+        def inverse(src, key):
+            op("V", lambda q: q.tensor_copy(T.ew[:, :].indirect(T[oc][:, 0:22]), src), [key, oc], ["ew"])
+
+        def by_place():
+            op("S", lambda q: q.activation(T.hr[:, :], T.fsr[:, :].indirect(T[f16][:, 0:22]), copy), ["fsr", f16], ["hr"])
+
+        def by_column():
+            op("S", lambda q: q.activation(T.hr[:, :], T[rep][:, C:2 * C].indirect(T.rf16[:, 0:22]), copy), [(rep, C, 2 * C), "rf16"], ["hr"])
+
+        def looked_up():
+            op("S", lambda q: q.activation(T.hr[:, :], T.fsr[:, :].indirect(T.pp16[:, 0:22]), copy), ["fsr", "pp16"], ["hr"])
+
+        def place_of():
+            inverse(T.idx[:, :], "idx")
+            wrapped(T.ew[:, :], "ew", T.rf16[:, :], "rf16")
+
+        def to_columns():
+            inverse(T.hr[:, :], "hr")
+            wrapped(T.ew[:, :], "ew", e_, "e16%d" % t)
+        parts = {
+            "P": lambda: compose(t + 1, rep, 0), "p": lambda: lists_scan(t + 1, 0),
+            "F": lambda: compose(t + 1, rep, 1), "f": lambda: lists_scan(t + 1, 1),
+            "b": lambda: lists_base(t + 1, T[sel][:, 0:22], (sel, 0, 22), fi_, fi), "K": lambda: kplus(t + 1, "S"), "r": lambda: lists_rest(t + 1),
+            "i": place_of, "C": by_column, "c": lambda: wrapped(T.hr[:, :], "hr", T.pp16[:, :], "pp16"),
+            "T": theirs, "E": looked_up, "e": lambda: wrapped(T.hr[:, :], "hr", e_, "e16%d" % t),
+            "H": by_place, "h": to_columns, "O": own_half,
+            "v": lambda: op("V", lambda q: q.quantize_mx(T.vq[:, :], T.vs[:, :], T.vt[:, :]), ["vt"], ["vq"]),
+        }
+        for n in SEQ[t][0]:
+            parts[n]()
+        for p in range(4 - XS[t], 4):
+            unpack(t, p, 0, C)
+        if t == 2:
+            dma("Y", T.pf[:, :], T[rep][0:128:16, :], [rep], ["pf"])
+        for p in range(4):
+            mm(p, "wq", "wsp", 128 * p, "zrq%d" % t, "zrs%d" % t, 0, H, ["wq", "wsp", "zr%d" % t])
+            o, i_ = T.bp[:, C * p + H:C * p + C], T["b%d" % p][:, 0:H]
+            if p not in EV:
+                op("S", lambda q: q.activation(o, i_, copy, scale=0.03125), [], ["b%d" % p, ("bp%d" % p, H, C)])
+            else:
+                op("V", lambda q: q.tensor_scalar(o, i_, 0.03125, None, A.mult), [], ["b%d" % p, ("bp%d" % p, H, C)])
+        for i, (a, b) in enumerate(CH):
+            e = T.e16a[:, 22 * t + a // 16:22 * t + b // 16]
+            for p in range(4 - XS[t], 4):
+                op("S", lambda q: q.activation(T.bg[:, C * p + a:C * p + b], T.bp[:, C * p:C * p + C].indirect(e), copy), ["bp%d" % p, "e16%d" % t], [("bg%d" % p, a, b)])
+        for n in SEQ[t][1]:
+            parts[n]()
+        for i, (a, b) in enumerate(CH):
+            for p in range(4):
+                if p >= 4 - XS[t]:
+                    op("V", lambda q: q.tensor_tensor(T.xt[:, 4 * a + p:4 * b:4], T["b%d" % (4 + p)][:, a:b], T.bg[:, C * p + a:C * p + b], A.add),
+                       [("bg%d" % p, a, b)], ["b%d" % (4 + p), ("xt%d" % p, a, b)])
+                    continue
+                op("V", lambda q: q.tensor_tensor(T.xt[:, 4 * a + p:4 * b:4], T.bp[:, C * p:C * p + C].indirect(T.e16a[:, 22 * t + a // 16:22 * t + b // 16]), T.fp[:, C * p + a:C * p + b], A.add),
+                   ["bp%d" % p, "e16%d" % t, ("fp%d" % p, a, b)], [("xt%d" % p, a, b)])
+            quant(t + 1, i, "xt", [("xt%d" % p, a, b) for p in range(4)])
+            if t < 2:
+                head(t + 1, i)
+            else:
+                xq, xs = "xq%d" % 3, "xs%d" % 3
+                mm(4 + i, "vq", "vs", 0, xq, xs, a, b, ["vq", (xq, a, b)])
+                dma("Y", T.oc[:, 4 * a:4 * b], T[xq][:, a:b].bitcast(dt.uint8), [(xq, a, b)], ["ocout%d" % i])
+                op("S", lambda q: q.activation(T.yt[:, a:b], T["b%d" % (4 + i)][:, 0:b - a], copy), [], ["b%d" % (4 + i), ("yt", a, b)])
+                dma("S", T.y[:, a:b], T.yt[:, a:b], [("yt", a, b)], ["yout%d" % i])
+                for k in range(4):
+                    dma("Y" if k < 3 else "S", T.osc[4 * k:4 * k + 4, a:b], T[xs][32 * k:32 * k + 4, a:b], [(xq, a, b)], ["oscout%d%d" % (i, k)])
+        for n in SEQ[t][2]:
+            parts[n]()
+        p16, p16key = T[oc][:, 0:22], oc
+    finish()

@@ -5,13 +5,17 @@ A, F = AluOpType, ActivationFunctionType
 N, C, H = 8, 352, 176
 STEP = [4, 1, 2]
 CH = [(0, 224), (224, 352)]
-SEQ = [("PFbpfTHOKh", "", "r"), ("PbpTHOh", "FK", "fr"), ("iOCcTEve", "", "")]
 CUT = ((0, 11), (11, 22))
-EARLY = ()
-POOL = ()
-EV = ()
 XS = [1, 1, 1]
-BIG = 16384.0
+BIG = 2.0 ** 20
+UP = 4096.0
+MID = 176.0
+SEQ = [
+    dict(idle="K", z="L2 L3 Q R l0 l1 P l2 l3 lq F g wg O b g16 T E p we p16 e16", x="", mid="", end="f f16 r0 r1"),
+    dict(idle="K", z="L2 L3 Q R l0 l1 T l2 l3 H lq O h wh b P e16", x="F", mid="p p16", end="f f16 r0 r1"),
+    dict(idle="", z="L2 L3 Q R l0 l1 l2 l3 lq O g wg v g16 T E we e16", x="", mid="", end=""),
+]
+GAPS = ["", "", "c0", "", "", "c1 u2", "", "u3", ""]
 
 SCRATCH = {
     "xin": ("sbuf", [128, 4 * C], "bfloat16"), "xt": ("sbuf", [128, 4 * C], "bfloat16"),
@@ -20,33 +24,39 @@ SCRATCH = {
     "ua": ("sbuf", [128, 256], "float8_e4m3fn_x4"), "uas": ("sbuf", [128, 256], "uint8"),
     "vq": ("sbuf", [128, 128], "float8_e4m3fn_x4"), "vs": ("sbuf", [128, 128], "uint8"),
     "wq": ("sbuf", [128, 512], "float8_e4m3fn_x4"), "wsp": ("sbuf", [128, 512], "uint8"),
-    "one": ("sbuf", [128, 128], "bfloat16"), "gb": ("sbuf", [128, C], "bfloat16"), "gsb": ("sbuf", [128, C], "bfloat16"), "c0b": ("sbuf", [128, C], "bfloat16"),
-    "bg": ("sbuf", [128, 4 * C], "bfloat16"), "et": ("sbuf", [128, 2048], "bfloat16"),
+    "one": ("sbuf", [128, 128], "bfloat16"), "et": ("sbuf", [128, 516], "bfloat16"),
     "eq": ("sbuf", [128, 512], "float8_e4m3fn_x4"), "es": ("sbuf", [128, 512], "uint8"),
     "ppi": ("sbuf", [128, 22], "int32"), "rfi": ("sbuf", [128, 22], "int32"), "pri": ("sbuf", [128, 66], "int32"),
     "pp16": ("sbuf", [128, 22], "uint16"), "rf16": ("sbuf", [128, 22], "uint16"), "pr16": ("sbuf", [128, 66], "uint16"),
-    "idx": ("sbuf", [128, C], "float32"), "jm": ("sbuf", [128, C], "float32"), "mk": ("sbuf", [128, 2 * C], "float32"),
-    "ck": ("sbuf", [128, C], "float32"), "c01": ("sbuf", [128, C], "float32"),
-    "wt": ("sbuf", [128, 8], "float32"), "uo": ("sbuf", [128, 16], "uint16"),
-    "pm": ("sbuf", [128, 66], "int32"), "q16": ("sbuf", [128, 82], "int32"),
-    "qq": ("sbuf", [128, 66], "int32"), "qk": ("sbuf", [128, 66], "float32"),
+    "idm": ("sbuf", [128, C], "bfloat16"), "ck": ("sbuf", [128, C], "bfloat16"), "ch": ("sbuf", [128, C], "bfloat16"),
+    "pm": ("sbuf", [128, 22], "int32"), "mo": ("sbuf", [128, 22], "uint16"), "d16": ("sbuf", [128, 16], "int32"),
+    "pat": ("sbuf", [128, 96], "float32"), "wt": ("sbuf", [128, 12], "float32"), "c4": ("sbuf", [128, 4], "float32"),
+    "uoi": ("sbuf", [128, 16], "int32"), "uo": ("sbuf", [128, 16], "uint16"),
+    "q16": ("sbuf", [128, 66], "int32"), "qk": ("sbuf", [128, 66], "float32"),
     "sa": ("sbuf", [128, C], "bfloat16"), "bw": ("sbuf", [128, 864], "float32"), "am": ("sbuf", [128, C], "float32"),
-    "sE": ("sbuf", [128, C], "float32"), "e3": ("sbuf", [128, 66], "float32"), "sm": ("sbuf", [128, 66], "float32"),
-    "gm": ("sbuf", [128, 2 * C], "float32"), "gs": ("sbuf", [128, 2 * C], "float32"),
-    "tt": ("sbuf", [128, 44], "float32"), "t3": ("sbuf", [128, 22], "int32"),
-    "pkf": ("sbuf", [128, 2 * C], "float32"), "sp": ("sbuf", [128, 2 * C], "float32"),
+    "sE": ("sbuf", [128, C], "float32"), "e3": ("sbuf", [128, 22], "float32"), "sm": ("sbuf", [128, 66], "float32"),
+    "gm": ("sbuf", [128, C], "float32"), "gs": ("sbuf", [128, C], "float32"),
+    "gb": ("sbuf", [128, C], "bfloat16"), "gsb": ("sbuf", [128, C], "bfloat16"),
+    "tt": ("sbuf", [128, 66], "float32"), "t3": ("sbuf", [128, 22], "int32"),
+    "pkf": ("sbuf", [128, 2 * C], "bfloat16"), "sp": ("sbuf", [128, 2 * C], "bfloat16"),
     "x1": ("sbuf", [128, 66], "int32"), "xx": ("sbuf", [128, 22], "float32"), "nn": ("sbuf", [128, 22], "int32"),
-    "fsr": ("sbuf", [128, C], "float32"), "hr": ("sbuf", [128, C], "float32"), "ew": ("sbuf", [128, C], "float32"),
-    "esc": ("sbuf", [128, C], "float32"), "ei": ("sbuf", [128, 22], "int32"),
+    "fsr": ("sbuf", [128, C], "bfloat16"), "hr": ("sbuf", [128, C], "bfloat16"), "ew": ("sbuf", [128, C], "bfloat16"),
+    "esc": ("sbuf", [128, C], "bfloat16"), "gsc": ("sbuf", [128, C], "bfloat16"),
     "fp": ("sbuf", [128, 4 * C], "bfloat16"), "gp": ("sbuf", [128, 4 * C], "bfloat16"), "bp": ("sbuf", [128, 4 * C], "bfloat16"),
+    "bg": ("sbuf", [128, 4 * C], "bfloat16"), "g2": ("sbuf", [128, 4 * C], "bfloat16"),
     "ztu": ("sbuf", [128, 4 * H], "bfloat16"), "ztl": ("sbuf", [128, 4 * H], "bfloat16"),
-    "yt": ("sbuf", [128, C], "float32"), "g2": ("sbuf", [128, 4 * C], "bfloat16"),
+    "yt": ("sbuf", [128, C], "float32"), "pfo": ("sbuf", [128, 2 * C], "float32"),
+    "pka": ("sbuf", [128, 66], "uint16"), "e16a": ("sbuf", [128, 66], "uint16"), "g16a": ("sbuf", [128, 66], "uint16"),
+    "fua": ("sbuf", [128, 36], "uint16"), "mra": ("sbuf", [128, 3 * C], "float32"),
+    "hq": ("sbuf", [128, H], "float8_e4m3fn_x4"), "hs": ("sbuf", [128, H], "uint8"), "hl": ("sbuf", [128, 22], "uint16"),
 }
 for k in range(8):
     SCRATCH["b%d" % k] = ("psum", [128, 512], "float32")
 for k in range(4):
     SCRATCH["xq%d" % k] = ("sbuf", [128, C], "float8_e4m3fn_x4")
     SCRATCH["xs%d" % k] = ("sbuf", [128, C], "uint8")
+    SCRATCH["ba%d" % k] = ("sbuf", [128, 66], "int32")
+    SCRATCH["rep%d" % k] = ("sbuf", [128, 2 * C], "bfloat16")
 for k in range(3):
     for nm in ("zu", "zl", "zr"):
         SCRATCH["%sq%d" % (nm, k)] = ("sbuf", [128, H], "float8_e4m3fn_x4")
@@ -54,19 +64,7 @@ for k in range(3):
     SCRATCH["oc%d" % k] = ("sbuf", [128, 44], "uint16")
     SCRATCH["f16%d" % k] = ("sbuf", [128, 22], "uint16")
     SCRATCH["fs%d" % k] = ("sbuf", [128, 22], "uint16")
-    SCRATCH["sel%d" % k] = ("sbuf", [128, 66], "float32")
-    SCRATCH["ba%d" % k] = ("sbuf", [128, 66], "float32")
     SCRATCH["di%d" % k] = ("sbuf", [128, 66], "float32")
-    SCRATCH["rep%d" % k] = ("sbuf", [128, 2 * C], "float32")
-SCRATCH["fia"] = ("sbuf", [128, 66], "int32")
-SCRATCH["pka"] = ("sbuf", [128, 66], "uint16")
-SCRATCH["e16a"] = ("sbuf", [128, 66], "uint16")
-SCRATCH["fua"] = ("sbuf", [128, 36], "uint16")
-SCRATCH["mra"] = ("sbuf", [128, 3 * C], "float32")
-SCRATCH["rep3"] = ("sbuf", [128, 2 * C], "float32")
-SCRATCH["hq"] = ("sbuf", [128, H], "float8_e4m3fn_x4")
-SCRATCH["hs"] = ("sbuf", [128, H], "uint8")
-SCRATCH["hl"] = ("sbuf", [128, 22], "uint16")
 
 ENG = {"V": "sv", "S": "ss", "P": "st", "G": "sg"}
 SEMAPHORES = ["sv", "ss", "st", "sg", "rl", "hla", "hca", "hsa"] + ["la%d" % k for k in range(3)] + ["za%d" % k for k in range(3)] + ["d%d" % k for k in range(40)]
@@ -201,51 +199,53 @@ def rank_program(g, core, T, topo):
             lands("fs%d" % t, "la%d" % t, bits(topo, src, core)[1])
             lands("zr%d" % t, "za%d" % t, 2 * bits(topo, src, core)[1])
 
+    dma("S", T.ppi[:, :], T.pp[:, :], [], ["ppi"])
+    dma("Y", T.ut[:, :], T.u[:, :], [], ["ut"])
+    dma("S", T.pri[:, :], T.pr[:, :], [], ["pri"])
     for i, (a, b) in enumerate(CH):
         dma("Y", T.xin[:, 4 * a:4 * b], T.x[:, 4 * a:4 * b], [], ["xin%d" % i])
-    dma("S", T.ppi[:, :], T.pp[:, :], [], ["ppi"])
-    dma("S", T.pri[:, :], T.pr[:, :], [], ["pri"])
-    dma("S", T.ut[:, :], T.u[:, :], [], ["ut"])
     dma("S", T.rfi[:, :], T.rf[:, :], [], ["rfi"])
-    dma("Y", T.wq[:, 0:512].bitcast(dt.uint8), T.wc[:, :], [], ["wq"])
+    dma("Y", T.wq[:, 0:512].bitcast(dt.uint8), T.wc[:, :], ["xin1"], ["wq"])
     dma("Y", T.wsp[:, 0:512], T.ws[:, :], [], ["wsp"])
     dma("Y", T.vt[:, :], T.v[:, :], [], ["vt"])
 
+    def ts(out, in0, s1, s2, ops, rd, wr):
+        op("V", lambda q: q.tensor_scalar(out, in0, s1, s2, *ops), rd, wr)
+
+    def tt(out, in0, in1, o, rd, wr):
+        op("V", lambda q: q.tensor_tensor(out, in0, in1, o), rd, wr)
+
+    def cp(out, in_, rd, wr):
+        op("V", lambda q: q.tensor_copy(out, in_), rd, wr)
+
+    def act(out, in_, rd, wr, func=copy, **kw):
+        op("S", lambda q: q.activation(out, in_, func, **kw), rd, wr)
+
+    op("G", lambda q: q.iota(T.pm[:, :], [[0, 22]], 0, 1), [], ["pm"])
+    op("G", lambda q: q.iota(T.d16[:, :], [[1, 16]], 128, -1), [], ["d16"])
+    op("G", lambda q: q.iota(T.idm[:, :], [[1, C]], -int(MID), 0, allow_small_or_imprecise_dtypes=True), [], ["idm"])
+    op("G", lambda q: q.iota(T.uoi[:, :], [[1, 2], [16, 8]], 0, 0), [], ["uoi"])
+    op("G", lambda q: q.iota(T.c4[:, :], [[512, 2], [int(MID), 2]], 0, 0, allow_small_or_imprecise_dtypes=True), [], ["c4"])
     op("V", lambda q: q.memset(T.one[:, :], 1.0), [], ["one"])
     op("V", lambda q: q.memset(T.et[:, :], 0.0), [], ["et"])
-    for nm, a, b, v in (("c01", 0, C, 1.0), ("bw", 352, 512, 0.0)):
-        op("V", lambda q: q.memset(T[nm][:, a:b], v), [], [(nm, a, b)])
-    op("G", lambda q: q.iota(T.pm[:, :], [[0, 66]], 0, 1), [], ["pm"])
-    op("G", lambda q: q.iota(T.gs[:, 0:16], [[1, 16]], 0, 0, allow_small_or_imprecise_dtypes=True), [], ["gs"])
-    op("G", lambda q: q.iota(T.idx[:, :], [[1, C]], 0, 0, allow_small_or_imprecise_dtypes=True), [], ["idx"])
-    op("G", lambda q: q.iota(T.q16[:, 66:82], [[1, 2], [16, 8]], 0, 0), [], ["uoi"])
-    for p in range(4):
-        op("G", lambda q: q.affine_select(T.et[:, 512 * p + p:512 * p + 512:4], T.one[:, :], [[-1, 128]], A.is_equal, 0.0, 0, 1), ["one", "et"], [("et_%d" % p)])
-    op("G", lambda q: q.iota(T.q16[:, 0:66], [[0, 3], [16, 22]], 352 - 512, 0), [], ["q16"])
-    op("G", lambda q: q.iota(T.jm[:, :], [[0, 22], [1, 16]], 0, 0, allow_small_or_imprecise_dtypes=True), [], ["jm"])
-    op("G", lambda q: q.affine_select(T.c01[:, :], T.c01[:, :], [[0, 22], [1, 16]], A.is_gt, 0.0, 0, 0), ["c01"], ["c01"])
-    op("V", lambda q: q.tensor_scalar(T.pm[:, :], T.pm[:, :], 15, None, A.bitwise_and), ["pm"], ["pm"])
-    op("V", lambda q: q.tensor_scalar(T.wt[:, 3:4], T.pm[:, 0:1], 1.0, None, A.add), ["pm"], ["wt3"])
-    op("V", lambda q: q.tensor_scalar(T.wt[:, 2:3], T.pm[:, 0:1], -1.0, None, A.mult), ["pm"], ["wt2"])
-    op("V", lambda q: q.tensor_copy(T.wt[:, 4:5], T.pm[:, 0:1]), ["pm"], ["wt4"])
-    op("V", lambda q: q.tensor_scalar(T.gm[:, 0:16], T.gs[:, 0:16], T.wt[:, 3:4], BIG - 1.0, A.is_equal, A.mult), ["gs", "wt3"], [("gm", 0, 16)])
-    op("V", lambda q: q.tensor_copy(T.e16a[:, 0:22], T.pm[:, 0:22]), ["pm"], ["e160"])
-    op("V", lambda q: q.tensor_scalar(T.gm[:, 16:32], T.gs[:, 0:16], T.wt[:, 4:5], None, A.not_equal), ["gs", "wt4"], [("gm", 16, 32)])
-    op("V", lambda q: q.tensor_scalar(T.wt[:, 1:2], T.pm[:, 0:1], 15.0, 1.0 - 1.0 / BIG, A.is_equal, A.mult), ["pm"], ["wt1"])
-    op("V", lambda q: q.tensor_tensor(T.gm[:, 32:48], T.gm[:, 0:16], T.gm[:, 16:32], A.add), [("gm", 0, 32)], [("gm", 32, 48)])
-    op("S", lambda q: q.activation(T.ck[:, :], T.gm[:, 32:48].indirect(T.e16a[:, 0:22]), copy), [("gm", 32, 48), "e160"], ["ck"])
-    op("V", lambda q: q.tensor_scalar(T.gm[:, 48:64], T.gs[:, 0:16], T.wt[:, 3:4], 15.0, A.is_equal, A.mult), ["gs", "wt3"], [("gm", 48, 64)])
-    op("V", lambda q: q.tensor_scalar(T.wt[:, 0:1], T.wt[:, 1:2], 1.0 / BIG, None, A.add), ["wt1"], ["wt0"])
-    op("V", lambda q: q.tensor_tensor(T.gm[:, 64:80], T.gm[:, 48:64], T.gm[:, 16:32], A.add), [("gm", 16, 64)], [("gm", 64, 80)])
-
-    op("V", lambda q: q.tensor_copy(T.pp16[:, :], T.ppi[:, :]), ["ppi"], ["pp16"])
-    op("V", lambda q: q.tensor_copy(T.pr16[:, :], T.pri[:, :]), ["pri"], ["pr16"])
-    op("S", lambda q: q.activation(T.rep0[:, 0:C], T.idx[:, :].indirect(T.pp16[:, 0:22]), copy), ["pp16", "idx"], [("rep0", 0, C)])
-    op("V", lambda q: q.tensor_copy(T.rf16[:, :], T.rfi[:, :]), ["rfi"], ["rf16"])
-    op("V", lambda q: q.tensor_copy(T.uo[:, :], T.q16[:, 66:82]), ["uoi"], ["uo"])
-    op("V", lambda q: q.quantize_mx(T.uq[:, :], T.us[:, :], T.ut[:, :]), ["ut"], ["uq"])
-    op("V", lambda q: q.tensor_copy(T.ua[:, 0:256].bitcast(dt.uint32), T.uq[:, 0:128].bitcast(dt.uint32).indirect(T.uo[:, 0:16])), ["uq", "uo"], ["ua"])
-    op("S", lambda q: q.activation(T.uas[:, 0:256], T.us[:, 0:128].indirect(T.uo[:, 0:16]), copy), ["uq", "uo"], ["uas"])
+    op("G", lambda q: q.affine_select(T.et[:, 3:515:4], T.one[:, :], [[-1, 128]], A.is_equal, 0.0, 0, 1), ["one"], ["et"])
+    op("G", lambda q: q.iota(T.q16[:, :], [[0, 3], [16, 22]], 352 - 512, 0), [], ["q16"])
+    ts(T.pm[:, :], T.pm[:, :], 15, None, [A.bitwise_and], ["pm"], ["pm"])
+    ts(T.d16[:, :], T.d16[:, :], 15, None, [A.bitwise_and], ["d16"], ["d16"])
+    cp(T.mo[:, :], T.pm[:, :], ["pm"], ["mo"])
+    ts(T.pat[:, 0:16], T.d16[:, :], 1.0, BIG - 1.0, [A.is_equal, A.mult], ["d16"], ["pat0"])
+    ts(T.pat[:, 16:32], T.d16[:, :], 1.0, None, [A.min], ["d16"], ["pat1"])
+    ts(T.wt[:, 1:2], T.pm[:, 0:1], 15.0, UP, [A.not_equal, A.mult], ["pm"], ["wt1"])
+    tt(T.pat[:, 32:48], T.pat[:, 0:16], T.pat[:, 16:32], A.add, ["pat0", "pat1"], ["pat2"])
+    ts(T.wt[:, 8:9], T.pm[:, 0:1], 15.0, 1.0 - 1.0 / BIG, [A.is_equal, A.mult], ["pm"], ["wt8"])
+    act(T.ck[:, :], T.pat[:, 32:48].indirect(T.mo[:, 0:22]), ["pat2", "mo"], ["ck"])
+    ts(T.pat[:, 48:64], T.d16[:, :], 1.0, UP, [A.is_equal, A.mult], ["d16"], ["pat3"])
+    ts(T.pat[:, 64:80], T.d16[:, :], 0.0, -8.0 * UP, [A.is_equal, A.mult], ["d16"], ["pat4"])
+    ts(T.wt[:, 0:1], T.wt[:, 8:9], 1.0 / BIG, None, [A.add], ["wt8"], ["wt0"])
+    ts(T.wt[:, 6:7], T.pm[:, 0:1], T.wt[:, 1:2], None, [A.subtract], ["pm", "wt1"], ["wt6"])
+    tt(T.pat[:, 80:96], T.pat[:, 48:64], T.pat[:, 64:80], A.add, ["pat3", "pat4"], ["pat5"])
+    op("V", lambda q: q.memset(T.bw[:, C:512], 0.0), [], [("bw", C, 512)])
+    down, up = T.wt[:, 0:1], T.wt[:, 1:2]
 
     def quant(t, i, buf, keys):
         a, b = CH[i]
@@ -255,137 +255,198 @@ def rank_program(g, core, T, topo):
         op("P", lambda q: q.matmul_mx(T["b%d" % bank][:, 0:b - a], T[side][:, c0:c0 + 128], T[scale][:, c0:c0 + 128],
                                       T[rq][:, a:b], T[rs][:, a:b], True, True), rd, ["b%d" % bank])
 
-    def unpack(t, p, a, b):
-        mm(4 + p, "eq", "es", 128 * p, "xq%d" % t, "xs%d" % t, a, b, ["eq", ("xq%d" % t, a, b)])
-
-    def evac(p, a, b):
-        op("S", lambda q: q.activation(T.fp[:, C * p + a:C * p + b], T["b%d" % (4 + p)][:, 0:b - a], copy), [], ["b%d" % (4 + p), ("fp%d" % p, a, b)])
+    def unpack(t, p):
+        mm(4 + p, "eq", "es", 128 * p, "xq%d" % t, "xs%d" % t, 0, C, ["eq%d" % p, "xq%d" % t])
 
     def signs(t, i):
         a, b = CH[i]
         for n in range(2):
             mm(2 * i + n, "ua", "uas", 128 * n, "xq%d" % t, "xs%d" % t, a, b, ["ua", "uas", ("xq%d" % t, a, b)])
         tiny = -(2.0 ** -100)
-        op("S", lambda q: q.activation(T.sa[:, a:b], T["b%d" % (2 * i)][:, 0:b - a], sign, bias=tiny), [], ["b%d" % (2 * i), ("sa", a, b)])
-        op("S", lambda q: q.activation(T.bw[:, a:b], T["b%d" % (2 * i + 1)][:, 0:b - a], sign, bias=tiny), [], ["b%d" % (2 * i + 1), ("bw", a, b)])
+        act(T.sa[:, a:b], T["b%d" % (2 * i)][:, 0:b - a], [], ["b%d" % (2 * i), ("sa", a, b)], sign, bias=tiny)
+        act(T.bw[:, a:b], T["b%d" % (2 * i + 1)][:, 0:b - a], [], ["b%d" % (2 * i + 1), ("bw", a, b)], sign, bias=tiny)
 
-    def head(t, i):
-        signs(t, i)
+    def values(t):
         for p in range(4):
-            if i == 0 and p in EARLY:
-                unpack(t, p, *CH[0])
-            elif i == 1 and p in EARLY:
-                evac(p, *CH[0])
-        for p in range(4):
-            if i == 1 and p not in EARLY:
-                unpack(t, p, 0, C)
-                evac(p, 0, C)
-        for p in range(4):
-            if i == 1 and p in EARLY:
-                unpack(t, p, *CH[1])
-                evac(p, *CH[1])
+            unpack(t, p)
+            act(T.fp[:, C * p:C * p + C], T["b%d" % (4 + p)][:, 0:C], [], ["b%d" % (4 + p), "fp%d" % p])
 
-    def compose(t, rep, n):
-        k, a, b = T.pr16[:, 22 * t:22 * t + 22], C * n, C * n + C
-        op("S", lambda q: q.activation(T.pkf[:, a:b], T[rep][:, a:b].indirect(k), copy), ["pr16", (rep, a, b)], [("pkf", a, b)])
+    def repeat(rep, n, off, key):
+        act(T[rep][:, C * n:C * n + C], T.idm[:, :].indirect(off), [key, "idm"], [(rep, C * n, C * n + C)])
+
+    def compose(t, n):
+        k, a, b, rep = T.pr16[:, 22 * t:22 * t + 22], C * n, C * n + C, "rep%d" % t
+        act(T.pkf[:, a:b], T[rep][:, a:b].indirect(k), ["pr16", (rep, a, b)], [("pkf", a, b)])
 
     def kplus(t, q0):
-        k = T.pr16[:, 22 * t:22 * t + 22]
+        k, o = T.pr16[:, 22 * t:22 * t + 22], T.mra[:, C * t:C * t + C]
         if q0 == "V":
-            op("V", lambda q: q.tensor_scalar(T.mra[:, C * t:C * t + C], T.idx[:, :].indirect(k), 1024.0, None, A.add), ["pr16", "idx"], ["mr%d" % t])
+            ts(o, T.idm[:, :].indirect(k), 1024.0 + MID, None, [A.add], ["pr16", "idm"], ["mr%d" % t])
         else:
-            op("S", lambda q: q.activation(T.mra[:, C * t:C * t + C], T.idx[:, :].indirect(k), F.Identity, bias=1024.0), ["pr16", "idx"], ["mr%d" % t])
+            act(o, T.idm[:, :].indirect(k), ["pr16", "idm"], ["mr%d" % t], F.Identity, bias=1024.0 + MID)
 
-    def scan(out, okey, lo, fac, data, dkey):
-        op("V", lambda q: q.tensor_tensor_scan(T[out][:, lo:lo + C], T[fac][:, :], data, 0.0, A.mult, A.add), [fac, dkey], [(okey, lo, lo + C)])
+    def scan(out, okey, data, dkey):
+        op("V", lambda q: q.tensor_tensor_scan(out, T.ck[:, :], data, 0.0, A.mult, A.add), ["ck", dkey], [okey])
 
-    def lists_base(t, psrc, pkey, fsrc, fkey):
-        ba = "ba%d" % t
-        for n, (s, key) in enumerate(((psrc, pkey), (fsrc, fkey), (fsrc, fkey))):
-            op("V", lambda q: q.tensor_scalar(T[ba][:, 22 * n:22 * n + 22], s, 512.0 if n == 1 else 0.0, None, A.add), [key], [(ba, 22 * n, 22 * n + 22)])
+    def held(out, okey, buf, key, lo, add, akey):
+        ts(out, T[buf][:, lo + 15:lo + C:16], down, add, [A.mult, A.add], [key, "wt0"] + akey, [okey])
 
-    def lists_scan(t, n):
+    def lists_scan(n):
         a, b = C * n, C * n + C
-        scan("sp", "sp", a, "ck", T.pkf[:, a:b], ("pkf", a, b))
-        op("V", lambda q: q.tensor_scalar(T.x1[:, 22 * n:22 * n + 22], T.sp[:, a + 15:b:16], T.wt[:, 0:1], 512.0 * n, A.mult, A.add), [("sp", a, b), "wt0"], [("x1", 22 * n, 22 * n + 22)])
+        scan(T.sp[:, a:b], ("sp", a, b), T.pkf[:, a:b], ("pkf", a, b))
+
+    def lists_held(t, n):
+        a, b = C * n, C * n + C
         if n == 0:
-            op("V", lambda q: q.tensor_scalar(T.pka[:, 22 * t:22 * t + 22], T.sp[:, a + 15:b:16], T.wt[:, 0:1], None, A.mult), [("sp", a, b), "wt0"], ["pk16%d" % t])
+            held(T.pka[:, 22 * t:22 * t + 22], "pk16%d" % t, "sp", ("sp", a, b), a, MID, [])
+        held(T.x1[:, 22 * n:22 * n + 22], ("x1", 22 * n, 22 * n + 22), "sp", ("sp", a, b), a, T.wt[:, 3 + 2 * n:4 + 2 * n], ["wt2"])
 
     def rest(t, n):
         ba, di = "ba%d" % t, "di%d" % t
         if n == 0:
-            op("V", lambda q: q.tensor_tensor(T.xx[:, :], T.x1[:, 22:44], T.qk[:, 22 * t:22 * t + 22], A.add), [("x1", 22, 44), "qk"], ["xx"])
+            tt(T.xx[:, :], T.x1[:, 22:44], T.qk[:, 22 * t:22 * t + 22], A.add, [("x1", 22, 44), "qk"], ["xx"])
         if n == 1:
-            op("V", lambda q: q.tensor_scalar(T.nn[:, :], T.xx[:, :], 1.0 / 352, 0.4986, A.mult, A.subtract), ["xx"], ["nn"])
+            ts(T.nn[:, :], T.xx[:, :], 1.0 / 352, 0.4986, [A.mult, A.subtract], ["xx"], ["nn"])
         if n == 2:
-            op("V", lambda q: q.tensor_scalar(T.nn[:, :], T.nn[:, :], -352.0, None, A.mult), ["nn"], ["nn"])
+            ts(T.nn[:, :], T.nn[:, :], -352.0, None, [A.mult], ["nn"], ["nn"])
         if n == 3:
-            op("V", lambda q: q.tensor_tensor(T.x1[:, 44:66], T.xx[:, :], T.nn[:, :], A.add), ["xx", "nn"], [("x1", 44, 66)])
+            tt(T.x1[:, 44:66], T.xx[:, :], T.nn[:, :], A.add, ["xx", "nn"], [("x1", 44, 66)])
         if n == 4:
-            op("V", lambda q: q.tensor_tensor(T[di][:, :], T.x1[:, :], T[ba][:, :], A.subtract), ["x1", ba], [di])
+            tt(T[di][:, :], T.x1[:, :], T[ba][:, :], A.subtract, ["x1", ba], [di])
 
-    def lists_rest(t):
-        rest(t, 0)
-        rest(t, 1)
-
+    cp(T.pp16[:, :], T.ppi[:, :], ["ppi"], ["pp16"])
+    cp(T.pr16[:, :], T.pri[:, :], ["pri"], ["pr16"])
+    repeat("rep0", 0, T.pp16[:, 0:22], "pp16")
+    cp(T.uo[:, :], T.uoi[:, :], ["uoi"], ["uo"])
+    cp(T.rf16[:, :], T.rfi[:, :], ["rfi"], ["rf16"])
+    ts(T.wt[:, 2:6], T.c4[:, :], up, None, [A.add], ["c4", "wt1"], ["wt2"])
+    op("V", lambda q: q.quantize_mx(T.uq[:, :], T.us[:, :], T.ut[:, :]), ["ut"], ["uq"])
+    kplus(0, "V")
+    compose(0, 0)
+    cp(T.ua[:, 0:256].bitcast(dt.uint32), T.uq[:, 0:128].bitcast(dt.uint32).indirect(T.uo[:, 0:16]), ["uq", "uo"], ["ua"])
+    act(T.uas[:, 0:256], T.us[:, 0:128].indirect(T.uo[:, 0:16]), ["uq", "uo"], ["uas"])
     quant(0, 0, "xin", ["xin0"])
     quant(0, 1, "xin", ["xin1"])
-    op("V", lambda q: q.tensor_copy(T.rep0[:, C:2 * C], T.idx[:, :].indirect(T.rf16[:, 0:22])), ["rf16", "idx"], [("rep0", C, 2 * C)])
-    kplus(0, "V")
-    compose(0, "rep0", 0)
-    compose(0, "rep0", 1)
-    op("V", lambda q: q.quantize_mx(T.eq[:, :], T.es[:, :], T.et[:, :]), ["et"] + ["et_%d" % p for p in range(4)], ["eq"])
-    head(0, 0)
-    head(0, 1)
-    op("S", lambda q: q.activation(T.hr[:, :], T.jm[:, :], F.Abs, bias=T.wt[:, 2:3]), ["jm", "wt2"], ["hr"])
-    op("S", lambda q: q.activation(T.mk[:, C:2 * C], T.hr[:, :], F.Relu, bias=1.0, scale=-1.0), ["hr"], [("mk", C, 2 * C)])
-    op("S", lambda q: q.activation(T.c0b[:, :], T.gm[:, 64:80].indirect(T.e16a[:, 0:22]), copy), [("gm", 64, 80), "e160"], ["c0b"])
-
-    op("V", lambda q: q.tensor_tensor(T.qq[:, :], T.pm[:, :], T.q16[:, 0:66], A.add), ["pm", "q16"], ["qq"])
-    op("V", lambda q: q.tensor_tensor(T.qk[:, :], T.qq[:, :], T.pri[:, :], A.subtract), ["qq", "pri"], ["qk"])
-    lists_base(0, T.ppi[:, :], "ppi", T.rfi[:, :], "rfi")
-    lists_scan(0, 0)
-    lists_scan(0, 1)
-    lists_rest(0)
+    repeat("rep0", 1, T.rf16[:, 0:22], "rf16")
+    lists_scan(0)
+    signs(0, 0)
+    signs(0, 1)
+    compose(0, 1)
+    for p in range(4):
+        op("V", lambda q: q.quantize_mx(T.eq[:, 128 * p:128 * p + 128], T.es[:, 128 * p:128 * p + 128], T.et[:, 3 - p:515 - p]), ["et"], ["eq%d" % p])
+        if p == 0:
+            lists_held(0, 0)
+    act(T.ch[:, :], T.pat[:, 80:96].indirect(T.mo[:, 0:22]), ["pat5", "mo"], ["ch"])
+    values(0)
+    tt(T.qk[:, :], T.q16[:, :], T.pri[:, :], A.subtract, ["q16", "pri"], ["qk"])
+    ts(T.ba0[:, 0:22], T.ppi[:, :], up, None, [A.add], ["ppi", "wt1"], [("ba0", 0, 22)])
+    ts(T.ba0[:, 22:44], T.rfi[:, :], T.wt[:, 4:5], None, [A.add], ["rfi", "wt2"], [("ba0", 22, 44)])
+    ts(T.qk[:, :], T.qk[:, :], T.wt[:, 6:7], None, [A.add], ["qk", "wt6"], ["qk"])
+    cp(T.ba0[:, 44:66], T.rfi[:, :], ["rfi"], [("ba0", 44, 66)])
 
     p16, p16key = T.pp16[:, 0:22], "pp16"
     for t in range(3):
-        fi_, fu_, e_ = T.fia[:, 22 * t:22 * t + 22], T.fua[:, 12 * t:12 * t + 11], T.e16a[:, 22 * t:22 * t + 22]
-        ba, di, oc, sel, f16, fu, fi = [n + str(t) for n in ("ba", "di", "oc", "sel", "f16", "fu", "fi")]
-        op("V", lambda q: q.tensor_tensor(T.am[:, :], T.sa[:, :].indirect(p16), T.mra[:, C * t:C * t + C], A.mult), ["sa", p16key, "mr%d" % t], ["am"])
-        rest(t, 2)
-        op("V", lambda q: q.tensor_tensor(T.bw[:, 512:864], T.sa[:, :].indirect(T.pka[:, 22 * t:22 * t + 22]), T.am[:, :], A.mult), ["sa", "pk16%d" % t, "am"], [("bw", 512, 864)])
-        rest(t, 3)
-        scan("sE", "sE", 0, "ck", T.bw[:, 512:864], ("bw", 512, 864))
-        rest(t, 4)
-
-        def eqs(n):
-            op("V", lambda q: q.tensor_scalar(T.e3[:, 22 * n:22 * n + 22], T.sE[:, 15:C:16], 0.0, None, A.is_gt), ["sE"], [("e3", 22 * n, 22 * n + 22)])
-
-        def choose(a, b):
-            op("V", lambda q: q.tensor_tensor(T.sm[:, a:b], T.e3[:, a:b], T[di][:, a:b], A.mult), [("e3", a, b), di], [("sm", a, b)])
-            op("V", lambda q: q.tensor_tensor(T[sel][:, a:b], T.sm[:, a:b], T[ba][:, a:b], A.add), [("sm", a, b), ba], [(sel, a, b)])
-        eqs(0)
-        eqs(1)
-        choose(0, 44)
-        op("V", lambda q: q.tensor_copy(T[oc][:, :], T[sel][:, 0:44]), [(sel, 0, 44)], [oc])
-        op("S", lambda q: q.activation(T.gb[:, :], T.bw[:, 0:C].indirect(T[oc][:, 0:22]), copy, scale=4096.0), [("bw", 0, C), oc], ["gb"])
-        for p in range(4):
-            op("S", lambda q: q.activation(T.gp[:, C * p:C * p + C], T.fp[:, C * p:C * p + C].indirect(T[oc][:, 0:22]), copy, scale=0.5), ["fp%d" % p, oc], ["gp%d" % p])
-        op("V", lambda q: q.tensor_tensor(T.gm[:, C:2 * C], T.bw[:, :].indirect(T[oc][:, 22:44]), T.mk[:, C:2 * C], A.mult), ["bw", oc, "mk"], ["gm"])
-        eqs(2)
-        scan("gs", "gs", C, "c01", T.gm[:, C:2 * C], "gm")
-        op("V", lambda q: q.tensor_tensor(T.sm[:, 44:66], T.e3[:, 44:66], T[di][:, 44:66], A.mult), [("e3", 44, 66), di], [("sm", 44, 66)])
-        scan("gsb", "gsb", 0, "c0b", T.gb[:, :], "gb")
-        op("V", lambda q: q.tensor_tensor(T[sel][:, 44:66], T.sm[:, 44:66], T[ba][:, 44:66], A.add), [("sm", 44, 66), ba], [(sel, 44, 66)])
-        op("V", lambda q: q.tensor_tensor(T.tt[:, 0:22], T.gs[:, C + 15:2 * C:16], T[sel][:, 22:44], A.max), ["gs", sel], ["t1"])
-        op("V", lambda q: q.tensor_tensor(T.tt[:, 22:44], T.gsb[:, 15:C:16], T.tt[:, 0:22], A.min), ["gsb", "t1"], ["t2"])
-        op("V", lambda q: q.tensor_tensor(T.t3[:, :], T.tt[:, 22:44], T[sel][:, 44:66], A.max), ["t2", sel], ["t3"])
-        op("V", lambda q: q.tensor_scalar(fi_, T.t3[:, :], 511, None, A.bitwise_and), ["t3"], [fi])
-        op("V", lambda q: q.tensor_copy(fu_, T.fia[:, 22 * t + 11:22 * t + 22]), [fi], [fu])
-        op("V", lambda q: q.tensor_copy(T[f16][:, :], fi_), [fi], [f16])
+        fu_, e_, g_ = T.fua[:, 12 * t:12 * t + 11], T.e16a[:, 22 * t:22 * t + 22], T.g16a[:, 22 * t:22 * t + 22]
+        ba, di, oc, f16, fu, e16, g16 = [n + str(t) for n in ("ba", "di", "oc", "f16", "fu", "e16", "g16")]
+        nb, rep = "ba%d" % (t + 1), "rep%d" % (t + 1)
         dst = T.cores[rank ^ STEP[t]]
         hp = helpers(T, topo, core, dst)
+
+        def half_copy(q0, p, a, b):
+            a, b = C * p + a, C * p + b
+            (cp if q0 == "V" else act)(T.g2[:, a:b], T.gp[:, a:b], ["gp%d" % p], [("g2", a, b)])
+
+        def mix(buf, off, okey, o, p):
+            a, b = C * p + o, C * p + o + H
+            tt(T[buf][:, p:4 * H:4], T.gp[:, C * p:C * p + C].indirect(off), T.g2[:, a:b], A.add, ["gp%d" % p, ("g2", a, b), okey], ["%s_%d" % (buf, p)])
+
+        def zquant(buf, nm):
+            zq, zs = "%sq%d" % (nm, t), "%ss%d" % (nm, t)
+            op("V", lambda q: q.quantize_mx(T[zq][:, :], T[zs][:, :], T[buf][:, :]), ["%s_%d" % (buf, p) for p in range(4)], [zq])
+
+        def lower_quant():
+            zquant("ztl", "zl")
+            for p in range(4):
+                mm(4 + p, "wq", "wsp", 128 * p, "zlq%d" % t, "zls%d" % t, 0, H, ["wq", "wsp", "zlq%d" % t])
+
+        def own_half():
+            for p in range(4):
+                act(T.bp[:, C * p:C * p + H], T["b%d" % (4 + p)][:, 0:H], [], ["b%d" % (4 + p), ("bp%d" % p, 0, H)], scale=0.03125)
+
+        def to_columns(src, key):
+            cp(T.ew[:, :].indirect(T[oc][:, 0:22]), src, [key, oc], ["ew"])
+
+        def places_out():
+            for n, (off, key) in enumerate(((T[oc][:, 0:22], oc), (T[f16][:, 0:22], f16))):
+                act(T.pfo[:, C * n:C * n + C], T.idm[:, :].indirect(off), [key, "idm"], [("pfo", C * n, C * n + C)], F.Identity, bias=MID)
+            dma("Y", T.pf[:, :], T.pfo[0:128:16, :], ["pfo"], ["pf"])
+
+        parts = {
+            "K": lambda: kplus(t + 1, "S"),
+            "R": (lambda: repeat(rep, 0, T[oc][:, 0:22], oc)) if t < 2 else places_out, "Q": lambda: repeat(rep, 1, T[f16][:, 0:22], f16),
+            "P": lambda: compose(t + 1, 0), "p": lambda: lists_scan(0), "p16": lambda: lists_held(t + 1, 0),
+            "F": lambda: compose(t + 1, 1), "f": lambda: lists_scan(1), "f16": lambda: lists_held(t + 1, 1),
+            "b": lambda: ts(T[nb][:, 22:44], T[nb][:, 44:66], T.wt[:, 4:5], None, [A.add], [(nb, 44, 66), "wt2"], [(nb, 22, 44)]),
+            "r0": lambda: rest(t + 1, 0), "r1": lambda: rest(t + 1, 1),
+            "lq": lower_quant, "O": own_half,
+            "T": lambda: act(T.fsr[:, :], T.idm[:, :].indirect(T["fs%d" % t][:, 0:22]), ["fs%d" % t, "idm"], ["fsr"]),
+            "H": lambda: act(T.hr[:, :], T.fsr[:, :].indirect(T[f16][:, 0:22]), ["fsr", f16], ["hr"]),
+            "h": lambda: to_columns(T.hr[:, :], "hr"), "wh": lambda: scan(T.esc[:, :], "esc", T.ew[:, :], "ew"),
+            "g": lambda: to_columns(T[rep][:, C:2 * C], (rep, C, 2 * C)), "wg": lambda: scan(T.gsc[:, :], "gsc", T.ew[:, :], "ew"),
+            "g16": lambda: held(g_, g16, "gsc", "gsc", 0, MID, []),
+            "E": lambda: act(T.hr[:, :], T.fsr[:, :].indirect(g_), ["fsr", g16], ["hr"]),
+            "we": lambda: scan(T.esc[:, :], "esc", T.hr[:, :], "hr"), "e16": lambda: held(e_, e16, "esc", "esc", 0, MID, []),
+            "v": lambda: op("V", lambda q: q.quantize_mx(T.vq[:, :], T.vs[:, :], T.vt[:, :]), ["vt"], ["vq"]),
+        }
+        for p in range(4):
+            parts["c%d" % p] = lambda p=p: half_copy("V", p, 0, C)
+            parts["u%d" % p] = lambda p=p: half_copy("V", p, H, C)
+            parts["m%d" % p] = lambda p=p: half_copy("V", p, 0, H)
+            parts["L%d" % p] = lambda p=p: half_copy("S", p, 0, H)
+            parts["l%d" % p] = lambda p=p: mix("ztl", T[f16][:, 0:11], f16, 0, p)
+
+        def run(names):
+            for n in names.split():
+                parts[n]()
+
+        tt(T.am[:, :], T.sa[:, :].indirect(p16), T.mra[:, C * t:C * t + C], A.mult, ["sa", p16key, "mr%d" % t], ["am"])
+        if t == 0:
+            lists_scan(1)
+        else:
+            rest(t, 2)
+        tt(T.bw[:, 512:864], T.sa[:, :].indirect(T.pka[:, 22 * t:22 * t + 22]), T.am[:, :], A.mult, ["sa", "pk16%d" % t, "am"], [("bw", 512, 864)])
+        if t == 0:
+            lists_held(0, 1)
+        else:
+            rest(t, 3)
+        scan(T.sE[:, :], "sE", T.bw[:, 512:864], ("bw", 512, 864))
+        for n in range(5) if t == 0 else (4,):
+            rest(t, n)
+        run(SEQ[t]["idle"])
+        ts(T.e3[:, :], T.sE[:, 15:C:16], 0.0, None, [A.is_gt], ["sE"], ["e3"])
+        for n in range(3):
+            a, b = 22 * n, 22 * n + 22
+            tt(T.sm[:, a:b], T.e3[:, :], T[di][:, a:b], A.mult, ["e3", di], [("sm", a, b)])
+        tt(T[nb][:, 0:44], T.sm[:, 0:44], T[ba][:, 0:44], A.add, [("sm", 0, 44), ba], [(nb, 0, 44)])
+        tt(T.tt[:, 44:66], T.sm[:, 44:66], T[ba][:, 44:66], A.add, [("sm", 44, 66), ba], ["alt"])
+        ts(T[oc][:, :], T[nb][:, 0:44], up, None, [A.subtract], [(nb, 0, 44), "wt1"], [oc])
+        act(T.gb[:, :], T.bw[:, 0:C].indirect(T[oc][:, 0:22]), [("bw", 0, C), oc], ["gb"], scale=UP)
+        for p in range(4):
+            act(T.gp[:, C * p:C * p + C], T.fp[:, C * p:C * p + C].indirect(T[oc][:, 0:22]), ["fp%d" % p, oc], ["gp%d" % p], scale=0.5)
+        cp(T.gm[:, :], T.bw[:, :].indirect(T[oc][:, 22:44]), ["bw", oc], ["gm"])
+        op("V", lambda q: q.tensor_tensor_scan(T.gs[:, :], T.ch[:, :], T.gm[:, :], 0.0, A.add, A.max), ["ch", "gm"], ["gs"])
+        scan(T.gsb[:, :], "gsb", T.gb[:, :], "gb")
+        run(GAPS[0])
+        tt(T.tt[:, 0:22], T.gs[:, 15:C:16], T[nb][:, 22:44], A.max, ["gs", (nb, 22, 44)], ["t1"])
+        run(GAPS[1])
+        tt(T.tt[:, 22:44], T.gsb[:, 15:C:16], T.tt[:, 0:22], A.min, ["gsb", "t1"], ["t2"])
+        run(GAPS[2])
+        tt(T.t3[:, :], T.tt[:, 22:44], T.tt[:, 44:66], A.max, ["t2", "alt"], ["t3"])
+        run(GAPS[3])
+        ts(T[nb][:, 44:66], T.t3[:, :], 511, None, [A.bitwise_and], ["t3"], [(nb, 44, 66)])
+        run(GAPS[4])
+        cp(T[f16][:, :], T[nb][:, 44:66], [(nb, 44, 66)], [f16])
+        cp(fu_, T[nb][:, 55:66], [(nb, 44, 66)], [fu])
         if hp:
             halves = []
             for n, (c, (a, b)) in enumerate(zip((hp[0], hp[-1]), CUT)):
@@ -395,112 +456,50 @@ def rank_program(g, core, T, topo):
             sends([f16], 16, lambda: g.remote_dma_fused(halves, local_sem=T.sem.rl))
         else:
             sends([f16], bits(topo, core, dst)[1], lambda: send(g, T, topo, core, dst, T["fs%d" % t][:, 0:22], T[f16][:, 0:22], "la%d" % t))
-        for p in POOL:
-            a, b = C * p, C * p + H
-            op("G", lambda q: q.affine_select(T.g2[:, a:b], T.gp[:, a:b], [[0, H]], A.is_ge, 0.0, 1, 0), ["gp%d" % p], [("g2", a, b)])
-        for half, (buf, off, o, nm) in enumerate((("ztu", fu_, H, "zu"), ("ztl", T[f16][:, 0:11], 0, "zl"))):
-            zq, zs = "%sq%d" % (nm, t), "%ss%d" % (nm, t)
-            for p in range(4):
-                a, b = C * p + o, C * p + o + H
-                if half == 1 and p not in POOL:
-                    op("S", lambda q: q.activation(T.g2[:, a:b], T.gp[:, a:b], copy), ["gp%d" % p], [("g2", a, b)])
-            for p in range(4):
-                for n in ((0, 1), (2,), (3,), ())[p] if half == 0 else ():
-                    a, b = C * n + o, C * n + o + H
-                    op("V", lambda q: q.tensor_copy(T.g2[:, a:b], T.gp[:, a:b]), ["gp%d" % n], [("g2", a, b)])
-                a, b = C * p + o, C * p + o + H
-                op("V", lambda q: q.tensor_tensor(T[buf][:, p:4 * H:4], T.gp[:, C * p:C * p + C].indirect(off), T.g2[:, a:b], A.add), ["gp%d" % p, ("g2", a, b), f16, fu], ["%s_%d" % (buf, p)])
-            op("V", lambda q: q.quantize_mx(T[zq][:, :], T[zs][:, :], T[buf][:, :]), ["%s_%d" % (buf, p) for p in range(4)], [zq])
-            if half == 0 and not hp:
-                k = bits(topo, core, dst)[1]
-                sends([zq], k, lambda: send(g, T, topo, core, dst, T["zrq%d" % t][:, 0:H].bitcast(dt.uint8), T[zq][:, 0:H].bitcast(dt.uint8), "za%d" % t))
-                sends([zq], k, lambda: send(g, T, topo, core, dst, T["zrs%d" % t][:, 0:H], T[zs][:, 0:H], "za%d" % t))
-            elif half == 0:
-                sends([zq], bits(topo, core, hp[0])[1], lambda: send(g, T, topo, core, hp[0], T.hq[:, 0:H].bitcast(dt.uint8), T[zq][:, 0:H].bitcast(dt.uint8), "hca"))
-                sends([zq], bits(topo, core, hp[-1])[1], lambda: send(g, T, topo, core, hp[-1], T.hs[:, 0:H], T[zs][:, 0:H], "hsa"))
-        rep = "rep%d" % (t + 1)
-        op("S", lambda q: q.activation(T[rep][:, 0:C], T.idx[:, :].indirect(T[oc][:, 0:22]), copy), [oc, "idx"], [(rep, 0, C)])
-        op("S", lambda q: q.activation(T[rep][:, C:2 * C], T.idx[:, :].indirect(T[f16][:, 0:22]), copy), [f16, "idx"], [(rep, C, 2 * C)])
         for p in range(4):
-            mm(4 + p, "wq", "wsp", 128 * p, "zlq%d" % t, "zls%d" % t, 0, H, ["wq", "wsp", "zlq%d" % t])
-        def own_half():
-            for p in range(4):
-                op("S", lambda q: q.activation(T.bp[:, C * p:C * p + H], T["b%d" % (4 + p)][:, 0:H], copy, scale=0.03125), [], ["b%d" % (4 + p), ("bp%d" % p, 0, H)])
-
-        def theirs():
-            op("S", lambda q: q.activation(T.fsr[:, :], T.idx[:, :].indirect(T["fs%d" % t][:, 0:22]), copy), ["fs%d" % t, "idx"], ["fsr"])
-
-        def wrapped(src, key, out, okey):
-            scan("esc", "esc", 0, "ck", src, key)
-            op("V", lambda q: q.tensor_scalar(out, T.esc[:, 15:C:16], T.wt[:, 0:1], None, A.mult), ["esc", "wt0"], [okey])
-
-        def inverse(src, key):
-            op("V", lambda q: q.tensor_copy(T.ew[:, :].indirect(T[oc][:, 0:22]), src), [key, oc], ["ew"])
-
-        def by_place():
-            op("S", lambda q: q.activation(T.hr[:, :], T.fsr[:, :].indirect(T[f16][:, 0:22]), copy), ["fsr", f16], ["hr"])
-
-        def by_column():
-            op("S", lambda q: q.activation(T.hr[:, :], T[rep][:, C:2 * C].indirect(T.rf16[:, 0:22]), copy), [(rep, C, 2 * C), "rf16"], ["hr"])
-
-        def looked_up():
-            op("S", lambda q: q.activation(T.hr[:, :], T.fsr[:, :].indirect(T.pp16[:, 0:22]), copy), ["fsr", "pp16"], ["hr"])
-
-        def place_of():
-            inverse(T.idx[:, :], "idx")
-            wrapped(T.ew[:, :], "ew", T.rf16[:, :], "rf16")
-
-        def to_columns():
-            inverse(T.hr[:, :], "hr")
-            wrapped(T.ew[:, :], "ew", e_, "e16%d" % t)
-        parts = {
-            "P": lambda: compose(t + 1, rep, 0), "p": lambda: lists_scan(t + 1, 0),
-            "F": lambda: compose(t + 1, rep, 1), "f": lambda: lists_scan(t + 1, 1),
-            "b": lambda: lists_base(t + 1, T[sel][:, 0:22], (sel, 0, 22), fi_, fi), "K": lambda: kplus(t + 1, "S"), "r": lambda: lists_rest(t + 1),
-            "i": place_of, "C": by_column, "c": lambda: wrapped(T.hr[:, :], "hr", T.pp16[:, :], "pp16"),
-            "T": theirs, "E": looked_up, "e": lambda: wrapped(T.hr[:, :], "hr", e_, "e16%d" % t),
-            "H": by_place, "h": to_columns, "O": own_half,
-            "v": lambda: op("V", lambda q: q.quantize_mx(T.vq[:, :], T.vs[:, :], T.vt[:, :]), ["vt"], ["vq"]),
-        }
-        for n in SEQ[t][0]:
-            parts[n]()
+            run(GAPS[5 + p])
+            mix("ztu", fu_, fu, H, p)
+        zquant("ztu", "zu")
+        zq, zs = "zuq%d" % t, "zus%d" % t
+        if not hp:
+            k = bits(topo, core, dst)[1]
+            sends([zq], k, lambda: send(g, T, topo, core, dst, T["zrq%d" % t][:, 0:H].bitcast(dt.uint8), T[zq][:, 0:H].bitcast(dt.uint8), "za%d" % t))
+            sends([zq], k, lambda: send(g, T, topo, core, dst, T["zrs%d" % t][:, 0:H], T[zs][:, 0:H], "za%d" % t))
+        else:
+            sends([zq], bits(topo, core, hp[0])[1], lambda: send(g, T, topo, core, hp[0], T.hq[:, 0:H].bitcast(dt.uint8), T[zq][:, 0:H].bitcast(dt.uint8), "hca"))
+            sends([zq], bits(topo, core, hp[-1])[1], lambda: send(g, T, topo, core, hp[-1], T.hs[:, 0:H], T[zs][:, 0:H], "hsa"))
+        run(SEQ[t]["z"])
         for p in range(4 - XS[t], 4):
-            unpack(t, p, 0, C)
-        if t == 2:
-            dma("Y", T.pf[:, :], T[rep][0:128:16, :], [rep], ["pf"])
+            unpack(t, p)
         for p in range(4):
             mm(p, "wq", "wsp", 128 * p, "zrq%d" % t, "zrs%d" % t, 0, H, ["wq", "wsp", "zr%d" % t])
-            o, i_ = T.bp[:, C * p + H:C * p + C], T["b%d" % p][:, 0:H]
-            if p not in EV:
-                op("S", lambda q: q.activation(o, i_, copy, scale=0.03125), [], ["b%d" % p, ("bp%d" % p, H, C)])
-            else:
-                op("V", lambda q: q.tensor_scalar(o, i_, 0.03125, None, A.mult), [], ["b%d" % p, ("bp%d" % p, H, C)])
+            act(T.bp[:, C * p + H:C * p + C], T["b%d" % p][:, 0:H], [], ["b%d" % p, ("bp%d" % p, H, C)], scale=0.03125)
         for i, (a, b) in enumerate(CH):
             e = T.e16a[:, 22 * t + a // 16:22 * t + b // 16]
             for p in range(4 - XS[t], 4):
-                op("S", lambda q: q.activation(T.bg[:, C * p + a:C * p + b], T.bp[:, C * p:C * p + C].indirect(e), copy), ["bp%d" % p, "e16%d" % t], [("bg%d" % p, a, b)])
-        for n in SEQ[t][1]:
-            parts[n]()
+                act(T.bg[:, C * p + a:C * p + b], T.bp[:, C * p:C * p + C].indirect(e), ["bp%d" % p, e16], [("bg%d" % p, a, b)])
+        run(SEQ[t]["x"])
         for i, (a, b) in enumerate(CH):
+            e = T.e16a[:, 22 * t + a // 16:22 * t + b // 16]
             for p in range(4):
+                o = T.xt[:, 4 * a + p:4 * b:4]
                 if p >= 4 - XS[t]:
-                    op("V", lambda q: q.tensor_tensor(T.xt[:, 4 * a + p:4 * b:4], T["b%d" % (4 + p)][:, a:b], T.bg[:, C * p + a:C * p + b], A.add),
-                       [("bg%d" % p, a, b)], ["b%d" % (4 + p), ("xt%d" % p, a, b)])
-                    continue
-                op("V", lambda q: q.tensor_tensor(T.xt[:, 4 * a + p:4 * b:4], T.bp[:, C * p:C * p + C].indirect(T.e16a[:, 22 * t + a // 16:22 * t + b // 16]), T.fp[:, C * p + a:C * p + b], A.add),
-                   ["bp%d" % p, "e16%d" % t, ("fp%d" % p, a, b)], [("xt%d" % p, a, b)])
+                    tt(o, T["b%d" % (4 + p)][:, a:b], T.bg[:, C * p + a:C * p + b], A.add, [("bg%d" % p, a, b)], ["b%d" % (4 + p), ("xt%d" % p, a, b)])
+                else:
+                    tt(o, T.bp[:, C * p:C * p + C].indirect(e), T.fp[:, C * p + a:C * p + b], A.add, ["bp%d" % p, e16, "fp%d" % p], [("xt%d" % p, a, b)])
             quant(t + 1, i, "xt", [("xt%d" % p, a, b) for p in range(4)])
             if t < 2:
-                head(t + 1, i)
+                signs(t + 1, i)
+                if i == 1:
+                    values(t + 1)
+                run(SEQ[t]["mid" if i == 0 else "end"])
             else:
-                xq, xs = "xq%d" % 3, "xs%d" % 3
-                mm(4 + i, "vq", "vs", 0, xq, xs, a, b, ["vq", (xq, a, b)])
+                xq, xs = "xq3", "xs3"
+                mm(i, "vq", "vs", 0, xq, xs, a, b, ["vq", (xq, a, b)])
                 dma("Y", T.oc[:, 4 * a:4 * b], T[xq][:, a:b].bitcast(dt.uint8), [(xq, a, b)], ["ocout%d" % i])
-                op("S", lambda q: q.activation(T.yt[:, a:b], T["b%d" % (4 + i)][:, 0:b - a], copy), [], ["b%d" % (4 + i), ("yt", a, b)])
-                dma("S", T.y[:, a:b], T.yt[:, a:b], [("yt", a, b)], ["yout%d" % i])
                 for k in range(4):
-                    dma("Y" if k < 3 else "S", T.osc[4 * k:4 * k + 4, a:b], T[xs][32 * k:32 * k + 4, a:b], [(xq, a, b)], ["oscout%d%d" % (i, k)])
-        for n in SEQ[t][2]:
-            parts[n]()
+                    dma("Y" if k < 2 or i == 0 else "S", T.osc[4 * k:4 * k + 4, a:b], T[xs][32 * k:32 * k + 4, a:b], [(xq, a, b)], ["oscout%d%d" % (i, k)])
+                (act if i == 0 else cp)(T.yt[:, a:b], T["b%d" % i][:, 0:b - a], [], ["b%d" % i, ("yt", a, b)])
+                dma("Y" if i == 0 else "S", T.y[:, a:b], T.yt[:, a:b], [("yt", a, b)], ["yout%d" % i])
         p16, p16key = T[oc][:, 0:22], oc
     finish()

@@ -6,16 +6,20 @@ N, C, H = 8, 352, 176
 STEP = [4, 1, 2]
 CH = [(0, 224), (224, 352)]
 CUT = ((0, 11), (11, 22))
-XS = [1, 1, 1]
+HQ = 132
 BIG = 2.0 ** 20
-UP = 4096.0
+W0 = 2.0 ** 18
+UP = 2.0 ** 19
 MID = 176.0
-SEQ = [
-    dict(idle="K", z="L2 L3 Q R l0 l1 P l2 l3 lq F g wg O b g16 T E p we p16 e16", x="", mid="", end="f f16 r0 r1"),
-    dict(idle="K", z="L2 L3 Q R l0 l1 T l2 l3 H lq O h wh b P e16", x="F", mid="p p16", end="f f16 r0 r1"),
-    dict(idle="", z="L2 L3 Q R l0 l1 l2 l3 lq O g wg v g16 T E we e16", x="", mid="", end=""),
+MIX = " S oc gm gs gsb t1 t2 c0 t3 and c1 f16 fu z0 u2 z1 u3 z2 z3 "
+NEW = " B0 B1 B2 B3 s20 s30 s21 s31 x00 x10 x01 a20 a30 x11 q0 a21 a31 "
+NEXT = " F0 F1 F2 F3"
+ORDER = [
+    "p16 R k16 f16 uo Q e0 Kv P ba bc uq qk ua e1 F us w0 q0 w1 q1 hx e2 hp r0 e3 r1 bp r2 ch" + NEXT,
+    "am r3 bw K M D sE" + MIX + "R L2 L3 Q F l0 zq l1 l2 l3 P lq g w1 O wg w0 g16 hx T E r0 ba r1 bc r2 bp r3 U2 U3 we D e16" + NEW + "hp q1 M" + NEXT,
+    "am bw sE K" + MIX + "R L2 L3 Q l0 zq P T Hb l1 l2 l3 bp lq Ha h bc O U2 U3 wh F w0 e16 w1" + NEW + "hx q1 r0 hp r1 ba r2" + NEXT,
+    "am r3 bw M D sE" + MIX + "L2 L3 Q l0 zq R l1 l2 l3 v lq O U2 U3 g wg g16 Ta Tb Ea Eb we e16" + NEW + "q1",
 ]
-GAPS = ["", "", "c0", "", "", "c1 u2", "", "u3", ""]
 
 SCRATCH = {
     "xin": ("sbuf", [128, 4 * C], "bfloat16"), "xt": ("sbuf", [128, 4 * C], "bfloat16"),
@@ -30,17 +34,19 @@ SCRATCH = {
     "pp16": ("sbuf", [128, 22], "uint16"), "rf16": ("sbuf", [128, 22], "uint16"), "pr16": ("sbuf", [128, 66], "uint16"),
     "idm": ("sbuf", [128, C], "bfloat16"), "ck": ("sbuf", [128, C], "bfloat16"), "ch": ("sbuf", [128, C], "bfloat16"),
     "pm": ("sbuf", [128, 22], "int32"), "mo": ("sbuf", [128, 22], "uint16"), "d16": ("sbuf", [128, 16], "int32"),
-    "pat": ("sbuf", [128, 96], "float32"), "wt": ("sbuf", [128, 12], "float32"), "c4": ("sbuf", [128, 4], "float32"),
+    "pat": ("sbuf", [128, 96], "float32"), "wt": ("sbuf", [128, 16], "float32"),
     "uoi": ("sbuf", [128, 16], "int32"), "uo": ("sbuf", [128, 16], "uint16"),
     "q16": ("sbuf", [128, 66], "int32"), "qk": ("sbuf", [128, 66], "float32"),
-    "sa": ("sbuf", [128, C], "bfloat16"), "bw": ("sbuf", [128, 864], "float32"), "am": ("sbuf", [128, C], "float32"),
-    "sE": ("sbuf", [128, C], "float32"), "e3": ("sbuf", [128, 22], "float32"), "sm": ("sbuf", [128, 66], "float32"),
+    "sa": ("sbuf", [128, C], "bfloat16"), "sb": ("sbuf", [128, C], "bfloat16"), "am": ("sbuf", [128, C], "float32"), "bw": ("sbuf", [128, C], "float32"),
+    "sE": ("sbuf", [128, 3 * C], "float32"), "dz": ("sbuf", [128, 198], "float32"), "sz": ("sbuf", [128, 198], "float32"),
     "gm": ("sbuf", [128, C], "float32"), "gs": ("sbuf", [128, C], "float32"),
     "gb": ("sbuf", [128, C], "bfloat16"), "gsb": ("sbuf", [128, C], "bfloat16"),
-    "tt": ("sbuf", [128, 66], "float32"), "t3": ("sbuf", [128, 22], "int32"),
+    "tt": ("sbuf", [128, 66], "float32"), "t3": ("sbuf", [128, 22], "int32"), "fi": ("sbuf", [128, 22], "int32"),
+    "wi": ("sbuf", [128, C], "float32"), "wj": ("sbuf", [128, C], "float32"), "ji": ("sbuf", [128, 44], "int32"),
+    "iv": ("sbuf", [128, 66], "uint16"),
     "pkf": ("sbuf", [128, 2 * C], "bfloat16"), "sp": ("sbuf", [128, 2 * C], "bfloat16"),
-    "x1": ("sbuf", [128, 66], "int32"), "xx": ("sbuf", [128, 22], "float32"), "nn": ("sbuf", [128, 22], "int32"),
-    "fsr": ("sbuf", [128, C], "bfloat16"), "hr": ("sbuf", [128, C], "bfloat16"), "ew": ("sbuf", [128, C], "bfloat16"),
+    "x1": ("sbuf", [128, 66], "float32"), "ba": ("sbuf", [128, 66], "float32"), "xx": ("sbuf", [128, 22], "float32"), "nn": ("sbuf", [128, 22], "int32"),
+    "fsr": ("sbuf", [128, C], "bfloat16"), "hr": ("sbuf", [128, C], "bfloat16"), "h2": ("sbuf", [128, C], "bfloat16"), "ew": ("sbuf", [128, C], "bfloat16"),
     "esc": ("sbuf", [128, C], "bfloat16"), "gsc": ("sbuf", [128, C], "bfloat16"),
     "fp": ("sbuf", [128, 4 * C], "bfloat16"), "gp": ("sbuf", [128, 4 * C], "bfloat16"), "bp": ("sbuf", [128, 4 * C], "bfloat16"),
     "bg": ("sbuf", [128, 4 * C], "bfloat16"), "g2": ("sbuf", [128, 4 * C], "bfloat16"),
@@ -55,7 +61,6 @@ for k in range(8):
 for k in range(4):
     SCRATCH["xq%d" % k] = ("sbuf", [128, C], "float8_e4m3fn_x4")
     SCRATCH["xs%d" % k] = ("sbuf", [128, C], "uint8")
-    SCRATCH["ba%d" % k] = ("sbuf", [128, 66], "int32")
     SCRATCH["rep%d" % k] = ("sbuf", [128, 2 * C], "bfloat16")
 for k in range(3):
     for nm in ("zu", "zl", "zr"):
@@ -64,7 +69,6 @@ for k in range(3):
     SCRATCH["oc%d" % k] = ("sbuf", [128, 44], "uint16")
     SCRATCH["f16%d" % k] = ("sbuf", [128, 22], "uint16")
     SCRATCH["fs%d" % k] = ("sbuf", [128, 22], "uint16")
-    SCRATCH["di%d" % k] = ("sbuf", [128, 66], "float32")
 
 ENG = {"V": "sv", "S": "ss", "P": "st", "G": "sg"}
 SEMAPHORES = ["sv", "ss", "st", "sg", "rl", "hla", "hca", "hsa"] + ["la%d" % k for k in range(3)] + ["za%d" % k for k in range(3)] + ["d%d" % k for k in range(40)]
@@ -152,32 +156,44 @@ def helpers(T, topo, src, dst):
     return [c for c in topo.cores_of(src) if c not in T.cores and topo.die(c) == topo.die(src) and topo.may_write(c, dst)][:2]
 
 
-def send(g, T, topo, src, dst, out, in_, rsem, n=16):
+def send(g, T, topo, src, dst, out, in_, rsem):
     rid, pid = topo.addr(dst, src)
-    m, k = bits(topo, src, dst, n)
+    m, k = bits(topo, src, dst)
     g.remote_dma(out_ap=out, in_ap=in_, remote_sem=T.sem[rsem], local_sem=T.sem.rl, pid=pid, routing_id=rid, dma_engine_mask=m)
     return k
+
+
+def send_two(g, T, topo, src, pieces):
+    both = []
+    for n, (dst, out, in_, rsem) in enumerate(pieces):
+        rid, pid = topo.addr(dst, src)
+        k = bits(topo, src, dst)[1] // 2
+        both.append(RemoteDMATransfer(dst_ids=[DstId(rid=rid, pnc=pid)], dma_engine_mask=bits(topo, src, dst, k, k * n)[0], remote_sem=T.sem[rsem], src=in_, dst=out))
+    g.remote_dma_fused(both, local_sem=T.sem.rl)
+    return 2 * k
+
+
+def codes(buf, a, b):
+    return buf[:, a:b].bitcast(dt.uint8)
 
 
 def hand_on(g, core, T, topo):
     n = [0]
     for r, src in enumerate(T.cores):
-        for s in STEP:
+        for t, s in enumerate(STEP):
             dst = T.cores[r ^ s]
             hp = helpers(T, topo, src, dst)
             if core not in hp:
                 continue
-            t, k = STEP.index(s), bits(topo, src, core)[1]
-            mine = [ab for c, ab in zip((hp[0], hp[-1]), CUT) if c == core]
-            g.wait_ge(T.sem.hla, 8 * len(mine))
-            for a, b in mine:
-                n[0] += send(g, T, topo, core, dst, T["fs%d" % t][:, a:b], T.hl[:, a:b], "la%d" % t)
+            k, zq, zs, za = bits(topo, src, core)[1], T["zrq%d" % t], T["zrs%d" % t], "za%d" % t
+            a, b = CUT[hp.index(core)]
+            g.wait_ge(T.sem.hla, k // 2)
+            n[0] += send(g, T, topo, core, dst, T["fs%d" % t][:, a:b], T.hl[:, a:b], "la%d" % t)
+            g.wait_ge(T.sem.hca, k)
             if core == hp[0]:
-                g.wait_ge(T.sem.hca, k)
-                n[0] += send(g, T, topo, core, dst, T["zrq%d" % t][:, 0:H].bitcast(dt.uint8), T.hq[:, 0:H].bitcast(dt.uint8), "za%d" % t)
-            if core == hp[-1]:
-                g.wait_ge(T.sem.hsa, k)
-                n[0] += send(g, T, topo, core, dst, T["zrs%d" % t][:, 0:H], T.hs[:, 0:H], "za%d" % t)
+                n[0] += send(g, T, topo, core, dst, codes(zq, 0, HQ), codes(T.hq, 0, HQ), za)
+            else:
+                n[0] += send_two(g, T, topo, core, [(dst, codes(zq, HQ, H), codes(T.hq, HQ, H), za), (dst, zs[:, 0:H], T.hs[:, 0:H], za)])
     if n[0]:
         g.wait_ge(T.sem.rl, n[0])
 
@@ -193,19 +209,19 @@ def rank_program(g, core, T, topo):
         src = T.cores[rank ^ STEP[t]]
         hp = helpers(T, topo, src, core)
         if hp:
-            lands("fs%d" % t, "la%d" % t, bits(topo, hp[0], core)[1] + bits(topo, hp[-1], core)[1])
-            lands("zr%d" % t, "za%d" % t, bits(topo, hp[0], core)[1] + bits(topo, hp[-1], core)[1])
+            lands("fs%d" % t, "la%d" % t, sum(bits(topo, c, core)[1] for c in hp))
+            lands("zr%d" % t, "za%d" % t, sum(bits(topo, c, core)[1] for c in hp))
         else:
             lands("fs%d" % t, "la%d" % t, bits(topo, src, core)[1])
             lands("zr%d" % t, "za%d" % t, 2 * bits(topo, src, core)[1])
 
     dma("S", T.ppi[:, :], T.pp[:, :], [], ["ppi"])
-    dma("Y", T.ut[:, :], T.u[:, :], [], ["ut"])
-    dma("S", T.pri[:, :], T.pr[:, :], [], ["pri"])
-    for i, (a, b) in enumerate(CH):
-        dma("Y", T.xin[:, 4 * a:4 * b], T.x[:, 4 * a:4 * b], [], ["xin%d" % i])
+    dma("Y", T.pri[:, :], T.pr[:, :], [], ["pri"])
     dma("S", T.rfi[:, :], T.rf[:, :], [], ["rfi"])
-    dma("Y", T.wq[:, 0:512].bitcast(dt.uint8), T.wc[:, :], ["xin1"], ["wq"])
+    dma("Y", T.ut[:, :], T.u[:, :], [], ["ut"])
+    for i, (a, b) in enumerate(CH):
+        dma("Y", T.xin[:, 4 * a:4 * b], T.x[:, 4 * a:4 * b], [], [("xin", a, b)])
+    dma("Y", codes(T.wq, 0, 512), T.wc[:, :], ["xin"], ["wq"])
     dma("Y", T.wsp[:, 0:512], T.ws[:, :], [], ["wsp"])
     dma("Y", T.vt[:, :], T.v[:, :], [], ["vt"])
 
@@ -221,136 +237,148 @@ def rank_program(g, core, T, topo):
     def act(out, in_, rd, wr, func=copy, **kw):
         op("S", lambda q: q.activation(out, in_, func, **kw), rd, wr)
 
-    op("G", lambda q: q.iota(T.pm[:, :], [[0, 22]], 0, 1), [], ["pm"])
-    op("G", lambda q: q.iota(T.d16[:, :], [[1, 16]], 128, -1), [], ["d16"])
-    op("G", lambda q: q.iota(T.idm[:, :], [[1, C]], -int(MID), 0, allow_small_or_imprecise_dtypes=True), [], ["idm"])
-    op("G", lambda q: q.iota(T.uoi[:, :], [[1, 2], [16, 8]], 0, 0), [], ["uoi"])
-    op("G", lambda q: q.iota(T.c4[:, :], [[512, 2], [int(MID), 2]], 0, 0, allow_small_or_imprecise_dtypes=True), [], ["c4"])
-    op("V", lambda q: q.memset(T.one[:, :], 1.0), [], ["one"])
-    op("V", lambda q: q.memset(T.et[:, :], 0.0), [], ["et"])
+    def fill(ap, v, wr):
+        op("V", lambda q: q.memset(ap, v), [], wr)
+
+    def iota(out, pattern, base, step, wr, **kw):
+        op("G", lambda q: q.iota(out, pattern, base, step, **kw), [], wr)
+
+    def quantize(cq, cs, tile, rd, wr):
+        op("V", lambda q: q.quantize_mx(cq, cs, tile), rd, wr)
+
+    def scan(out, okey, data, dkey, fac="ck", ops=(A.mult, A.add)):
+        op("V", lambda q: q.tensor_tensor_scan(out, T[fac][:, :], data, 0.0, *ops), [fac, dkey], [okey])
+
+    down, half_down, rk, o_, half_o, mid_o, full_o, qo = [T.wt[:, n:n + 1] for n in range(8)]
+    loose = dict(allow_small_or_imprecise_dtypes=True)
+    iota(T.pm[:, :], [[0, 22]], 0, 1, ["pm"])
+    iota(T.d16[:, :], [[1, 16]], 128, -1, ["d16"])
+    iota(T.idm[:, :], [[1, C]], -int(MID), 0, ["idm"], **loose)
+    iota(T.uoi[:, :], [[1, 2], [16, 8]], 0, 0, ["uoi"])
+    fill(T.one[:, :], 1.0, ["one"])
+    fill(T.et[:, :], 0.0, ["et"])
     op("G", lambda q: q.affine_select(T.et[:, 3:515:4], T.one[:, :], [[-1, 128]], A.is_equal, 0.0, 0, 1), ["one"], ["et"])
-    op("G", lambda q: q.iota(T.q16[:, :], [[0, 3], [16, 22]], 352 - 512, 0), [], ["q16"])
+    iota(T.q16[:, :], [[0, 3], [16, 22]], 0, 0, ["q16"])
     ts(T.pm[:, :], T.pm[:, :], 15, None, [A.bitwise_and], ["pm"], ["pm"])
+    fill(T.sE[:, 13:3 * C:48], 0.0, ["sE0"])
     ts(T.d16[:, :], T.d16[:, :], 15, None, [A.bitwise_and], ["d16"], ["d16"])
     cp(T.mo[:, :], T.pm[:, :], ["pm"], ["mo"])
+    ts(T.wt[:, 8:9], T.pm[:, 0:1], 15.0, UP, [A.not_equal, A.mult], ["pm"], ["wt8"])
+    ts(T.wt[:, 9:10], T.pm[:, 0:1], 15.0, 1.0 - 1.0 / BIG, [A.is_equal, A.mult], ["pm"], ["wt9"])
     ts(T.pat[:, 0:16], T.d16[:, :], 1.0, BIG - 1.0, [A.is_equal, A.mult], ["d16"], ["pat0"])
     ts(T.pat[:, 16:32], T.d16[:, :], 1.0, None, [A.min], ["d16"], ["pat1"])
-    ts(T.wt[:, 1:2], T.pm[:, 0:1], 15.0, UP, [A.not_equal, A.mult], ["pm"], ["wt1"])
-    tt(T.pat[:, 32:48], T.pat[:, 0:16], T.pat[:, 16:32], A.add, ["pat0", "pat1"], ["pat2"])
-    ts(T.wt[:, 8:9], T.pm[:, 0:1], 15.0, 1.0 - 1.0 / BIG, [A.is_equal, A.mult], ["pm"], ["wt8"])
-    act(T.ck[:, :], T.pat[:, 32:48].indirect(T.mo[:, 0:22]), ["pat2", "mo"], ["ck"])
     ts(T.pat[:, 48:64], T.d16[:, :], 1.0, UP, [A.is_equal, A.mult], ["d16"], ["pat3"])
     ts(T.pat[:, 64:80], T.d16[:, :], 0.0, -8.0 * UP, [A.is_equal, A.mult], ["d16"], ["pat4"])
-    ts(T.wt[:, 0:1], T.wt[:, 8:9], 1.0 / BIG, None, [A.add], ["wt8"], ["wt0"])
-    ts(T.wt[:, 6:7], T.pm[:, 0:1], T.wt[:, 1:2], None, [A.subtract], ["pm", "wt1"], ["wt6"])
+    ts(o_, T.wt[:, 8:9], 512.0, None, [A.add], ["wt8"], ["o"])
+    tt(T.pat[:, 32:48], T.pat[:, 0:16], T.pat[:, 16:32], A.add, ["pat0", "pat1"], ["pat2"])
+    act(T.ck[:, :], T.pat[:, 32:48].indirect(T.mo[:, 0:22]), ["pat2", "mo"], ["ck"])
+    ts(down, T.wt[:, 9:10], 1.0 / BIG, None, [A.add], ["wt9"], ["down"])
+    ts(half_down, T.wt[:, 9:10], 1.0 / BIG, 0.5, [A.add, A.mult], ["wt9"], ["half_down"])
+    ts(rk, T.wt[:, 9:10], 1.0 / BIG, 1.0 / (W0 + MID), [A.add, A.mult], ["wt9"], ["rk"])
+    ts(half_o, T.wt[:, 8:9], 512.0, 0.5, [A.add, A.mult], ["wt8"], ["half_o"])
+    ts(mid_o, T.wt[:, 8:9], 512.0 + MID, 0.5, [A.add, A.mult], ["wt8"], ["mid_o"])
+    ts(full_o, T.wt[:, 8:9], 512.0 + MID, None, [A.add], ["wt8"], ["full_o"])
+    ts(T.wt[:, 10:11], T.pm[:, 0:1], o_, 352.0, [A.subtract, A.add], ["pm", "o"], ["wt10"])
     tt(T.pat[:, 80:96], T.pat[:, 48:64], T.pat[:, 64:80], A.add, ["pat3", "pat4"], ["pat5"])
-    op("V", lambda q: q.memset(T.bw[:, C:512], 0.0), [], [("bw", C, 512)])
-    down, up = T.wt[:, 0:1], T.wt[:, 1:2]
-
-    def quant(t, i, buf, keys):
-        a, b = CH[i]
-        op("V", lambda q: q.quantize_mx(T["xq%d" % t][:, a:b], T["xs%d" % t][:, a:b], T[buf][:, 4 * a:4 * b]), keys, [("xq%d" % t, a, b)])
+    fill(T.dz[:, 1:198:3], 0.0, ["dz0"])
+    ts(T.sE[:, 29:3 * C:48], T.pm[:, :], 0.0, rk, [A.mult, A.add], ["pm", "rk"], ["sE1"])
 
     def mm(bank, side, scale, c0, rq, rs, a, b, rd):
         op("P", lambda q: q.matmul_mx(T["b%d" % bank][:, 0:b - a], T[side][:, c0:c0 + 128], T[scale][:, c0:c0 + 128],
                                       T[rq][:, a:b], T[rs][:, a:b], True, True), rd, ["b%d" % bank])
 
-    def unpack(t, p):
-        mm(4 + p, "eq", "es", 128 * p, "xq%d" % t, "xs%d" % t, 0, C, ["eq%d" % p, "xq%d" % t])
+    def held(out, okey, view, key, mul, mkey, add, akey):
+        ts(out, view, mul, add, [A.mult, A.add], [key, mkey] + akey, [okey])
 
-    def signs(t, i):
-        a, b = CH[i]
-        for n in range(2):
-            mm(2 * i + n, "ua", "uas", 128 * n, "xq%d" % t, "xs%d" % t, a, b, ["ua", "uas", ("xq%d" % t, a, b)])
-        tiny = -(2.0 ** -100)
-        act(T.sa[:, a:b], T["b%d" % (2 * i)][:, 0:b - a], [], ["b%d" % (2 * i), ("sa", a, b)], sign, bias=tiny)
-        act(T.bw[:, a:b], T["b%d" % (2 * i + 1)][:, 0:b - a], [], ["b%d" % (2 * i + 1), ("bw", a, b)], sign, bias=tiny)
+    def parts_of(t):
+        n1 = t + 1
+        xq, xs, xq1, xs1 = "xq%d" % t, "xs%d" % t, "xq%d" % n1, "xs%d" % n1
+        oc, f16, fu, e16, g16, iv0, iv1 = [n + str(t) for n in ("oc", "f16", "fu", "e16", "g16", "iv", "iw")]
+        rep, fs = "rep%d" % n1, "fs%d" % t
+        c0, c1 = 22 * t, 22 * n1
+        if t >= 0:
+            fu_, e_, g_ = T.fua[:, 12 * t:12 * t + 11], T.e16a[:, c0:c0 + 22], T.g16a[:, c0:c0 + 22]
+            p_, f_, c_ = T[oc][:, 0:22], T[f16][:, 0:22], T[oc][:, 22:44]
+            was, wkey = (T["oc%d" % (t - 1)][:, 0:22], "oc%d" % (t - 1)) if t else (T.pp16[:, 0:22], "oc-1")
+            dst = T.cores[rank ^ STEP[t]]
+            hp = helpers(T, topo, core, dst)
+        else:
+            p_, f_ = T.pp16[:, 0:22], T.rf16[:, 0:22]
+        k1 = T.pr16[:, c1:c1 + 22] if t < 2 else None
 
-    def values(t):
-        for p in range(4):
-            unpack(t, p)
+        def unpack(tq, p):
+            mm(4 + p, "eq", "es", 128 * p, "xq%d" % tq, "xs%d" % tq, 0, C, ["eq%d" % p, "xq%d" % tq])
+
+        def values(p):
+            unpack(n1, p)
             act(T.fp[:, C * p:C * p + C], T["b%d" % (4 + p)][:, 0:C], [], ["b%d" % (4 + p), "fp%d" % p])
 
-    def repeat(rep, n, off, key):
-        act(T[rep][:, C * n:C * n + C], T.idm[:, :].indirect(off), [key, "idm"], [(rep, C * n, C * n + C)])
+        def quant(i):
+            a, b = CH[i]
+            buf, keys = ("xt", [("xt%d" % p, a, b) for p in range(4)]) if t >= 0 else ("xin", [("xin", a, b)])
+            quantize(T[xq1][:, a:b], T[xs1][:, a:b], T[buf][:, 4 * a:4 * b], keys, [(xq1, a, b)])
+            if t == 2:
+                return store(i)
+            for n in range(2):
+                mm(2 * i + n, "ua", "uas", 128 * n, xq1, xs1, a, b, ["ua", "uas", (xq1, a, b)])
+            for n, nm in enumerate(("sa", "sb")):
+                act(T[nm][:, a:b], T["b%d" % (2 * i + n)][:, 0:b - a], [], ["b%d" % (2 * i + n), (nm, a, b)], sign, bias=-(2.0 ** -100))
 
-    def compose(t, n):
-        k, a, b, rep = T.pr16[:, 22 * t:22 * t + 22], C * n, C * n + C, "rep%d" % t
-        act(T.pkf[:, a:b], T[rep][:, a:b].indirect(k), ["pr16", (rep, a, b)], [("pkf", a, b)])
+        def store(i):
+            a, b = CH[i]
+            mm(i, "vq", "vs", 0, xq1, xs1, a, b, ["vq", (xq1, a, b)])
+            dma("Y", T.oc[:, 4 * a:4 * b], codes(T[xq1], a, b), [(xq1, a, b)], ["ocout%d" % i])
+            for k in range(4):
+                dma("Y" if k < 2 or i == 0 else "S", T.osc[4 * k:4 * k + 4, a:b], T[xs1][32 * k:32 * k + 4, a:b], [(xq1, a, b)], ["oscout%d%d" % (i, k)])
+            (act if i == 0 else cp)(T.yt[:, a:b], T["b%d" % i][:, 0:b - a], [], ["b%d" % i, ("yt", a, b)])
+            dma("Y" if i == 0 else "S", T.y[:, a:b], T.yt[:, a:b], [("yt", a, b)], ["yout%d" % i])
 
-    def kplus(t, q0):
-        k, o = T.pr16[:, 22 * t:22 * t + 22], T.mra[:, C * t:C * t + C]
-        if q0 == "V":
-            ts(o, T.idm[:, :].indirect(k), 1024.0 + MID, None, [A.add], ["pr16", "idm"], ["mr%d" % t])
-        else:
-            act(o, T.idm[:, :].indirect(k), ["pr16", "idm"], ["mr%d" % t], F.Identity, bias=1024.0 + MID)
+        def pick(q0, out, okey, win, wkey, off, key, a=0, b=22):
+            buf, lo = off
+            (cp if q0 == "V" else act)(T[out[0]][:, out[1] + 16 * a:out[1] + 16 * b], win.indirect(T[buf][:, lo + a:lo + b]), [wkey, key], [(okey, out[1] + 16 * a, out[1] + 16 * b)])
 
-    def scan(out, okey, data, dkey):
-        op("V", lambda q: q.tensor_tensor_scan(out, T.ck[:, :], data, 0.0, A.mult, A.add), ["ck", dkey], [okey])
+        def both(name, *args):
+            parts[name] = lambda: pick("S", *args)
+            parts[name + "v"] = lambda: pick("V", *args)
+            parts[name + "a"] = lambda: pick("V", *args, 0, 12)
+            parts[name + "b"] = lambda: pick("S", *args, 12, 22)
 
-    def held(out, okey, buf, key, lo, add, akey):
-        ts(out, T[buf][:, lo + 15:lo + C:16], down, add, [A.mult, A.add], [key, "wt0"] + akey, [okey])
+        def kplus(q0):
+            o = T.mra[:, C * n1:C * n1 + C]
+            if q0 == "V":
+                ts(o, T.idm[:, :].indirect(k1), W0 + MID, None, [A.add], ["pr16", "idm"], ["mr%d" % n1])
+            else:
+                act(o, T.idm[:, :].indirect(k1), ["pr16", "idm"], ["mr%d" % n1], F.Identity, bias=W0 + MID)
 
-    def lists_scan(n):
-        a, b = C * n, C * n + C
-        scan(T.sp[:, a:b], ("sp", a, b), T.pkf[:, a:b], ("pkf", a, b))
+        def wrap_lists():
+            for a in (0, C):
+                scan(T.sp[:, a:a + C], ("sp", a, a + C), T.pkf[:, a:a + C], ("pkf", a, a + C))
 
-    def lists_held(t, n):
-        a, b = C * n, C * n + C
-        if n == 0:
-            held(T.pka[:, 22 * t:22 * t + 22], "pk16%d" % t, "sp", ("sp", a, b), a, MID, [])
-        held(T.x1[:, 22 * n:22 * n + 22], ("x1", 22 * n, 22 * n + 22), "sp", ("sp", a, b), a, T.wt[:, 3 + 2 * n:4 + 2 * n], ["wt2"])
+        def held_lists():
+            held(T.x1[:, 0:44], ("x1", 0, 44), T.sp[:, 15:2 * C:16], "sp", half_down, "half_down", mid_o, ["mid_o"])
+            held(T.pka[:, c1:c1 + 22], "pk16%d" % n1, T.sp[:, 15:C:16], ("sp", 0, C), down, "down", MID, [])
 
-    def rest(t, n):
-        ba, di = "ba%d" % t, "di%d" % t
-        if n == 0:
-            tt(T.xx[:, :], T.x1[:, 22:44], T.qk[:, 22 * t:22 * t + 22], A.add, [("x1", 22, 44), "qk"], ["xx"])
-        if n == 1:
-            ts(T.nn[:, :], T.xx[:, :], 1.0 / 352, 0.4986, [A.mult, A.subtract], ["xx"], ["nn"])
-        if n == 2:
-            ts(T.nn[:, :], T.nn[:, :], -352.0, None, [A.mult], ["nn"], ["nn"])
-        if n == 3:
-            tt(T.x1[:, 44:66], T.xx[:, :], T.nn[:, :], A.add, ["xx", "nn"], [("x1", 44, 66)])
-        if n == 4:
-            tt(T[di][:, :], T.x1[:, :], T[ba][:, :], A.subtract, ["x1", ba], [di])
+        def choose(n):
+            a = 66 * n
+            op("V", lambda q: q.tensor_tensor_scan(T.sz[:, a:a + 66], T.sE[:, 13:3 * C:16], T.dz[:, a:a + 66], 0.0, A.mult, A.add),
+               ["sE", "sE0", "sE1", "dz0", "D", "M"], [("sz", a, a + 66)])
 
-    cp(T.pp16[:, :], T.ppi[:, :], ["ppi"], ["pp16"])
-    cp(T.pr16[:, :], T.pri[:, :], ["pri"], ["pr16"])
-    repeat("rep0", 0, T.pp16[:, 0:22], "pp16")
-    cp(T.uo[:, :], T.uoi[:, :], ["uoi"], ["uo"])
-    cp(T.rf16[:, :], T.rfi[:, :], ["rfi"], ["rf16"])
-    ts(T.wt[:, 2:6], T.c4[:, :], up, None, [A.add], ["c4", "wt1"], ["wt2"])
-    op("V", lambda q: q.quantize_mx(T.uq[:, :], T.us[:, :], T.ut[:, :]), ["ut"], ["uq"])
-    kplus(0, "V")
-    compose(0, 0)
-    cp(T.ua[:, 0:256].bitcast(dt.uint32), T.uq[:, 0:128].bitcast(dt.uint32).indirect(T.uo[:, 0:16]), ["uq", "uo"], ["ua"])
-    act(T.uas[:, 0:256], T.us[:, 0:128].indirect(T.uo[:, 0:16]), ["uq", "uo"], ["uas"])
-    quant(0, 0, "xin", ["xin0"])
-    quant(0, 1, "xin", ["xin1"])
-    repeat("rep0", 1, T.rf16[:, 0:22], "rf16")
-    lists_scan(0)
-    signs(0, 0)
-    signs(0, 1)
-    compose(0, 1)
-    for p in range(4):
-        op("V", lambda q: q.quantize_mx(T.eq[:, 128 * p:128 * p + 128], T.es[:, 128 * p:128 * p + 128], T.et[:, 3 - p:515 - p]), ["et"], ["eq%d" % p])
-        if p == 0:
-            lists_held(0, 0)
-    act(T.ch[:, :], T.pat[:, 80:96].indirect(T.mo[:, 0:22]), ["pat5", "mo"], ["ch"])
-    values(0)
-    tt(T.qk[:, :], T.q16[:, :], T.pri[:, :], A.subtract, ["q16", "pri"], ["qk"])
-    ts(T.ba0[:, 0:22], T.ppi[:, :], up, None, [A.add], ["ppi", "wt1"], [("ba0", 0, 22)])
-    ts(T.ba0[:, 22:44], T.rfi[:, :], T.wt[:, 4:5], None, [A.add], ["rfi", "wt2"], [("ba0", 22, 44)])
-    ts(T.qk[:, :], T.qk[:, :], T.wt[:, 6:7], None, [A.add], ["qk", "wt6"], ["qk"])
-    cp(T.ba0[:, 44:66], T.rfi[:, :], ["rfi"], [("ba0", 44, 66)])
+        def mixed_base():
+            choose(2)
+            act(T.gb[:, :], T.sb[:, :].indirect(p_), ["sb", oc], ["gb"], scale=UP)
+            for p in range(4):
+                act(T.gp[:, C * p:C * p + C], T.fp[:, C * p:C * p + C].indirect(p_), ["fp%d" % p, oc], ["gp%d" % p], scale=0.5)
 
-    p16, p16key = T.pp16[:, 0:22], "pp16"
-    for t in range(3):
-        fu_, e_, g_ = T.fua[:, 12 * t:12 * t + 11], T.e16a[:, 22 * t:22 * t + 22], T.g16a[:, 22 * t:22 * t + 22]
-        ba, di, oc, f16, fu, e16, g16 = [n + str(t) for n in ("ba", "di", "oc", "f16", "fu", "e16", "g16")]
-        nb, rep = "ba%d" % (t + 1), "rep%d" % (t + 1)
-        dst = T.cores[rank ^ STEP[t]]
-        hp = helpers(T, topo, core, dst)
+        def offsets():
+            ts(T[oc][:, :], T.sz[:, 2:132:3], o_, None, [A.subtract], [("sz", 0, 132), "o"], [oc])
+            mixed_base()
+
+        def list_out():
+            cp(f_, T.fi[:, :], ["fi"], [f16])
+            if hp:
+                sends([f16], bits(topo, core, hp[0])[1], lambda: send_two(g, T, topo, core, [(c, T.hl[:, a:b], T[f16][:, a:b], "hla") for c, (a, b) in zip(hp, CUT)]))
+            else:
+                sends([f16], bits(topo, core, dst)[1], lambda: send(g, T, topo, core, dst, T[fs][:, 0:22], f_, "la%d" % t))
 
         def half_copy(q0, p, a, b):
             a, b = C * p + a, C * p + b
@@ -361,145 +389,143 @@ def rank_program(g, core, T, topo):
             tt(T[buf][:, p:4 * H:4], T.gp[:, C * p:C * p + C].indirect(off), T.g2[:, a:b], A.add, ["gp%d" % p, ("g2", a, b), okey], ["%s_%d" % (buf, p)])
 
         def zquant(buf, nm):
-            zq, zs = "%sq%d" % (nm, t), "%ss%d" % (nm, t)
-            op("V", lambda q: q.quantize_mx(T[zq][:, :], T[zs][:, :], T[buf][:, :]), ["%s_%d" % (buf, p) for p in range(4)], [zq])
+            quantize(T["%sq%d" % (nm, t)][:, :], T["%ss%d" % (nm, t)][:, :], T[buf][:, :], ["%s_%d" % (buf, p) for p in range(4)], ["%sq%d" % (nm, t)])
+
+        def upper_out():
+            zquant("ztu", "zu")
+            zq, zs, za = "zuq%d" % t, "zus%d" % t, "za%d" % t
+            if hp:
+                k = bits(topo, core, hp[0])[1]
+                sends([zq], k, lambda: send(g, T, topo, core, hp[0], codes(T.hq, 0, HQ), codes(T[zq], 0, HQ), "hca"))
+                sends([zq], k, lambda: send_two(g, T, topo, core, [(hp[1], codes(T.hq, HQ, H), codes(T[zq], HQ, H), "hca"), (hp[1], T.hs[:, 0:H], T[zs][:, 0:H], "hca")]))
+            else:
+                k = bits(topo, core, dst)[1]
+                sends([zq], k, lambda: send(g, T, topo, core, dst, codes(T["zrq%d" % t], 0, H), codes(T[zq], 0, H), za))
+                sends([zq], k, lambda: send(g, T, topo, core, dst, T["zrs%d" % t][:, 0:H], T[zs][:, 0:H], za))
 
         def lower_quant():
             zquant("ztl", "zl")
             for p in range(4):
                 mm(4 + p, "wq", "wsp", 128 * p, "zlq%d" % t, "zls%d" % t, 0, H, ["wq", "wsp", "zlq%d" % t])
 
-        def own_half():
-            for p in range(4):
-                act(T.bp[:, C * p:C * p + H], T["b%d" % (4 + p)][:, 0:H], [], ["b%d" % (4 + p), ("bp%d" % p, 0, H)], scale=0.03125)
+        def scaled(q0, bank, p, a):
+            o, i_, wr = T.bp[:, C * p + a:C * p + a + H], T["b%d" % bank][:, 0:H], ["b%d" % bank, ("bp%d" % p, a, a + H)]
+            if q0 == "S":
+                act(o, i_, [], wr, scale=0.03125)
+            else:
+                ts(o, i_, 0.03125, None, [A.mult], [], wr)
+
+        def their_half(q0, p):
+            mm(p, "wq", "wsp", 128 * p, "zrq%d" % t, "zrs%d" % t, 0, H, ["wq", "wsp", "zr%d" % t])
+            scaled(q0, p, p, H)
 
         def to_columns(src, key):
-            cp(T.ew[:, :].indirect(T[oc][:, 0:22]), src, [key, oc], ["ew"])
+            cp(T.ew[:, :].indirect(p_), src, [key, oc], ["ew"])
 
         def places_out():
-            for n, (off, key) in enumerate(((T[oc][:, 0:22], oc), (T[f16][:, 0:22], f16))):
+            for n, (off, key) in enumerate(((p_, oc), (f_, f16))):
                 act(T.pfo[:, C * n:C * n + C], T.idm[:, :].indirect(off), [key, "idm"], [("pfo", C * n, C * n + C)], F.Identity, bias=MID)
             dma("Y", T.pf[:, :], T.pfo[0:128:16, :], ["pfo"], ["pf"])
 
+        def new_x(how, p, i):
+            a, b = CH[i]
+            o, e = T.xt[:, 4 * a + p:4 * b:4], T.e16a[:, c0 + a // 16:c0 + b // 16]
+            if how == "s":
+                act(T.bg[:, C * p + a:C * p + b], T.bp[:, C * p:C * p + C].indirect(e), ["bp%d" % p, e16], [("bg%d" % p, a, b)])
+            elif how == "a":
+                tt(o, T["b%d" % (4 + p)][:, a:b], T.bg[:, C * p + a:C * p + b], A.add, [("bg%d" % p, a, b)], ["b%d" % (4 + p), ("xt%d" % p, a, b)])
+            else:
+                tt(o, T.bp[:, C * p:C * p + C].indirect(e), T.fp[:, C * p + a:C * p + b], A.add, ["bp%d" % p, e16, "fp%d" % p], [("xt%d" % p, a, b)])
+
+        def differences():
+            tt(T.qk[:, :], T.q16[:, :], T.pri[:, :], A.subtract, ["q16", "pri"], ["qk"])
+            ts(T.qk[:, :], T.qk[:, :], T.wt[:, 10:11], 0.5, [A.add, A.mult], ["qk", "wt10"], ["qk"])
+
         parts = {
-            "K": lambda: kplus(t + 1, "S"),
-            "R": (lambda: repeat(rep, 0, T[oc][:, 0:22], oc)) if t < 2 else places_out, "Q": lambda: repeat(rep, 1, T[f16][:, 0:22], f16),
-            "P": lambda: compose(t + 1, 0), "p": lambda: lists_scan(0), "p16": lambda: lists_held(t + 1, 0),
-            "F": lambda: compose(t + 1, 1), "f": lambda: lists_scan(1), "f16": lambda: lists_held(t + 1, 1),
-            "b": lambda: ts(T[nb][:, 22:44], T[nb][:, 44:66], T.wt[:, 4:5], None, [A.add], [(nb, 44, 66), "wt2"], [(nb, 22, 44)]),
-            "r0": lambda: rest(t + 1, 0), "r1": lambda: rest(t + 1, 1),
-            "lq": lower_quant, "O": own_half,
-            "T": lambda: act(T.fsr[:, :], T.idm[:, :].indirect(T["fs%d" % t][:, 0:22]), ["fs%d" % t, "idm"], ["fsr"]),
-            "H": lambda: act(T.hr[:, :], T.fsr[:, :].indirect(T[f16][:, 0:22]), ["fsr", f16], ["hr"]),
-            "h": lambda: to_columns(T.hr[:, :], "hr"), "wh": lambda: scan(T.esc[:, :], "esc", T.ew[:, :], "ew"),
-            "g": lambda: to_columns(T[rep][:, C:2 * C], (rep, C, 2 * C)), "wg": lambda: scan(T.gsc[:, :], "gsc", T.ew[:, :], "ew"),
-            "g16": lambda: held(g_, g16, "gsc", "gsc", 0, MID, []),
-            "E": lambda: act(T.hr[:, :], T.fsr[:, :].indirect(g_), ["fsr", g16], ["hr"]),
-            "we": lambda: scan(T.esc[:, :], "esc", T.hr[:, :], "hr"), "e16": lambda: held(e_, e16, "esc", "esc", 0, MID, []),
-            "v": lambda: op("V", lambda q: q.quantize_mx(T.vq[:, :], T.vs[:, :], T.vt[:, :]), ["vt"], ["vq"]),
+            "p16": lambda: cp(T.pp16[:, :], T.ppi[:, :], ["ppi"], [oc]), "k16": lambda: cp(T.pr16[:, :], T.pri[:, :], ["pri"], ["pr16"]),
+            "uo": lambda: cp(T.uo[:, :], T.uoi[:, :], ["uoi"], ["uo"]), "uq": lambda: quantize(T.uq[:, :], T.us[:, :], T.ut[:, :], ["ut"], ["uq"]),
+            "ua": lambda: cp(T.ua[:, 0:256].bitcast(dt.uint32), T.uq[:, 0:128].bitcast(dt.uint32).indirect(T.uo[:, 0:16]), ["uq", "uo"], ["ua"]),
+            "us": lambda: act(T.uas[:, 0:256], T.us[:, 0:128].indirect(T.uo[:, 0:16]), ["uq", "uo"], ["uas"]),
+            "usv": lambda: cp(T.uas[:, 0:256], T.us[:, 0:128].indirect(T.uo[:, 0:16]), ["uq", "uo"], ["uas"]),
+            "ch": lambda: act(T.ch[:, :], T.pat[:, 80:96].indirect(T.mo[:, 0:22]), ["pat5", "mo"], ["ch"]), "qk": differences,
+            "am": lambda: tt(T.am[:, :], T.sa[:, :].indirect(was), T.mra[:, C * t:C * t + C], A.mult, ["sa", wkey, "mr%d" % t], ["am"]),
+            "bw": lambda: tt(T.bw[:, :], T.sa[:, :].indirect(T.pka[:, c0:c0 + 22]), T.am[:, :], A.mult, ["sa", "pk16%d" % t, "am"], ["bw"]),
+            "sE": lambda: scan(T.sE[:, 0:3 * C:3], "sE", T.bw[:, :], "bw"),
+            "D": lambda: tt(T.dz[:, 0:198:3], T.x1[:, :], T.ba[:, :], A.subtract, ["x1", "ba"], ["D"]),
+            "M": lambda: tt(T.dz[:, 2:198:3], T.x1[:, :], T.ba[:, :], A.add, ["x1", "ba"], ["M"]),
+            "S": lambda: [choose(0), choose(1)], "oc": offsets,
+            "gm": lambda: cp(T.gm[:, :], T.bw[:, :].indirect(c_), ["bw", oc], ["gm"]),
+            "gs": lambda: scan(T.gs[:, :], "gs", T.gm[:, :], "gm", "ch", (A.add, A.max)), "gsb": lambda: scan(T.gsb[:, :], "gsb", T.gb[:, :], "gb"),
+            "t1": lambda: tt(T.tt[:, 0:22], T.gs[:, 15:C:16], T.sz[:, 68:132:3], A.max, ["gs", ("sz", 66, 132)], ["t1"]),
+            "t2": lambda: tt(T.tt[:, 22:44], T.gsb[:, 15:C:16], T.tt[:, 0:22], A.min, ["gsb", "t1"], ["t2"]),
+            "t3": lambda: tt(T.t3[:, :], T.tt[:, 22:44], T.sz[:, 134:198:3], A.max, ["t2", ("sz", 132, 198)], ["t3"]),
+            "and": lambda: ts(T.fi[:, :], T.t3[:, :], 511, None, [A.bitwise_and], ["t3"], ["fi"]),
+            "f16": list_out if t >= 0 else lambda: cp(T.rf16[:, :], T.rfi[:, :], ["rfi"], [f16]),
+            "fu": lambda: cp(fu_, T.fi[:, 11:22], ["fi"], [fu]),
+            "zq": upper_out, "lq": lower_quant, "O": lambda: [scaled("S", 4 + p, p, 0) for p in range(4)],
+            "h": lambda: to_columns(T.hr[:, :], "hr"), "g": lambda: to_columns(T[rep][:, C:2 * C], (rep, C, 2 * C)), "i": lambda: to_columns(T.idm[:, :], "idm"),
+            "wh": lambda: scan(T.esc[:, :], "esc", T.ew[:, :], "ew"), "wg": lambda: scan(T.gsc[:, :], "gsc", T.ew[:, :], "ew"),
+            "wc": lambda: scan(T.gsc[:, :], "gsc", T.h2[:, :], "h2"),
+            "we": lambda: scan(T.esc[:, :], "esc", T.hr[:, :], "hr"), "wd": lambda: scan(T.esc[:, :], "esc", T.h2[:, :], "h2"),
+            "g16": lambda: held(g_, g16, T.gsc[:, 15:C:16], "gsc", down, "down", MID, []),
+            "e16": lambda: held(e_, e16, T.esc[:, 15:C:16], "esc", down, "down", MID, []),
+            "i16": lambda: held(T.iv[:, c0:c0 + 22], iv0, T.gsc[:, 15:C:16], "gsc", down, "down", MID, []),
+            "io": lambda: ts(T.tt[:, 44:66], T.iv[:, c0:c0 + 22], o_, None, [A.add], [iv0, "o"], ["ivo"]),
+            "wj": lambda: scan(T.wj[:, :], "wj", T.wi[:, :], "wi", "ch", (A.add, A.max)),
+            "j1": lambda: tt(T.ji[:, 0:22], T.wj[:, 15:C:16], T.tt[:, 44:66], A.max, ["wj", "ivo"], ["j1"]),
+            "j2": lambda: ts(T.ji[:, 22:44], T.ji[:, 0:22], 511, None, [A.bitwise_and], ["j1"], ["j2"]),
+            "j3": lambda: cp(T.iv[:, c0:c0 + 22], T.ji[:, 22:44], ["j2"], [iv0]),
+            "K": lambda: kplus("S"), "Kv": lambda: kplus("V"), "w": wrap_lists, "h0": held_lists,
+            "w0": lambda: scan(T.sp[:, 0:C], ("sp", 0, C), T.pkf[:, 0:C], ("pkf", 0, C)),
+            "w1": lambda: scan(T.sp[:, C:2 * C], ("sp", C, 2 * C), T.pkf[:, C:2 * C], ("pkf", C, 2 * C)),
+            "hx": lambda: held(T.x1[:, 0:44], ("x1", 0, 44), T.sp[:, 15:2 * C:16], "sp", half_down, "half_down", mid_o, ["mid_o"]),
+            "hp": lambda: held(T.pka[:, c1:c1 + 22], "pk16%d" % n1, T.sp[:, 15:C:16], ("sp", 0, C), down, "down", MID, []),
+            "bp": lambda: held(T.ba[:, 0:22], ("ba", 0, 22), p_, oc, 0.5, "half_o", half_o, []),
+            "bc": lambda: held(T.ba[:, 22:44], ("ba", 22, 44), f_, f16, 0.5, "half_o", half_o, []),
+            "ba": lambda: ts(T.ba[:, 44:66], f_, 0.5, None, [A.mult], [f16], [("ba", 44, 66)]),
+            "v": lambda: quantize(T.vq[:, :], T.vs[:, :], T.vt[:, :], ["vt"], ["vq"]),
         }
+        for nm, r in (("r", n1), ("n", t)):
+            parts[nm + "0"] = lambda r=r: tt(T.xx[:, :], T.x1[:, 22:44], T.qk[:, 22 * r:22 * r + 22], A.add, [("x1", 22, 44), "qk"], ["xx"])
+        parts["r1"] = lambda: ts(T.nn[:, :], T.xx[:, :], 1.0 / MID, 0.4986, [A.mult, A.subtract], ["xx"], ["nn"])
+        parts["r2"] = lambda: ts(T.nn[:, :], T.nn[:, :], -176.0, None, [A.mult], ["nn"], ["nn"])
+        parts["r3"] = lambda: tt(T.x1[:, 44:66], T.xx[:, :], T.nn[:, :], A.add, ["xx", "nn"], [("x1", 44, 66)])
+        pb, fb = ((oc, 0), (f16, 0)) if t >= 0 else (("pp16", 0), ("rf16", 0))
+        both("R", (rep, 0), rep, T.idm[:, :], "idm", pb, oc)
+        both("Q", (rep, C), rep, T.idm[:, :], "idm", fb, f16)
+        both("P", ("pkf", 0), "pkf", T[rep][:, 0:C], (rep, 0, C), ("pr16", c1), "pr16")
+        both("F", ("pkf", C), "pkf", T[rep][:, C:2 * C], (rep, C, 2 * C), ("pr16", c1), "pr16")
+        if t == 2:
+            parts["R"] = places_out
+        if t >= 0:
+            both("T", ("fsr", 0), "fsr", T.idm[:, :], "idm", (fs, 0), fs)
+            both("H", ("hr", 0), "hr", T.fsr[:, :], "fsr", fb, f16)
+            both("E", ("hr", 0), "hr", T.fsr[:, :], "fsr", ("g16a", c0), g16)
+            both("Y", ("h2", 0), "h2", T.hr[:, :], "hr", ("iv", c0), iv0)
+            both("C", ("h2", 0), "h2", T[rep][:, C:2 * C], (rep, C, 2 * C), ("iv", c0), iv0)
+            both("W", ("wi", 0), "wi", T.bw[:, :], "bw", ("iv", c0 - 22), "iv%d" % (t - 1))
         for p in range(4):
+            parts["e%d" % p] = lambda p=p: quantize(T.eq[:, 128 * p:128 * p + 128], T.es[:, 128 * p:128 * p + 128], T.et[:, 3 - p:515 - p], ["et"], ["eq%d" % p])
+            parts["F%d" % p] = lambda p=p: values(p)
+            parts["U%d" % p] = lambda p=p: unpack(t, p)
             parts["c%d" % p] = lambda p=p: half_copy("V", p, 0, C)
             parts["u%d" % p] = lambda p=p: half_copy("V", p, H, C)
             parts["m%d" % p] = lambda p=p: half_copy("V", p, 0, H)
             parts["L%d" % p] = lambda p=p: half_copy("S", p, 0, H)
+            parts["z%d" % p] = lambda p=p: mix("ztu", fu_, fu, H, p)
             parts["l%d" % p] = lambda p=p: mix("ztl", T[f16][:, 0:11], f16, 0, p)
+            parts["B%d" % p] = lambda p=p: their_half("S", p)
+            parts["V%d" % p] = lambda p=p: their_half("V", p)
+            parts["O%d" % p] = lambda p=p: scaled("S", 4 + p, p, 0)
+            parts["o%d" % p] = lambda p=p: scaled("V", 4 + p, p, 0)
+            for i in range(2):
+                parts["q%d" % i] = lambda i=i: quant(i)
+                for how in "sax":
+                    parts["%s%d%d" % (how, p, i)] = lambda how=how, p=p, i=i: new_x(how, p, i)
+        return parts
 
-        def run(names):
-            for n in names.split():
-                parts[n]()
-
-        tt(T.am[:, :], T.sa[:, :].indirect(p16), T.mra[:, C * t:C * t + C], A.mult, ["sa", p16key, "mr%d" % t], ["am"])
-        if t == 0:
-            lists_scan(1)
-        else:
-            rest(t, 2)
-        tt(T.bw[:, 512:864], T.sa[:, :].indirect(T.pka[:, 22 * t:22 * t + 22]), T.am[:, :], A.mult, ["sa", "pk16%d" % t, "am"], [("bw", 512, 864)])
-        if t == 0:
-            lists_held(0, 1)
-        else:
-            rest(t, 3)
-        scan(T.sE[:, :], "sE", T.bw[:, 512:864], ("bw", 512, 864))
-        for n in range(5) if t == 0 else (4,):
-            rest(t, n)
-        run(SEQ[t]["idle"])
-        ts(T.e3[:, :], T.sE[:, 15:C:16], 0.0, None, [A.is_gt], ["sE"], ["e3"])
-        for n in range(3):
-            a, b = 22 * n, 22 * n + 22
-            tt(T.sm[:, a:b], T.e3[:, :], T[di][:, a:b], A.mult, ["e3", di], [("sm", a, b)])
-        tt(T[nb][:, 0:44], T.sm[:, 0:44], T[ba][:, 0:44], A.add, [("sm", 0, 44), ba], [(nb, 0, 44)])
-        tt(T.tt[:, 44:66], T.sm[:, 44:66], T[ba][:, 44:66], A.add, [("sm", 44, 66), ba], ["alt"])
-        ts(T[oc][:, :], T[nb][:, 0:44], up, None, [A.subtract], [(nb, 0, 44), "wt1"], [oc])
-        act(T.gb[:, :], T.bw[:, 0:C].indirect(T[oc][:, 0:22]), [("bw", 0, C), oc], ["gb"], scale=UP)
-        for p in range(4):
-            act(T.gp[:, C * p:C * p + C], T.fp[:, C * p:C * p + C].indirect(T[oc][:, 0:22]), ["fp%d" % p, oc], ["gp%d" % p], scale=0.5)
-        cp(T.gm[:, :], T.bw[:, :].indirect(T[oc][:, 22:44]), ["bw", oc], ["gm"])
-        op("V", lambda q: q.tensor_tensor_scan(T.gs[:, :], T.ch[:, :], T.gm[:, :], 0.0, A.add, A.max), ["ch", "gm"], ["gs"])
-        scan(T.gsb[:, :], "gsb", T.gb[:, :], "gb")
-        run(GAPS[0])
-        tt(T.tt[:, 0:22], T.gs[:, 15:C:16], T[nb][:, 22:44], A.max, ["gs", (nb, 22, 44)], ["t1"])
-        run(GAPS[1])
-        tt(T.tt[:, 22:44], T.gsb[:, 15:C:16], T.tt[:, 0:22], A.min, ["gsb", "t1"], ["t2"])
-        run(GAPS[2])
-        tt(T.t3[:, :], T.tt[:, 22:44], T.tt[:, 44:66], A.max, ["t2", "alt"], ["t3"])
-        run(GAPS[3])
-        ts(T[nb][:, 44:66], T.t3[:, :], 511, None, [A.bitwise_and], ["t3"], [(nb, 44, 66)])
-        run(GAPS[4])
-        cp(T[f16][:, :], T[nb][:, 44:66], [(nb, 44, 66)], [f16])
-        cp(fu_, T[nb][:, 55:66], [(nb, 44, 66)], [fu])
-        if hp:
-            halves = []
-            for n, (c, (a, b)) in enumerate(zip((hp[0], hp[-1]), CUT)):
-                rid, pid = topo.addr(c, core)
-                halves.append(RemoteDMATransfer(dst_ids=[DstId(rid=rid, pnc=pid)], dma_engine_mask=bits(topo, core, c, 8, 8 * n)[0],
-                                                remote_sem=T.sem.hla, src=T[f16][:, a:b], dst=T.hl[:, a:b]))
-            sends([f16], 16, lambda: g.remote_dma_fused(halves, local_sem=T.sem.rl))
-        else:
-            sends([f16], bits(topo, core, dst)[1], lambda: send(g, T, topo, core, dst, T["fs%d" % t][:, 0:22], T[f16][:, 0:22], "la%d" % t))
-        for p in range(4):
-            run(GAPS[5 + p])
-            mix("ztu", fu_, fu, H, p)
-        zquant("ztu", "zu")
-        zq, zs = "zuq%d" % t, "zus%d" % t
-        if not hp:
-            k = bits(topo, core, dst)[1]
-            sends([zq], k, lambda: send(g, T, topo, core, dst, T["zrq%d" % t][:, 0:H].bitcast(dt.uint8), T[zq][:, 0:H].bitcast(dt.uint8), "za%d" % t))
-            sends([zq], k, lambda: send(g, T, topo, core, dst, T["zrs%d" % t][:, 0:H], T[zs][:, 0:H], "za%d" % t))
-        else:
-            sends([zq], bits(topo, core, hp[0])[1], lambda: send(g, T, topo, core, hp[0], T.hq[:, 0:H].bitcast(dt.uint8), T[zq][:, 0:H].bitcast(dt.uint8), "hca"))
-            sends([zq], bits(topo, core, hp[-1])[1], lambda: send(g, T, topo, core, hp[-1], T.hs[:, 0:H], T[zs][:, 0:H], "hsa"))
-        run(SEQ[t]["z"])
-        for p in range(4 - XS[t], 4):
-            unpack(t, p)
-        for p in range(4):
-            mm(p, "wq", "wsp", 128 * p, "zrq%d" % t, "zrs%d" % t, 0, H, ["wq", "wsp", "zr%d" % t])
-            act(T.bp[:, C * p + H:C * p + C], T["b%d" % p][:, 0:H], [], ["b%d" % p, ("bp%d" % p, H, C)], scale=0.03125)
-        for i, (a, b) in enumerate(CH):
-            e = T.e16a[:, 22 * t + a // 16:22 * t + b // 16]
-            for p in range(4 - XS[t], 4):
-                act(T.bg[:, C * p + a:C * p + b], T.bp[:, C * p:C * p + C].indirect(e), ["bp%d" % p, e16], [("bg%d" % p, a, b)])
-        run(SEQ[t]["x"])
-        for i, (a, b) in enumerate(CH):
-            e = T.e16a[:, 22 * t + a // 16:22 * t + b // 16]
-            for p in range(4):
-                o = T.xt[:, 4 * a + p:4 * b:4]
-                if p >= 4 - XS[t]:
-                    tt(o, T["b%d" % (4 + p)][:, a:b], T.bg[:, C * p + a:C * p + b], A.add, [("bg%d" % p, a, b)], ["b%d" % (4 + p), ("xt%d" % p, a, b)])
-                else:
-                    tt(o, T.bp[:, C * p:C * p + C].indirect(e), T.fp[:, C * p + a:C * p + b], A.add, ["bp%d" % p, e16, "fp%d" % p], [("xt%d" % p, a, b)])
-            quant(t + 1, i, "xt", [("xt%d" % p, a, b) for p in range(4)])
-            if t < 2:
-                signs(t + 1, i)
-                if i == 1:
-                    values(t + 1)
-                run(SEQ[t]["mid" if i == 0 else "end"])
-            else:
-                xq, xs = "xq3", "xs3"
-                mm(i, "vq", "vs", 0, xq, xs, a, b, ["vq", (xq, a, b)])
-                dma("Y", T.oc[:, 4 * a:4 * b], T[xq][:, a:b].bitcast(dt.uint8), [(xq, a, b)], ["ocout%d" % i])
-                for k in range(4):
-                    dma("Y" if k < 2 or i == 0 else "S", T.osc[4 * k:4 * k + 4, a:b], T[xs][32 * k:32 * k + 4, a:b], [(xq, a, b)], ["oscout%d%d" % (i, k)])
-                (act if i == 0 else cp)(T.yt[:, a:b], T["b%d" % i][:, 0:b - a], [], ["b%d" % i, ("yt", a, b)])
-                dma("Y" if i == 0 else "S", T.y[:, a:b], T.yt[:, a:b], [("yt", a, b)], ["yout%d" % i])
-        p16, p16key = T[oc][:, 0:22], oc
+    for t, names in enumerate(ORDER):
+        parts = parts_of(t - 1)
+        for n in names.split():
+            parts[n]()
     finish()

@@ -5,20 +5,21 @@ A, F = AluOpType, ActivationFunctionType
 N, C, H = 8, 352, 176
 STEP = [4, 1, 2]
 CH = [(0, 224), (224, 352)]
+LOW = 160
 CUT = ((0, 11), (11, 22))
 HQ = 132
-BIG = 2.0 ** 20
+BIG = 2.0 ** 40
 W0 = 2.0 ** 18
-UP = 2.0 ** 19
 MID = 176.0
-MIX = " S oc gm gs gsb t1 t2 c0 t3 and c1 f16 fu z0 u2 z1 u3 z2 z3 "
-NEW = " B0 B1 B2 B3 s20 s30 s21 s31 x00 x10 x01 a20 a30 x11 q0 a21 a31 "
-NEXT = " F0 F1 F2 F3"
+HEAD = "f0 Bp Bk f1 f2 f3 "
+LISTS = " wk S0 S1 Db Mb oc G0 G1 G2 G3 S2 S3 gw y0 y1 gk y2 y3 yc ys y u0 f16 u1 "
+UPPER = " z0 u2 z1 u3 z2 z3 "
+NEW = " B0 B1 B2 B3 s20 s30 s21 s31 s11 x0 x10 a20 a30 a21 q0 a31 a11 "
 ORDER = [
-    "p16 R k16 f16 uo Q e0 Kv P ba bc uq qk ua e1 F us w0 q0 w1 q1 hx e2 hp r0 e3 r1 bp r2 ch" + NEXT,
-    "am r3 bw K M D sE" + MIX + "R L2 L3 Q F l0 zq l1 l2 l3 P lq g w1 O wg w0 g16 hx T E r0 ba r1 bc r2 bp r3 U2 U3 we D e16" + NEW + "hp q1 M" + NEXT,
-    "am bw sE K" + MIX + "R L2 L3 Q l0 zq P T Hb l1 l2 l3 bp lq Ha h bc O U2 U3 wh F w0 e16 w1" + NEW + "hx q1 r0 hp r1 ba r2" + NEXT,
-    "am r3 bw M D sE" + MIX + "L2 L3 Q l0 zq R l1 l2 l3 v lq O U2 U3 g wg g16 Ta Tb Ea Eb we e16" + NEW + "q1",
+    "e0 e1 p16 R k16 f16 Q e2 uo e3 uq F us P ba bc qk ua q0 d0 d1 w1 d2 q1 sa0 sa1 sb0 sb1 hf Kv w0 r0 r1 r2 hp hk",
+    HEAD + "am n3 bw wp D M sE" + LISTS + "m0 m1" + UPPER + "m2 m3 zq Q R F l0 l1 l2 l3 lq g K P T O w1 wg bc g16 w0 ba r0 E hx r1 r2 hp r3 we D e16" + NEW + "sa0 sb0 M q1 sa1 Jv sb1",
+    HEAD + "am bw wp sE" + LISTS + "Y0 Y1 Y2 Y3" + UPPER + "ba zq R Q T Hb l0 l1 l2 l3 Ha P lq h F O wh w1 e16 w0" + NEW + "hp sa0 sb0 q1 hx bc r0 r1 r2 sa1 sb1 r3",
+    HEAD + "M am D bw wp sE" + LISTS + "Y0 Y1 Y2 Y3" + UPPER + "v zq R Q l0 l1 l2 l3 lq g O wg Ta Tb g16 Ea Eb we e16" + NEW + "q1",
 ]
 
 SCRATCH = {
@@ -31,43 +32,43 @@ SCRATCH = {
     "one": ("sbuf", [128, 128], "bfloat16"), "et": ("sbuf", [128, 516], "bfloat16"),
     "eq": ("sbuf", [128, 512], "float8_e4m3fn_x4"), "es": ("sbuf", [128, 512], "uint8"),
     "ppi": ("sbuf", [128, 22], "int32"), "rfi": ("sbuf", [128, 22], "int32"), "pri": ("sbuf", [128, 66], "int32"),
-    "pp16": ("sbuf", [128, 22], "uint16"), "rf16": ("sbuf", [128, 22], "uint16"), "pr16": ("sbuf", [128, 66], "uint16"),
-    "idm": ("sbuf", [128, C], "bfloat16"), "ck": ("sbuf", [128, C], "bfloat16"), "ch": ("sbuf", [128, C], "bfloat16"),
+    "pr16": ("sbuf", [128, 66], "uint16"), "idm": ("sbuf", [128, C], "bfloat16"), "ck": ("sbuf", [128, C], "bfloat16"),
     "pm": ("sbuf", [128, 22], "int32"), "mo": ("sbuf", [128, 22], "uint16"), "d16": ("sbuf", [128, 16], "int32"),
-    "pat": ("sbuf", [128, 96], "float32"), "wt": ("sbuf", [128, 16], "float32"),
+    "pat": ("sbuf", [128, 48], "float32"), "wt": ("sbuf", [128, 26], "float32"),
     "uoi": ("sbuf", [128, 16], "int32"), "uo": ("sbuf", [128, 16], "uint16"),
     "q16": ("sbuf", [128, 66], "int32"), "qk": ("sbuf", [128, 66], "float32"),
-    "sa": ("sbuf", [128, C], "bfloat16"), "sb": ("sbuf", [128, C], "bfloat16"), "am": ("sbuf", [128, C], "float32"), "bw": ("sbuf", [128, C], "float32"),
-    "sE": ("sbuf", [128, 3 * C], "float32"), "dz": ("sbuf", [128, 198], "float32"), "sz": ("sbuf", [128, 198], "float32"),
-    "gm": ("sbuf", [128, C], "float32"), "gs": ("sbuf", [128, C], "float32"),
-    "gb": ("sbuf", [128, C], "bfloat16"), "gsb": ("sbuf", [128, C], "bfloat16"),
-    "tt": ("sbuf", [128, 66], "float32"), "t3": ("sbuf", [128, 22], "int32"), "fi": ("sbuf", [128, 22], "int32"),
-    "wi": ("sbuf", [128, C], "float32"), "wj": ("sbuf", [128, C], "float32"), "ji": ("sbuf", [128, 44], "int32"),
-    "iv": ("sbuf", [128, 66], "uint16"),
+    "sa": ("sbuf", [128, C], "bfloat16"), "sb": ("sbuf", [128, C], "bfloat16"), "am": ("sbuf", [128, C], "bfloat16"), "bw": ("sbuf", [128, C], "bfloat16"),
+    "sE": ("sbuf", [128, 3 * C], "bfloat16"), "dz": ("sbuf", [128, 264], "float32"), "sz": ("sbuf", [128, 264], "float32"),
+    "gm": ("sbuf", [128, C], "bfloat16"), "gs": ("sbuf", [128, 2576], "bfloat16"), "kc": ("sbuf", [128, C], "bfloat16"), "gk": ("sbuf", [128, 2576], "bfloat16"),
+    "gb": ("sbuf", [128, 2 * C], "bfloat16"), "gsb": ("sbuf", [128, 2 * C], "bfloat16"),
+    "zf": ("sbuf", [128, 154], "bfloat16"),
     "pkf": ("sbuf", [128, 2 * C], "bfloat16"), "sp": ("sbuf", [128, 2 * C], "bfloat16"),
-    "x1": ("sbuf", [128, 66], "float32"), "ba": ("sbuf", [128, 66], "float32"), "xx": ("sbuf", [128, 22], "float32"), "nn": ("sbuf", [128, 22], "int32"),
-    "fsr": ("sbuf", [128, C], "bfloat16"), "hr": ("sbuf", [128, C], "bfloat16"), "h2": ("sbuf", [128, C], "bfloat16"), "ew": ("sbuf", [128, C], "bfloat16"),
+    "x1": ("sbuf", [128, 264], "float32"), "ba": ("sbuf", [128, 66], "float32"),
+    "r0": ("sbuf", [128, 88], "float32"), "r1": ("sbuf", [128, 264], "float32"), "thr": ("sbuf", [128, 132], "float32"),
+    "fsr": ("sbuf", [128, C], "bfloat16"), "hr": ("sbuf", [128, C], "bfloat16"), "ew": ("sbuf", [128, C], "bfloat16"),
     "esc": ("sbuf", [128, C], "bfloat16"), "gsc": ("sbuf", [128, C], "bfloat16"),
     "fp": ("sbuf", [128, 4 * C], "bfloat16"), "gp": ("sbuf", [128, 4 * C], "bfloat16"), "bp": ("sbuf", [128, 4 * C], "bfloat16"),
     "bg": ("sbuf", [128, 4 * C], "bfloat16"), "g2": ("sbuf", [128, 4 * C], "bfloat16"),
-    "ztu": ("sbuf", [128, 4 * H], "bfloat16"), "ztl": ("sbuf", [128, 4 * H], "bfloat16"),
+    "zt": ("sbuf", [128, 4 * C], "bfloat16"),
     "yt": ("sbuf", [128, C], "float32"), "pfo": ("sbuf", [128, 2 * C], "float32"),
     "pka": ("sbuf", [128, 66], "uint16"), "e16a": ("sbuf", [128, 66], "uint16"), "g16a": ("sbuf", [128, 66], "uint16"),
-    "fua": ("sbuf", [128, 36], "uint16"), "mra": ("sbuf", [128, 3 * C], "float32"),
+    "mra": ("sbuf", [128, 3 * C], "bfloat16"),
     "hq": ("sbuf", [128, H], "float8_e4m3fn_x4"), "hs": ("sbuf", [128, H], "uint8"), "hl": ("sbuf", [128, 22], "uint16"),
 }
+if W0:
+    for k in ("am", "bw", "sE", "mra"):
+        SCRATCH[k] = SCRATCH[k][:2] + ("float32",)
 for k in range(8):
     SCRATCH["b%d" % k] = ("psum", [128, 512], "float32")
 for k in range(4):
     SCRATCH["xq%d" % k] = ("sbuf", [128, C], "float8_e4m3fn_x4")
     SCRATCH["xs%d" % k] = ("sbuf", [128, C], "uint8")
     SCRATCH["rep%d" % k] = ("sbuf", [128, 2 * C], "bfloat16")
+    SCRATCH["cpf%d" % k] = ("sbuf", [128, 66], "uint16")
 for k in range(3):
     for nm in ("zu", "zl", "zr"):
         SCRATCH["%sq%d" % (nm, k)] = ("sbuf", [128, H], "float8_e4m3fn_x4")
         SCRATCH["%ss%d" % (nm, k)] = ("sbuf", [128, H], "uint8")
-    SCRATCH["oc%d" % k] = ("sbuf", [128, 44], "uint16")
-    SCRATCH["f16%d" % k] = ("sbuf", [128, 22], "uint16")
     SCRATCH["fs%d" % k] = ("sbuf", [128, 22], "uint16")
 
 ENG = {"V": "sv", "S": "ss", "P": "st", "G": "sg"}
@@ -249,39 +250,42 @@ def rank_program(g, core, T, topo):
     def scan(out, okey, data, dkey, fac="ck", ops=(A.mult, A.add)):
         op("V", lambda q: q.tensor_tensor_scan(out, T[fac][:, :], data, 0.0, *ops), [fac, dkey], [okey])
 
-    down, half_down, rk, o_, half_o, mid_o, full_o, qo = [T.wt[:, n:n + 1] for n in range(8)]
+    def step(buf, first, n):
+        return buf[:, first + 16 * n:first + 16 * n + 7 * C - 111:112]
+
+    down, half_down, own = T.wt[:, 0:1], T.wt[:, 22:23], T.wt[:, 23:24]
     loose = dict(allow_small_or_imprecise_dtypes=True)
     iota(T.pm[:, :], [[0, 22]], 0, 1, ["pm"])
     iota(T.d16[:, :], [[1, 16]], 128, -1, ["d16"])
-    iota(T.idm[:, :], [[1, C]], -int(MID), 0, ["idm"], **loose)
-    iota(T.uoi[:, :], [[1, 2], [16, 8]], 0, 0, ["uoi"])
     fill(T.one[:, :], 1.0, ["one"])
     fill(T.et[:, :], 0.0, ["et"])
     op("G", lambda q: q.affine_select(T.et[:, 3:515:4], T.one[:, :], [[-1, 128]], A.is_equal, 0.0, 0, 1), ["one"], ["et"])
-    iota(T.q16[:, :], [[0, 3], [16, 22]], 0, 0, ["q16"])
+    iota(T.idm[:, :], [[1, C]], -int(MID), 0, ["idm"], **loose)
+    iota(T.uoi[:, :], [[1, 2], [16, 8]], 0, 0, ["uoi"])
+    iota(T.q16[:, :], [[0, 3], [16, 22]], C, 0, ["q16"])
+    for view, n, v, key in ((T.sE[:, 13:3 * C:48], 22, 0.0, "sE0"), (T.dz[:, 1:264:3], 88, 0.0, "dz0"),
+                            (step(T.gs, 57, 0), 22, 0.0, ("zc", 0, 1)), (step(T.gs, 57, 4), 22, 1.0, ("zc", 4, 5)), (step(T.gs, 57, 6), 22, 1.0, ("zc", 6, 7)),
+                            (step(T.gk, 105, 2), 22, 0.0, ("zc", 7, 8)), (step(T.gk, 105, 6), 22, 0.0, ("zc", 8, 9)),
+                            (T.r0[:, 0:88:4], 22, 0.0, ("rc", 0, 1)), (T.r0[:, 3:88:4], 22, 1.0, ("rc", 1, 2)),
+                            (T.r1[:, 0:264:4], 66, -MID, ("rc", 2, 3)), (T.r1[:, 1:264:4], 66, -MID, ("rc", 3, 4))):
+        act(view, T.one[:, 0:n], ["one"], [key], scale=v)
     ts(T.pm[:, :], T.pm[:, :], 15, None, [A.bitwise_and], ["pm"], ["pm"])
-    fill(T.sE[:, 13:3 * C:48], 0.0, ["sE0"])
     ts(T.d16[:, :], T.d16[:, :], 15, None, [A.bitwise_and], ["d16"], ["d16"])
     cp(T.mo[:, :], T.pm[:, :], ["pm"], ["mo"])
-    ts(T.wt[:, 8:9], T.pm[:, 0:1], 15.0, UP, [A.not_equal, A.mult], ["pm"], ["wt8"])
-    ts(T.wt[:, 9:10], T.pm[:, 0:1], 15.0, 1.0 - 1.0 / BIG, [A.is_equal, A.mult], ["pm"], ["wt9"])
-    ts(T.pat[:, 0:16], T.d16[:, :], 1.0, BIG - 1.0, [A.is_equal, A.mult], ["d16"], ["pat0"])
+    ts(T.wt[:, 0:22], T.pm[:, :], 15.0, 1.0 / BIG, [A.is_equal, A.max], ["pm"], ["down"])
+    ts(T.pat[:, 0:16], T.d16[:, :], 1.0, BIG, [A.is_equal, A.mult], ["d16"], ["pat0"])
     ts(T.pat[:, 16:32], T.d16[:, :], 1.0, None, [A.min], ["d16"], ["pat1"])
-    ts(T.pat[:, 48:64], T.d16[:, :], 1.0, UP, [A.is_equal, A.mult], ["d16"], ["pat3"])
-    ts(T.pat[:, 64:80], T.d16[:, :], 0.0, -8.0 * UP, [A.is_equal, A.mult], ["d16"], ["pat4"])
-    ts(o_, T.wt[:, 8:9], 512.0, None, [A.add], ["wt8"], ["o"])
-    tt(T.pat[:, 32:48], T.pat[:, 0:16], T.pat[:, 16:32], A.add, ["pat0", "pat1"], ["pat2"])
+    for n, v in enumerate((0.0, 0.5 - C, 0.5 - 2 * C)):
+        ts(T.wt[:, 23 + n:24 + n], T.pm[:, 0:1], v, None, [A.add], ["pm"], [("own", n, n + 1)])
+    tt(T.pat[:, 32:48], T.pat[:, 0:16], T.pat[:, 16:32], A.max, ["pat0", "pat1"], ["pat2"])
     act(T.ck[:, :], T.pat[:, 32:48].indirect(T.mo[:, 0:22]), ["pat2", "mo"], ["ck"])
-    ts(down, T.wt[:, 9:10], 1.0 / BIG, None, [A.add], ["wt9"], ["down"])
-    ts(half_down, T.wt[:, 9:10], 1.0 / BIG, 0.5, [A.add, A.mult], ["wt9"], ["half_down"])
-    ts(rk, T.wt[:, 9:10], 1.0 / BIG, 1.0 / (W0 + MID), [A.add, A.mult], ["wt9"], ["rk"])
-    ts(half_o, T.wt[:, 8:9], 512.0, 0.5, [A.add, A.mult], ["wt8"], ["half_o"])
-    ts(mid_o, T.wt[:, 8:9], 512.0 + MID, 0.5, [A.add, A.mult], ["wt8"], ["mid_o"])
-    ts(full_o, T.wt[:, 8:9], 512.0 + MID, None, [A.add], ["wt8"], ["full_o"])
-    ts(T.wt[:, 10:11], T.pm[:, 0:1], o_, 352.0, [A.subtract, A.add], ["pm", "o"], ["wt10"])
-    tt(T.pat[:, 80:96], T.pat[:, 48:64], T.pat[:, 64:80], A.add, ["pat3", "pat4"], ["pat5"])
-    fill(T.dz[:, 1:198:3], 0.0, ["dz0"])
-    ts(T.sE[:, 29:3 * C:48], T.pm[:, :], 0.0, rk, [A.mult, A.add], ["pm", "rk"], ["sE1"])
+    ts(half_down, down, 0.5, None, [A.mult], ["down"], ["half_down"])
+    ts(T.sE[:, 29:3 * C:48], T.wt[:, 0:22], 1.0 / (W0 + MID) if W0 else 1.0, None, [A.mult], ["down"], ["sE1"])
+    cp(step(T.gs, 57, 1), T.wt[:, 0:22], ["down"], [("zc", 1, 2)])
+    if W0:
+        fill(step(T.gs, 57, 2), 1.0, [("zc", 2, 3)])
+    else:
+        cp(step(T.gs, 57, 2), T.wt[:, 0:22], ["down"], [("zc", 2, 3)])
 
     def mm(bank, side, scale, c0, rq, rs, a, b, rd):
         op("P", lambda q: q.matmul_mx(T["b%d" % bank][:, 0:b - a], T[side][:, c0:c0 + 128], T[scale][:, c0:c0 + 128],
@@ -293,24 +297,22 @@ def rank_program(g, core, T, topo):
     def parts_of(t):
         n1 = t + 1
         xq, xs, xq1, xs1 = "xq%d" % t, "xs%d" % t, "xq%d" % n1, "xs%d" % n1
-        oc, f16, fu, e16, g16, iv0, iv1 = [n + str(t) for n in ("oc", "f16", "fu", "e16", "g16", "iv", "iw")]
+        oc, f16, fu, e16, g16 = [n + str(t) for n in ("oc", "f16", "fu", "e16", "g16")]
         rep, fs = "rep%d" % n1, "fs%d" % t
         c0, c1 = 22 * t, 22 * n1
         if t >= 0:
-            fu_, e_, g_ = T.fua[:, 12 * t:12 * t + 11], T.e16a[:, c0:c0 + 22], T.g16a[:, c0:c0 + 22]
-            p_, f_, c_ = T[oc][:, 0:22], T[f16][:, 0:22], T[oc][:, 22:44]
-            was, wkey = (T["oc%d" % (t - 1)][:, 0:22], "oc%d" % (t - 1)) if t else (T.pp16[:, 0:22], "oc-1")
+            e_, g_ = T.e16a[:, c0:c0 + 22], T.g16a[:, c0:c0 + 22]
+            was, wkey = T["cpf%d" % t][:, 22:44], "oc%d" % (t - 1)
             dst = T.cores[rank ^ STEP[t]]
             hp = helpers(T, topo, core, dst)
-        else:
-            p_, f_ = T.pp16[:, 0:22], T.rf16[:, 0:22]
-        k1 = T.pr16[:, c1:c1 + 22] if t < 2 else None
+        cpf = "cpf%d" % n1
+        c_, p_, f_ = T[cpf][:, 0:22], T[cpf][:, 22:44], T[cpf][:, 44:66]
 
         def unpack(tq, p):
             mm(4 + p, "eq", "es", 128 * p, "xq%d" % tq, "xs%d" % tq, 0, C, ["eq%d" % p, "xq%d" % tq])
 
-        def values(p):
-            unpack(n1, p)
+        def values(p, r):
+            unpack(r, p)
             act(T.fp[:, C * p:C * p + C], T["b%d" % (4 + p)][:, 0:C], [], ["b%d" % (4 + p), "fp%d" % p])
 
         def quant(i):
@@ -321,8 +323,10 @@ def rank_program(g, core, T, topo):
                 return store(i)
             for n in range(2):
                 mm(2 * i + n, "ua", "uas", 128 * n, xq1, xs1, a, b, ["ua", "uas", (xq1, a, b)])
-            for n, nm in enumerate(("sa", "sb")):
-                act(T[nm][:, a:b], T["b%d" % (2 * i + n)][:, 0:b - a], [], ["b%d" % (2 * i + n), (nm, a, b)], sign, bias=-(2.0 ** -100))
+
+        def signs(n, i):
+            (a, b), nm = CH[i], ("sa", "sb")[n]
+            act(T[nm][:, a:b], T["b%d" % (2 * i + n)][:, 0:b - a], [], ["b%d" % (2 * i + n), (nm, a, b)], sign, bias=-(2.0 ** -100))
 
         def store(i):
             a, b = CH[i]
@@ -343,40 +347,24 @@ def rank_program(g, core, T, topo):
             parts[name + "a"] = lambda: pick("V", *args, 0, 12)
             parts[name + "b"] = lambda: pick("S", *args, 12, 22)
 
-        def kplus(q0):
-            o = T.mra[:, C * n1:C * n1 + C]
-            if q0 == "V":
-                ts(o, T.idm[:, :].indirect(k1), W0 + MID, None, [A.add], ["pr16", "idm"], ["mr%d" % n1])
+        def kplus(q0, r):
+            o, k = T.mra[:, C * r:C * r + C], T.pr16[:, 22 * r:22 * r + 22]
+            if not W0:
+                (cp if q0 == "V" else act)(o, T.idm[:, :].indirect(k), ["pr16", "idm"], ["mr%d" % r])
+            elif q0 == "V":
+                ts(o, T.idm[:, :].indirect(k), W0 + MID, None, [A.add], ["pr16", "idm"], ["mr%d" % r])
             else:
-                act(o, T.idm[:, :].indirect(k1), ["pr16", "idm"], ["mr%d" % n1], F.Identity, bias=W0 + MID)
-
-        def wrap_lists():
-            for a in (0, C):
-                scan(T.sp[:, a:a + C], ("sp", a, a + C), T.pkf[:, a:a + C], ("pkf", a, a + C))
-
-        def held_lists():
-            held(T.x1[:, 0:44], ("x1", 0, 44), T.sp[:, 15:2 * C:16], "sp", half_down, "half_down", mid_o, ["mid_o"])
-            held(T.pka[:, c1:c1 + 22], "pk16%d" % n1, T.sp[:, 15:C:16], ("sp", 0, C), down, "down", MID, [])
+                act(o, T.idm[:, :].indirect(k), ["pr16", "idm"], ["mr%d" % r], F.Identity, bias=W0 + MID)
 
         def choose(n):
             a = 66 * n
             op("V", lambda q: q.tensor_tensor_scan(T.sz[:, a:a + 66], T.sE[:, 13:3 * C:16], T.dz[:, a:a + 66], 0.0, A.mult, A.add),
-               ["sE", "sE0", "sE1", "dz0", "D", "M"], [("sz", a, a + 66)])
-
-        def mixed_base():
-            choose(2)
-            act(T.gb[:, :], T.sb[:, :].indirect(p_), ["sb", oc], ["gb"], scale=UP)
-            for p in range(4):
-                act(T.gp[:, C * p:C * p + C], T.fp[:, C * p:C * p + C].indirect(p_), ["fp%d" % p, oc], ["gp%d" % p], scale=0.5)
-
-        def offsets():
-            ts(T[oc][:, :], T.sz[:, 2:132:3], o_, None, [A.subtract], [("sz", 0, 132), "o"], [oc])
-            mixed_base()
+               ["sE", "sE0", "sE1", "dz0", ("D", n, n + 1), ("M", n, n + 1)], [("sz", a, a + 66)])
 
         def list_out():
-            cp(f_, T.fi[:, :], ["fi"], [f16])
+            ts(f_, T.zf[:, 5:154:7], MID, None, [A.add], ["zf"], [f16])
             if hp:
-                sends([f16], bits(topo, core, hp[0])[1], lambda: send_two(g, T, topo, core, [(c, T.hl[:, a:b], T[f16][:, a:b], "hla") for c, (a, b) in zip(hp, CUT)]))
+                sends([f16], bits(topo, core, hp[0])[1], lambda: send_two(g, T, topo, core, [(c, T.hl[:, a:b], T[cpf][:, 44 + a:44 + b], "hla") for c, (a, b) in zip(hp, CUT)]))
             else:
                 sends([f16], bits(topo, core, dst)[1], lambda: send(g, T, topo, core, dst, T[fs][:, 0:22], f_, "la%d" % t))
 
@@ -384,15 +372,16 @@ def rank_program(g, core, T, topo):
             a, b = C * p + a, C * p + b
             (cp if q0 == "V" else act)(T.g2[:, a:b], T.gp[:, a:b], ["gp%d" % p], [("g2", a, b)])
 
-        def mix(buf, off, okey, o, p):
-            a, b = C * p + o, C * p + o + H
-            tt(T[buf][:, p:4 * H:4], T.gp[:, C * p:C * p + C].indirect(off), T.g2[:, a:b], A.add, ["gp%d" % p, ("g2", a, b), okey], ["%s_%d" % (buf, p)])
+        def mix(p, a, b):
+            o = C * p
+            tt(T.zt[:, 4 * a + p:4 * b:4], T.gp[:, o:o + C].indirect(T[cpf][:, 44 + a // 16:44 + b // 16]), T.g2[:, o + a:o + b], A.add,
+               ["gp%d" % p, ("g2", o + a, o + b), f16], [("zt%d" % p, a, b)])
 
-        def zquant(buf, nm):
-            quantize(T["%sq%d" % (nm, t)][:, :], T["%ss%d" % (nm, t)][:, :], T[buf][:, :], ["%s_%d" % (buf, p) for p in range(4)], ["%sq%d" % (nm, t)])
+        def zquant(a, nm):
+            quantize(T["%sq%d" % (nm, t)][:, :], T["%ss%d" % (nm, t)][:, :], T.zt[:, 4 * a:4 * (a + H)], [("zt%d" % p, a, a + H) for p in range(4)], ["%sq%d" % (nm, t)])
 
         def upper_out():
-            zquant("ztu", "zu")
+            zquant(H, "zu")
             zq, zs, za = "zuq%d" % t, "zus%d" % t, "za%d" % t
             if hp:
                 k = bits(topo, core, hp[0])[1]
@@ -404,9 +393,9 @@ def rank_program(g, core, T, topo):
                 sends([zq], k, lambda: send(g, T, topo, core, dst, T["zrs%d" % t][:, 0:H], T[zs][:, 0:H], za))
 
         def lower_quant():
-            zquant("ztl", "zl")
+            zquant(0, "zl")
             for p in range(4):
-                mm(4 + p, "wq", "wsp", 128 * p, "zlq%d" % t, "zls%d" % t, 0, H, ["wq", "wsp", "zlq%d" % t])
+                mm(p, "wq", "wsp", 128 * p, "zlq%d" % t, "zls%d" % t, 0, H, ["wq", "wsp", "zlq%d" % t])
 
         def scaled(q0, bank, p, a):
             o, i_, wr = T.bp[:, C * p + a:C * p + a + H], T["b%d" % bank][:, 0:H], ["b%d" % bank, ("bp%d" % p, a, a + H)]
@@ -428,7 +417,7 @@ def rank_program(g, core, T, topo):
             dma("Y", T.pf[:, :], T.pfo[0:128:16, :], ["pfo"], ["pf"])
 
         def new_x(how, p, i):
-            a, b = CH[i]
+            a, b = (0, C) if i is None else CH[i]
             o, e = T.xt[:, 4 * a + p:4 * b:4], T.e16a[:, c0 + a // 16:c0 + b // 16]
             if how == "s":
                 act(T.bg[:, C * p + a:C * p + b], T.bp[:, C * p:C * p + C].indirect(e), ["bp%d" % p, e16], [("bg%d" % p, a, b)])
@@ -438,88 +427,116 @@ def rank_program(g, core, T, topo):
                 tt(o, T.bp[:, C * p:C * p + C].indirect(e), T.fp[:, C * p + a:C * p + b], A.add, ["bp%d" % p, e16, "fp%d" % p], [("xt%d" % p, a, b)])
 
         def differences():
-            tt(T.qk[:, :], T.q16[:, :], T.pri[:, :], A.subtract, ["q16", "pri"], ["qk"])
-            ts(T.qk[:, :], T.qk[:, :], T.wt[:, 10:11], 0.5, [A.add, A.mult], ["qk", "wt10"], ["qk"])
+            tt(T.qk[:, :], T.q16[:, :], T.pri[:, :], A.subtract, ["q16", "pri"], ["qk0"])
+
+        def bounds(n):
+            if n == 0:
+                ts(T.r1[:, 3:264:4], T.qk[:, :], own, 0.5, [A.add, A.mult], ["qk0", "own"], ["qk"])
+            else:
+                ts(T.thr[:, 66 * n - 66:66 * n], T.qk[:, :], T.wt[:, 23 + n:24 + n], -0.5, [A.add, A.mult], ["qk0", "own"], [("thr", n, n + 1)])
 
         parts = {
-            "p16": lambda: cp(T.pp16[:, :], T.ppi[:, :], ["ppi"], [oc]), "k16": lambda: cp(T.pr16[:, :], T.pri[:, :], ["pri"], ["pr16"]),
+            "p16": lambda: cp(p_, T.ppi[:, :], ["ppi"], [oc]), "k16": lambda: cp(T.pr16[:, :], T.pri[:, :], ["pri"], ["pr16"]),
             "uo": lambda: cp(T.uo[:, :], T.uoi[:, :], ["uoi"], ["uo"]), "uq": lambda: quantize(T.uq[:, :], T.us[:, :], T.ut[:, :], ["ut"], ["uq"]),
             "ua": lambda: cp(T.ua[:, 0:256].bitcast(dt.uint32), T.uq[:, 0:128].bitcast(dt.uint32).indirect(T.uo[:, 0:16]), ["uq", "uo"], ["ua"]),
             "us": lambda: act(T.uas[:, 0:256], T.us[:, 0:128].indirect(T.uo[:, 0:16]), ["uq", "uo"], ["uas"]),
             "usv": lambda: cp(T.uas[:, 0:256], T.us[:, 0:128].indirect(T.uo[:, 0:16]), ["uq", "uo"], ["uas"]),
-            "ch": lambda: act(T.ch[:, :], T.pat[:, 80:96].indirect(T.mo[:, 0:22]), ["pat5", "mo"], ["ch"]), "qk": differences,
-            "am": lambda: tt(T.am[:, :], T.sa[:, :].indirect(was), T.mra[:, C * t:C * t + C], A.mult, ["sa", wkey, "mr%d" % t], ["am"]),
+            "qk": differences, "d0": lambda: bounds(0), "d1": lambda: bounds(1), "d2": lambda: bounds(2),
             "bw": lambda: tt(T.bw[:, :], T.sa[:, :].indirect(T.pka[:, c0:c0 + 22]), T.am[:, :], A.mult, ["sa", "pk16%d" % t, "am"], ["bw"]),
             "sE": lambda: scan(T.sE[:, 0:3 * C:3], "sE", T.bw[:, :], "bw"),
-            "D": lambda: tt(T.dz[:, 0:198:3], T.x1[:, :], T.ba[:, :], A.subtract, ["x1", "ba"], ["D"]),
-            "M": lambda: tt(T.dz[:, 2:198:3], T.x1[:, :], T.ba[:, :], A.add, ["x1", "ba"], ["M"]),
-            "S": lambda: [choose(0), choose(1)], "oc": offsets,
-            "gm": lambda: cp(T.gm[:, :], T.bw[:, :].indirect(c_), ["bw", oc], ["gm"]),
-            "gs": lambda: scan(T.gs[:, :], "gs", T.gm[:, :], "gm", "ch", (A.add, A.max)), "gsb": lambda: scan(T.gsb[:, :], "gsb", T.gb[:, :], "gb"),
-            "t1": lambda: tt(T.tt[:, 0:22], T.gs[:, 15:C:16], T.sz[:, 68:132:3], A.max, ["gs", ("sz", 66, 132)], ["t1"]),
-            "t2": lambda: tt(T.tt[:, 22:44], T.gsb[:, 15:C:16], T.tt[:, 0:22], A.min, ["gsb", "t1"], ["t2"]),
-            "t3": lambda: tt(T.t3[:, :], T.tt[:, 22:44], T.sz[:, 134:198:3], A.max, ["t2", ("sz", 132, 198)], ["t3"]),
-            "and": lambda: ts(T.fi[:, :], T.t3[:, :], 511, None, [A.bitwise_and], ["t3"], ["fi"]),
-            "f16": list_out if t >= 0 else lambda: cp(T.rf16[:, :], T.rfi[:, :], ["rfi"], [f16]),
-            "fu": lambda: cp(fu_, T.fi[:, 11:22], ["fi"], [fu]),
-            "zq": upper_out, "lq": lower_quant, "O": lambda: [scaled("S", 4 + p, p, 0) for p in range(4)],
-            "h": lambda: to_columns(T.hr[:, :], "hr"), "g": lambda: to_columns(T[rep][:, C:2 * C], (rep, C, 2 * C)), "i": lambda: to_columns(T.idm[:, :], "idm"),
+            "D": lambda: tt(T.dz[:, 0:198:3], T.x1[:, 3:264:4], T.ba[:, :], A.subtract, ["x1", "ba"], [("D", 0, 3)]),
+            "M": lambda: tt(T.dz[:, 2:198:3], T.x1[:, 3:264:4], T.ba[:, :], A.add, ["x1", "ba"], [("M", 0, 3)]),
+            "S0": lambda: choose(0), "S1": lambda: choose(1), "S2": lambda: choose(2),
+            "oc": lambda: cp(T[cpf][:, 0:44], T.sz[:, 2:132:3], [("sz", 0, 132)], [oc]),
+            "gb": lambda: act(T.gb[:, 0:C], T.sb[:, :].indirect(p_), ["sb", oc], ["gb"]),
+            "Bp": lambda: act(T.gb[:, 0:C], T.sb[:, :].indirect(was), ["sb", wkey], [("gb", 0, C)]),
+            "Bk": lambda: act(T.gb[:, C:2 * C], T.sb[:, :].indirect(T.pka[:, c0:c0 + 22]), ["sb", "pk16%d" % t], [("gb", C, 2 * C)]),
+            "wp": lambda: scan(T.gsb[:, 0:C], ("gsb", 0, C), T.gb[:, 0:C], ("gb", 0, C)),
+            "wk": lambda: scan(T.gsb[:, C:2 * C], ("gsb", C, 2 * C), T.gb[:, C:2 * C], ("gb", C, 2 * C)),
+            "Db": lambda: tt(T.dz[:, 198:264:3], T.gsb[:, C + 15:2 * C:16], T.gsb[:, 15:C:16], A.subtract, ["gsb"], [("D", 3, 4)]),
+            "Mb": lambda: tt(T.dz[:, 200:264:3], T.gsb[:, C + 15:2 * C:16], T.gsb[:, 15:C:16], A.add, ["gsb"], [("M", 3, 4)]),
+            "S3": lambda: choose(3), "yc": lambda: ts(step(T.gs, 57, 5), T.sz[:, 200:264:3], 0.0, None, [A.is_gt], [("sz", 198, 264)], ["yb"]),
+            "gm": lambda: ts(T.gm[:, :], T.bw[:, :].indirect(c_), 1.0, 0.5, [A.add, A.mult], ["bw", oc], ["gm"]),
+            "gs": lambda: scan(T.gs[:, 0:7 * C:7], "gs", T.gm[:, :], "gm"), "gsb": lambda: scan(T.gsb[:, 0:C], "gsb", T.gb[:, 0:C], "gb"),
+            "am": lambda: tt(T.am[:, :], T.sa[:, :].indirect(was), T.mra[:, C * t:C * t + C], A.mult, ["sa", wkey, "mr%d" % t], ["am"]),
+            "gw": lambda: ts(T.kc[:, :], T.bw[:, :].indirect(c_), W0 + MID, -MID - 1, [A.subtract, A.max], ["bw", oc], ["kc"]),
+            "ys": lambda: ts(step(T.gs, 57, 3), step(T.gk, 105, 0), down, -MID - 0.5, [A.mult, A.is_gt], ["gk", "down"], ["gs"]),
+            "gk": lambda: scan(T.gk[:, 0:7 * C:7], "gk", T.kc[:, :], "kc"),
+            "y0": lambda: ts(step(T.gk, 105, 1), T.sz[:, 2:66:3], MID, -1.0, [A.subtract, A.mult], [("sz", 0, 66)], ["y0"]),
+            "y1": lambda: ts(step(T.gk, 105, 3), T.sz[:, 2:66:3], MID, None, [A.subtract], [("sz", 0, 66)], ["y1"]),
+            "y2": lambda: ts(step(T.gk, 105, 4), T.sz[:, 134:198:3], MID, -1.0, [A.subtract, A.mult], [("sz", 132, 198)], ["y2"]),
+            "y3": lambda: ts(step(T.gk, 105, 5), T.sz[:, 134:198:3], MID, None, [A.subtract], [("sz", 132, 198)], ["y3"]),
+            "yb": lambda: ts(step(T.gs, 57, 5), T.gsb[:, 15:C:16], 0.0, None, [A.is_gt], ["gsb"], ["yb"]),
+            "y": lambda: op("V", lambda q: q.tensor_tensor_scan(T.zf[:, :], T.gs[:, 57:57 + 7 * C:16], T.gk[:, 105:105 + 7 * C:16], 0.0, A.mult, A.add),
+                            ["zc", "gs", "gk", "y0", "y1", "y2", "y3", "yb"], ["zf"]),
+            "f16": list_out if t >= 0 else lambda: cp(f_, T.rfi[:, :], ["rfi"], [f16]),
+            "zq": upper_out, "lq": lower_quant, "O": lambda: [scaled("S", p, p, 0) for p in range(4)],
+            "h": lambda: to_columns(T.hr[:, :], "hr"), "g": lambda: to_columns(T[rep][:, C:2 * C], (rep, C, 2 * C)),
             "wh": lambda: scan(T.esc[:, :], "esc", T.ew[:, :], "ew"), "wg": lambda: scan(T.gsc[:, :], "gsc", T.ew[:, :], "ew"),
-            "wc": lambda: scan(T.gsc[:, :], "gsc", T.h2[:, :], "h2"),
-            "we": lambda: scan(T.esc[:, :], "esc", T.hr[:, :], "hr"), "wd": lambda: scan(T.esc[:, :], "esc", T.h2[:, :], "h2"),
+            "we": lambda: scan(T.esc[:, :], "esc", T.hr[:, :], "hr"),
             "g16": lambda: held(g_, g16, T.gsc[:, 15:C:16], "gsc", down, "down", MID, []),
             "e16": lambda: held(e_, e16, T.esc[:, 15:C:16], "esc", down, "down", MID, []),
-            "i16": lambda: held(T.iv[:, c0:c0 + 22], iv0, T.gsc[:, 15:C:16], "gsc", down, "down", MID, []),
-            "io": lambda: ts(T.tt[:, 44:66], T.iv[:, c0:c0 + 22], o_, None, [A.add], [iv0, "o"], ["ivo"]),
-            "wj": lambda: scan(T.wj[:, :], "wj", T.wi[:, :], "wi", "ch", (A.add, A.max)),
-            "j1": lambda: tt(T.ji[:, 0:22], T.wj[:, 15:C:16], T.tt[:, 44:66], A.max, ["wj", "ivo"], ["j1"]),
-            "j2": lambda: ts(T.ji[:, 22:44], T.ji[:, 0:22], 511, None, [A.bitwise_and], ["j1"], ["j2"]),
-            "j3": lambda: cp(T.iv[:, c0:c0 + 22], T.ji[:, 22:44], ["j2"], [iv0]),
-            "K": lambda: kplus("S"), "Kv": lambda: kplus("V"), "w": wrap_lists, "h0": held_lists,
-            "w0": lambda: scan(T.sp[:, 0:C], ("sp", 0, C), T.pkf[:, 0:C], ("pkf", 0, C)),
-            "w1": lambda: scan(T.sp[:, C:2 * C], ("sp", C, 2 * C), T.pkf[:, C:2 * C], ("pkf", C, 2 * C)),
-            "hx": lambda: held(T.x1[:, 0:44], ("x1", 0, 44), T.sp[:, 15:2 * C:16], "sp", half_down, "half_down", mid_o, ["mid_o"]),
-            "hp": lambda: held(T.pka[:, c1:c1 + 22], "pk16%d" % n1, T.sp[:, 15:C:16], ("sp", 0, C), down, "down", MID, []),
-            "bp": lambda: held(T.ba[:, 0:22], ("ba", 0, 22), p_, oc, 0.5, "half_o", half_o, []),
-            "bc": lambda: held(T.ba[:, 22:44], ("ba", 22, 44), f_, f16, 0.5, "half_o", half_o, []),
-            "ba": lambda: ts(T.ba[:, 44:66], f_, 0.5, None, [A.mult], [f16], [("ba", 44, 66)]),
+            "K": lambda: kplus("S", n1), "Kv": lambda: kplus("V", n1), "J": lambda: kplus("S", n1 + 1), "Jv": lambda: kplus("V", n1 + 1),
+            "I": lambda: kplus("S", t), "Iv": lambda: kplus("V", t),
+            "w1": lambda: scan(T.sp[:, 0:C], ("sp", 0, C), T.pkf[:, 0:C], ("pkf", 0, C)),
+            "w0": lambda: scan(T.sp[:, C:2 * C], ("sp", C, 2 * C), T.pkf[:, C:2 * C], ("pkf", C, 2 * C)),
+            "hx": lambda: held(T.x1[:, 3:176:4], ("x1", 0, 44), T.sp[:, 15:2 * C:16], "sp", half_down, "half_down", MID / 2, []),
+            "hf": lambda: held(T.x1[:, 3:88:4], ("x1", 0, 22), T.sp[:, 15:C:16], ("sp", 0, C), half_down, "half_down", MID / 2, []),
+            "hk": lambda: held(T.x1[:, 91:176:4], ("x1", 22, 44), T.sp[:, C + 15:2 * C:16], ("sp", C, 2 * C), half_down, "half_down", MID / 2, []),
+            "hp": lambda: held(T.pka[:, c1:c1 + 22], "pk16%d" % n1, T.sp[:, C + 15:2 * C:16], ("sp", C, 2 * C), down, "down", MID, []),
+            "bc": lambda: ts(T.ba[:, 0:22], f_, 0.5, None, [A.mult], [f16], [("ba", 0, 22)]),
+            "ba": lambda: ts(T.ba[:, 22:66], T[cpf][:, 22:66], 0.5, None, [A.mult], [oc, f16], [("ba", 22, 66)]),
             "v": lambda: quantize(T.vq[:, :], T.vs[:, :], T.vt[:, :], ["vt"], ["vq"]),
         }
+        parts["r0"] = lambda: held(T.r1[:, 88 * n1 + 2:88 * n1 + 88:4], "rx", T.sp[:, 15:C:16], ("sp", 0, C), half_down, "half_down", MID / 2, [])
+        parts["r1"] = lambda: tt(T.r0[:, 1:88:4], T.x1[:, 3:88:4], T.thr[:, 66 + c1:88 + c1], A.is_ge, [("x1", 0, 22), "thr"], ["rb"])
+        parts["r2"] = lambda: tt(T.r0[:, 2:88:4], T.x1[:, 3:88:4], T.thr[:, c1:c1 + 22], A.is_ge, [("x1", 0, 22), "thr"], ["ra"])
         for nm, r in (("r", n1), ("n", t)):
-            parts[nm + "0"] = lambda r=r: tt(T.xx[:, :], T.x1[:, 22:44], T.qk[:, 22 * r:22 * r + 22], A.add, [("x1", 22, 44), "qk"], ["xx"])
-        parts["r1"] = lambda: ts(T.nn[:, :], T.xx[:, :], 1.0 / MID, 0.4986, [A.mult, A.subtract], ["xx"], ["nn"])
-        parts["r2"] = lambda: ts(T.nn[:, :], T.nn[:, :], -176.0, None, [A.mult], ["nn"], ["nn"])
-        parts["r3"] = lambda: tt(T.x1[:, 44:66], T.xx[:, :], T.nn[:, :], A.add, ["xx", "nn"], [("x1", 44, 66)])
-        pb, fb = ((oc, 0), (f16, 0)) if t >= 0 else (("pp16", 0), ("rf16", 0))
+            parts[nm + "3"] = lambda r=r: op("V", lambda q: q.tensor_tensor_scan(T.x1[:, 176:264], T.r0[:, :], T.r1[:, 88 * r:88 * r + 88], 0.0, A.mult, A.add),
+                                             ["rc", "rx", "ra", "rb", "qk"], [("x1", 44, 66)])
+        pb, fb = (cpf, 22), (cpf, 44)
         both("R", (rep, 0), rep, T.idm[:, :], "idm", pb, oc)
         both("Q", (rep, C), rep, T.idm[:, :], "idm", fb, f16)
-        both("P", ("pkf", 0), "pkf", T[rep][:, 0:C], (rep, 0, C), ("pr16", c1), "pr16")
-        both("F", ("pkf", C), "pkf", T[rep][:, C:2 * C], (rep, C, 2 * C), ("pr16", c1), "pr16")
+        both("P", ("pkf", C), "pkf", T[rep][:, 0:C], (rep, 0, C), ("pr16", c1), "pr16")
+        both("F", ("pkf", 0), "pkf", T[rep][:, C:2 * C], (rep, C, 2 * C), ("pr16", c1), "pr16")
         if t == 2:
             parts["R"] = places_out
         if t >= 0:
+            both("A", ("am", 0), "am", T.sa[:, :], "sa", ("cpf%d" % t, 22), wkey)
+            both("C", ("kc", 0), "kc", T.mra[:, C * t:C * t + C], "mr%d" % t, (cpf, 0), oc)
             both("T", ("fsr", 0), "fsr", T.idm[:, :], "idm", (fs, 0), fs)
             both("H", ("hr", 0), "hr", T.fsr[:, :], "fsr", fb, f16)
             both("E", ("hr", 0), "hr", T.fsr[:, :], "fsr", ("g16a", c0), g16)
-            both("Y", ("h2", 0), "h2", T.hr[:, :], "hr", ("iv", c0), iv0)
-            both("C", ("h2", 0), "h2", T[rep][:, C:2 * C], (rep, C, 2 * C), ("iv", c0), iv0)
-            both("W", ("wi", 0), "wi", T.bw[:, :], "bw", ("iv", c0 - 22), "iv%d" % (t - 1))
         for p in range(4):
+            parts["G%d" % p] = lambda p=p: act(T.gp[:, C * p:C * p + C], T.fp[:, C * p:C * p + C].indirect(p_), ["fp%d" % p, oc], ["gp%d" % p], scale=0.5)
             parts["e%d" % p] = lambda p=p: quantize(T.eq[:, 128 * p:128 * p + 128], T.es[:, 128 * p:128 * p + 128], T.et[:, 3 - p:515 - p], ["et"], ["eq%d" % p])
-            parts["F%d" % p] = lambda p=p: values(p)
+            parts["F%d" % p] = lambda p=p: values(p, n1)
+            parts["f%d" % p] = lambda p=p: values(p, t)
             parts["U%d" % p] = lambda p=p: unpack(t, p)
+            parts["Y%d" % p] = lambda p=p: dma("Y", T.g2[:, C * p:C * p + LOW], T.gp[:, C * p:C * p + LOW], ["gp%d" % p], [("g2", C * p, C * p + LOW)])
+            for nm, a in (("fa", 0), ("fb", H)):
+                parts["%s%d" % (nm, p)] = lambda p=p, a=a: cp(T.fp[:, C * p + a:C * p + a + H], T["b%d" % (4 + p)][:, a:a + H], [("b%d" % (4 + p), 0, 1)], [("fp%d" % p, a, a + H)])
             parts["c%d" % p] = lambda p=p: half_copy("V", p, 0, C)
-            parts["u%d" % p] = lambda p=p: half_copy("V", p, H, C)
-            parts["m%d" % p] = lambda p=p: half_copy("V", p, 0, H)
-            parts["L%d" % p] = lambda p=p: half_copy("S", p, 0, H)
-            parts["z%d" % p] = lambda p=p: mix("ztu", fu_, fu, H, p)
-            parts["l%d" % p] = lambda p=p: mix("ztl", T[f16][:, 0:11], f16, 0, p)
+            parts["u%d" % p] = lambda p=p: half_copy("V", p, LOW, C)
+            parts["m%d" % p] = lambda p=p: half_copy("V", p, 0, LOW)
+            parts["L%d" % p] = lambda p=p: half_copy("S", p, 0, LOW)
+            parts["N%d" % p] = lambda p=p: half_copy("S", p, LOW, C)
+            parts["W%d" % p] = lambda p=p: op("G", lambda q: q.affine_select(T.g2[:, C * p + LOW:C * p + C], T.gp[:, C * p + LOW:C * p + C], [[0, C - LOW]], A.is_ge, 0.0, 1, 0),
+                                              ["gp%d" % p, "Gq"], [("g2", C * p + LOW, C * p + C)])
+            lo, hi, n, v = ((2, 66, 1, -1.0), (2, 66, 3, 1.0), (134, 198, 4, -1.0), (134, 198, 5, 1.0))[p]
+            parts["j%d" % p] = lambda p=p, lo=lo, hi=hi, n=n, v=v: act(step(T.gk, 105, n), T.sz[:, lo:hi:3], [("sz", lo - 2, hi)], ["y%d" % p], F.Identity, scale=v, bias=-v * MID)
+            parts["z%d" % p] = lambda p=p: mix(p, LOW, C)
+            parts["l%d" % p] = lambda p=p: mix(p, 0, LOW)
             parts["B%d" % p] = lambda p=p: their_half("S", p)
             parts["V%d" % p] = lambda p=p: their_half("V", p)
-            parts["O%d" % p] = lambda p=p: scaled("S", 4 + p, p, 0)
-            parts["o%d" % p] = lambda p=p: scaled("V", 4 + p, p, 0)
+            parts["O%d" % p] = lambda p=p: scaled("S", p, p, 0)
+            parts["o%d" % p] = lambda p=p: scaled("V", p, p, 0)
+            for how in "sax":
+                parts["%s%d" % (how, p)] = lambda how=how, p=p: new_x(how, p, None)
             for i in range(2):
                 parts["q%d" % i] = lambda i=i: quant(i)
+                parts["sa%d" % i] = lambda i=i: signs(0, i)
+                parts["sb%d" % i] = lambda i=i: signs(1, i)
                 for how in "sax":
                     parts["%s%d%d" % (how, p, i)] = lambda how=how, p=p, i=i: new_x(how, p, i)
         return parts

from concourse.bass import DstId, RemoteDMATransfer
from concourse.mybir import dt, AluOpType, ActivationFunctionType

A, F = AluOpType, ActivationFunctionType
N, C, H = 8, 352, 176
STEP = [4, 1, 2]
CH = [(0, 224), (224, 352)]
LOW = 160
CUT = ((0, 11), (11, 22))
HQ = 132
BIG = 2.0 ** 40
W0 = 2.0 ** 18
MID = 176.0
HEAD = "f0 Bp Bk f1 f2 f3 "
LISTS = " wk S0 S1 Db Mb oc G0 G1 G2 G3 S2 S3 gw y0 y1 gk y2 y3 yc ys y u0 f16 u1 "
UPPER = " z0 u2 z1 u3 z2 z3 "
NEW = " B0 B1 B2 B3 s20 s30 s21 s31 s11 x0 x10 a20 a30 a21 q0 a31 a11 "
ORDER = [
    "e0 e1 p16 R k16 f16 Q e2 uo e3 uq F us P ba bc qk ua q0 d0 d1 w1 d2 q1 sa0 sa1 sb0 sb1 hf Kv w0 r0 r1 r2 hp hk",
    HEAD + "am n3 bw wp D M sE" + LISTS + "m0 m1" + UPPER + "m2 m3 zq Q R F l0 l1 l2 l3 lq g K P T O w1 wg bc g16 w0 ba r0 E hx r1 r2 hp r3 we D e16" + NEW + "sa0 sb0 M q1 sa1 Jv sb1",
    HEAD + "am bw wp sE" + LISTS + "Y0 Y1 Y2 Y3" + UPPER + "ba zq R Q T Hb l0 l1 l2 l3 Ha P lq h F O wh w1 e16 w0" + NEW + "hp sa0 sb0 q1 hx bc r0 r1 r2 sa1 sb1 r3",
    HEAD + "M am D bw wp sE" + LISTS + "Y0 Y1 Y2 Y3" + UPPER + "v zq R Q l0 l1 l2 l3 lq g O wg Ta Tb g16 Ea Eb we e16" + NEW + "q1",
]

SCRATCH = {
    "xin": ("sbuf", [128, 4 * C], "bfloat16"), "xt": ("sbuf", [128, 4 * C], "bfloat16"),
    "ut": ("sbuf", [128, 512], "bfloat16"), "vt": ("sbuf", [128, 512], "bfloat16"),
    "uq": ("sbuf", [128, 128], "float8_e4m3fn_x4"), "us": ("sbuf", [128, 128], "uint8"),
    "ua": ("sbuf", [128, 256], "float8_e4m3fn_x4"), "uas": ("sbuf", [128, 256], "uint8"),
    "vq": ("sbuf", [128, 128], "float8_e4m3fn_x4"), "vs": ("sbuf", [128, 128], "uint8"),
    "wq": ("sbuf", [128, 512], "float8_e4m3fn_x4"), "wsp": ("sbuf", [128, 512], "uint8"),
    "one": ("sbuf", [128, 128], "bfloat16"), "et": ("sbuf", [128, 516], "bfloat16"),
    "eq": ("sbuf", [128, 512], "float8_e4m3fn_x4"), "es": ("sbuf", [128, 512], "uint8"),
    "ppi": ("sbuf", [128, 22], "int32"), "rfi": ("sbuf", [128, 22], "int32"), "pri": ("sbuf", [128, 66], "int32"),
    "pr16": ("sbuf", [128, 66], "uint16"), "idm": ("sbuf", [128, C], "bfloat16"), "ck": ("sbuf", [128, C], "bfloat16"),
    "pm": ("sbuf", [128, 22], "int32"), "mo": ("sbuf", [128, 22], "uint16"), "d16": ("sbuf", [128, 16], "int32"),
    "pat": ("sbuf", [128, 48], "float32"), "wt": ("sbuf", [128, 26], "float32"),
    "uoi": ("sbuf", [128, 16], "int32"), "uo": ("sbuf", [128, 16], "uint16"),
    "q16": ("sbuf", [128, 66], "int32"), "qk": ("sbuf", [128, 66], "float32"),
    "sa": ("sbuf", [128, C], "bfloat16"), "sb": ("sbuf", [128, C], "bfloat16"), "am": ("sbuf", [128, C], "bfloat16"), "bw": ("sbuf", [128, C], "bfloat16"),
    "sE": ("sbuf", [128, 3 * C], "bfloat16"), "dz": ("sbuf", [128, 264], "float32"), "sz": ("sbuf", [128, 264], "float32"),
    "gm": ("sbuf", [128, C], "bfloat16"), "gs": ("sbuf", [128, 2576], "bfloat16"), "kc": ("sbuf", [128, C], "bfloat16"), "gk": ("sbuf", [128, 2576], "bfloat16"),
    "gb": ("sbuf", [128, 2 * C], "bfloat16"), "gsb": ("sbuf", [128, 2 * C], "bfloat16"),
    "zf": ("sbuf", [128, 154], "bfloat16"),
    "pkf": ("sbuf", [128, 2 * C], "bfloat16"), "sp": ("sbuf", [128, 2 * C], "bfloat16"),
    "x1": ("sbuf", [128, 264], "float32"), "ba": ("sbuf", [128, 66], "float32"),
    "r0": ("sbuf", [128, 88], "float32"), "r1": ("sbuf", [128, 264], "float32"), "thr": ("sbuf", [128, 132], "float32"),
    "fsr": ("sbuf", [128, C], "bfloat16"), "hr": ("sbuf", [128, C], "bfloat16"), "ew": ("sbuf", [128, C], "bfloat16"),
    "esc": ("sbuf", [128, C], "bfloat16"), "gsc": ("sbuf", [128, C], "bfloat16"),
    "fp": ("sbuf", [128, 4 * C], "bfloat16"), "gp": ("sbuf", [128, 4 * C], "bfloat16"), "bp": ("sbuf", [128, 4 * C], "bfloat16"),
    "bg": ("sbuf", [128, 4 * C], "bfloat16"), "g2": ("sbuf", [128, 4 * C], "bfloat16"),
    "zt": ("sbuf", [128, 4 * C], "bfloat16"),
    "yt": ("sbuf", [128, C], "float32"), "pfo": ("sbuf", [128, 2 * C], "float32"),
    "pka": ("sbuf", [128, 66], "uint16"), "e16a": ("sbuf", [128, 66], "uint16"), "g16a": ("sbuf", [128, 66], "uint16"),
    "mra": ("sbuf", [128, 3 * C], "bfloat16"),
    "hq": ("sbuf", [128, H], "float8_e4m3fn_x4"), "hs": ("sbuf", [128, H], "uint8"), "hl": ("sbuf", [128, 22], "uint16"),
}
if W0:
    for k in ("am", "bw", "sE", "mra"):
        SCRATCH[k] = SCRATCH[k][:2] + ("float32",)
for k in range(8):
    SCRATCH["b%d" % k] = ("psum", [128, 512], "float32")
for k in range(4):
    SCRATCH["xq%d" % k] = ("sbuf", [128, C], "float8_e4m3fn_x4")
    SCRATCH["xs%d" % k] = ("sbuf", [128, C], "uint8")
    SCRATCH["rep%d" % k] = ("sbuf", [128, 2 * C], "bfloat16")
    SCRATCH["cpf%d" % k] = ("sbuf", [128, 66], "uint16")
for k in range(3):
    for nm in ("zu", "zl", "zr"):
        SCRATCH["%sq%d" % (nm, k)] = ("sbuf", [128, H], "float8_e4m3fn_x4")
        SCRATCH["%ss%d" % (nm, k)] = ("sbuf", [128, H], "uint8")
    SCRATCH["fs%d" % k] = ("sbuf", [128, 22], "uint16")

ENG = {"V": "sv", "S": "ss", "P": "st", "G": "sg"}
SEMAPHORES = ["sv", "ss", "st", "sg", "rl", "hla", "hca", "hsa"] + ["la%d" % k for k in range(3)] + ["za%d" % k for k in range(3)] + ["d%d" % k for k in range(40)]


def machine(g, T):
    queues = {"V": g.vector, "S": g.scalar, "P": g.tensor, "G": g, "Y": g.sync}
    know = {q: {} for q in queues}
    cnt, hist, behind, ndma = {}, {}, {}, [0]

    def need(q, tok):
        sem, val = tok
        k = know[q]
        if k.get(sem, 0) >= val:
            return
        queues[q].wait_ge(T.sem[sem], val)
        k[sem] = val
        for s, v in behind.get(tok, {}).items():
            k[s] = max(k.get(s, 0), v)

    def norm(rs):
        return [(r, 0, 1 << 30) if isinstance(r, str) else r for r in rs]

    def before(q, rd, wr):
        toks = []
        for key, lo, hi in rd:
            toks += [tok for (l, h, tok, w) in hist.get(key, []) if w and l < hi and lo < h]
        for key, lo, hi in wr:
            toks += [tok for (l, h, tok, w) in hist.get(key, []) if l < hi and lo < h]
        best = {}
        for s, v in toks:
            best[s] = max(best.get(s, 0), v)
        own = ENG.get(q)
        for s in sorted(best, key=lambda s: s == own):
            need(q, (s, best[s]))

    def after(tok, rd, wr):
        for key, lo, hi in wr:
            hist[key] = [e for e in hist.get(key, []) if not (lo <= e[0] and e[1] <= hi)] + [(lo, hi, tok, True)]
        for key, lo, hi in rd:
            hist.setdefault(key, []).append((lo, hi, tok, False))

    def op(q, call, rd, wr):
        rd, wr = norm(rd), norm(wr)
        before(q, rd, wr)
        sem = ENG[q]
        cnt[sem] = cnt.get(sem, 0) + 1
        tok = (sem, cnt[sem])
        call(queues[q]).then_inc(T.sem[sem], 1)
        behind[tok] = dict(know[q])
        after(tok, rd, wr)

    def dma(q, out, in_, rd, wr):
        rd, wr = norm(rd), norm(wr)
        before(q, rd, wr)
        sem = "d%d" % ndma[0]
        ndma[0] += 1
        cnt[sem] = 16
        queues[q].dma_start(out, in_).then_inc(T.sem[sem], 16)
        behind[(sem, 16)] = dict(know[q])
        after((sem, 16), rd, wr)

    def lands(key, sem, val):
        after((sem, val), [], norm([key]))

    def sends(rd, n, call):
        before("G", norm(rd), [])
        call()
        cnt["rl"] = cnt.get("rl", 0) + n

    def finish():
        for s in sorted(cnt, key=lambda s: s[0] == "d"):
            need("Y", (s, cnt[s]))
    return op, dma, lands, sends, finish


def bits(topo, src, dst, n=16, skip=0):
    e = topo.engines(src, dst)[skip:skip + n]
    return sum(1 << i for i in e), len(e)


def helpers(T, topo, src, dst):
    if topo.may_write(src, dst):
        return []
    return [c for c in topo.cores_of(src) if c not in T.cores and topo.die(c) == topo.die(src) and topo.may_write(c, dst)][:2]


def send(g, T, topo, src, dst, out, in_, rsem):
    rid, pid = topo.addr(dst, src)
    m, k = bits(topo, src, dst)
    g.remote_dma(out_ap=out, in_ap=in_, remote_sem=T.sem[rsem], local_sem=T.sem.rl, pid=pid, routing_id=rid, dma_engine_mask=m)
    return k


def send_two(g, T, topo, src, pieces):
    both = []
    for n, (dst, out, in_, rsem) in enumerate(pieces):
        rid, pid = topo.addr(dst, src)
        k = bits(topo, src, dst)[1] // 2
        both.append(RemoteDMATransfer(dst_ids=[DstId(rid=rid, pnc=pid)], dma_engine_mask=bits(topo, src, dst, k, k * n)[0], remote_sem=T.sem[rsem], src=in_, dst=out))
    g.remote_dma_fused(both, local_sem=T.sem.rl)
    return 2 * k


def codes(buf, a, b):
    return buf[:, a:b].bitcast(dt.uint8)


def hand_on(g, core, T, topo):
    n = [0]
    for r, src in enumerate(T.cores):
        for t, s in enumerate(STEP):
            dst = T.cores[r ^ s]
            hp = helpers(T, topo, src, dst)
            if core not in hp:
                continue
            k, zq, zs, za = bits(topo, src, core)[1], T["zrq%d" % t], T["zrs%d" % t], "za%d" % t
            a, b = CUT[hp.index(core)]
            g.wait_ge(T.sem.hla, k // 2)
            n[0] += send(g, T, topo, core, dst, T["fs%d" % t][:, a:b], T.hl[:, a:b], "la%d" % t)
            g.wait_ge(T.sem.hca, k)
            if core == hp[0]:
                n[0] += send(g, T, topo, core, dst, codes(zq, 0, HQ), codes(T.hq, 0, HQ), za)
            else:
                n[0] += send_two(g, T, topo, core, [(dst, codes(zq, HQ, H), codes(T.hq, HQ, H), za), (dst, zs[:, 0:H], T.hs[:, 0:H], za)])
    if n[0]:
        g.wait_ge(T.sem.rl, n[0])


def rank_program(g, core, T, topo):
    rank = T.rank_of(core)
    if rank is None:
        return hand_on(g, core, T, topo)
    op, dma, lands, sends, finish = machine(g, T)
    copy, sign = F.Copy, F.Sign

    for t in range(3):
        src = T.cores[rank ^ STEP[t]]
        hp = helpers(T, topo, src, core)
        if hp:
            lands("fs%d" % t, "la%d" % t, sum(bits(topo, c, core)[1] for c in hp))
            lands("zr%d" % t, "za%d" % t, sum(bits(topo, c, core)[1] for c in hp))
        else:
            lands("fs%d" % t, "la%d" % t, bits(topo, src, core)[1])
            lands("zr%d" % t, "za%d" % t, 2 * bits(topo, src, core)[1])

    dma("S", T.ppi[:, :], T.pp[:, :], [], ["ppi"])
    dma("Y", T.pri[:, :], T.pr[:, :], [], ["pri"])
    dma("S", T.rfi[:, :], T.rf[:, :], [], ["rfi"])
    dma("Y", T.ut[:, :], T.u[:, :], [], ["ut"])
    for i, (a, b) in enumerate(CH):
        dma("Y", T.xin[:, 4 * a:4 * b], T.x[:, 4 * a:4 * b], [], [("xin", a, b)])
    dma("Y", codes(T.wq, 0, 512), T.wc[:, :], ["xin"], ["wq"])
    dma("Y", T.wsp[:, 0:512], T.ws[:, :], [], ["wsp"])
    dma("Y", T.vt[:, :], T.v[:, :], [], ["vt"])

    def ts(out, in0, s1, s2, ops, rd, wr):
        op("V", lambda q: q.tensor_scalar(out, in0, s1, s2, *ops), rd, wr)

    def tt(out, in0, in1, o, rd, wr):
        op("V", lambda q: q.tensor_tensor(out, in0, in1, o), rd, wr)

    def cp(out, in_, rd, wr):
        op("V", lambda q: q.tensor_copy(out, in_), rd, wr)

    def act(out, in_, rd, wr, func=copy, **kw):
        op("S", lambda q: q.activation(out, in_, func, **kw), rd, wr)

    def fill(ap, v, wr):
        op("V", lambda q: q.memset(ap, v), [], wr)

    def iota(out, pattern, base, step, wr, **kw):
        op("G", lambda q: q.iota(out, pattern, base, step, **kw), [], wr)

    def quantize(cq, cs, tile, rd, wr):
        op("V", lambda q: q.quantize_mx(cq, cs, tile), rd, wr)

    def scan(out, okey, data, dkey, fac="ck", ops=(A.mult, A.add)):
        op("V", lambda q: q.tensor_tensor_scan(out, T[fac][:, :], data, 0.0, *ops), [fac, dkey], [okey])

    def step(buf, first, n):
        return buf[:, first + 16 * n:first + 16 * n + 7 * C - 111:112]

    down, half_down, own = T.wt[:, 0:1], T.wt[:, 22:23], T.wt[:, 23:24]
    loose = dict(allow_small_or_imprecise_dtypes=True)
    iota(T.pm[:, :], [[0, 22]], 0, 1, ["pm"])
    iota(T.d16[:, :], [[1, 16]], 128, -1, ["d16"])
    fill(T.one[:, :], 1.0, ["one"])
    fill(T.et[:, :], 0.0, ["et"])
    op("G", lambda q: q.affine_select(T.et[:, 3:515:4], T.one[:, :], [[-1, 128]], A.is_equal, 0.0, 0, 1), ["one"], ["et"])
    iota(T.idm[:, :], [[1, C]], -int(MID), 0, ["idm"], **loose)
    iota(T.uoi[:, :], [[1, 2], [16, 8]], 0, 0, ["uoi"])
    iota(T.q16[:, :], [[0, 3], [16, 22]], C, 0, ["q16"])
    for view, n, v, key in ((T.sE[:, 13:3 * C:48], 22, 0.0, "sE0"), (T.dz[:, 1:264:3], 88, 0.0, "dz0"),
                            (step(T.gs, 57, 0), 22, 0.0, ("zc", 0, 1)), (step(T.gs, 57, 4), 22, 1.0, ("zc", 4, 5)), (step(T.gs, 57, 6), 22, 1.0, ("zc", 6, 7)),
                            (step(T.gk, 105, 2), 22, 0.0, ("zc", 7, 8)), (step(T.gk, 105, 6), 22, 0.0, ("zc", 8, 9)),
                            (T.r0[:, 0:88:4], 22, 0.0, ("rc", 0, 1)), (T.r0[:, 3:88:4], 22, 1.0, ("rc", 1, 2)),
                            (T.r1[:, 0:264:4], 66, -MID, ("rc", 2, 3)), (T.r1[:, 1:264:4], 66, -MID, ("rc", 3, 4))):
        act(view, T.one[:, 0:n], ["one"], [key], scale=v)
    ts(T.pm[:, :], T.pm[:, :], 15, None, [A.bitwise_and], ["pm"], ["pm"])
    ts(T.d16[:, :], T.d16[:, :], 15, None, [A.bitwise_and], ["d16"], ["d16"])
    cp(T.mo[:, :], T.pm[:, :], ["pm"], ["mo"])
    ts(T.wt[:, 0:22], T.pm[:, :], 15.0, 1.0 / BIG, [A.is_equal, A.max], ["pm"], ["down"])
    ts(T.pat[:, 0:16], T.d16[:, :], 1.0, BIG, [A.is_equal, A.mult], ["d16"], ["pat0"])
    ts(T.pat[:, 16:32], T.d16[:, :], 1.0, None, [A.min], ["d16"], ["pat1"])
    for n, v in enumerate((0.0, 0.5 - C, 0.5 - 2 * C)):
        ts(T.wt[:, 23 + n:24 + n], T.pm[:, 0:1], v, None, [A.add], ["pm"], [("own", n, n + 1)])
    tt(T.pat[:, 32:48], T.pat[:, 0:16], T.pat[:, 16:32], A.max, ["pat0", "pat1"], ["pat2"])
    act(T.ck[:, :], T.pat[:, 32:48].indirect(T.mo[:, 0:22]), ["pat2", "mo"], ["ck"])
    ts(half_down, down, 0.5, None, [A.mult], ["down"], ["half_down"])
    ts(T.sE[:, 29:3 * C:48], T.wt[:, 0:22], 1.0 / (W0 + MID) if W0 else 1.0, None, [A.mult], ["down"], ["sE1"])
    cp(step(T.gs, 57, 1), T.wt[:, 0:22], ["down"], [("zc", 1, 2)])
    if W0:
        fill(step(T.gs, 57, 2), 1.0, [("zc", 2, 3)])
    else:
        cp(step(T.gs, 57, 2), T.wt[:, 0:22], ["down"], [("zc", 2, 3)])

    def mm(bank, side, scale, c0, rq, rs, a, b, rd):
        op("P", lambda q: q.matmul_mx(T["b%d" % bank][:, 0:b - a], T[side][:, c0:c0 + 128], T[scale][:, c0:c0 + 128],
                                      T[rq][:, a:b], T[rs][:, a:b], True, True), rd, ["b%d" % bank])

    def held(out, okey, view, key, mul, mkey, add, akey):
        ts(out, view, mul, add, [A.mult, A.add], [key, mkey] + akey, [okey])

    def parts_of(t):
        n1 = t + 1
        xq, xs, xq1, xs1 = "xq%d" % t, "xs%d" % t, "xq%d" % n1, "xs%d" % n1
        oc, f16, fu, e16, g16 = [n + str(t) for n in ("oc", "f16", "fu", "e16", "g16")]
        rep, fs = "rep%d" % n1, "fs%d" % t
        c0, c1 = 22 * t, 22 * n1
        if t >= 0:
            e_, g_ = T.e16a[:, c0:c0 + 22], T.g16a[:, c0:c0 + 22]
            was, wkey = T["cpf%d" % t][:, 22:44], "oc%d" % (t - 1)
            dst = T.cores[rank ^ STEP[t]]
            hp = helpers(T, topo, core, dst)
        cpf = "cpf%d" % n1
        c_, p_, f_ = T[cpf][:, 0:22], T[cpf][:, 22:44], T[cpf][:, 44:66]

        def unpack(tq, p):
            mm(4 + p, "eq", "es", 128 * p, "xq%d" % tq, "xs%d" % tq, 0, C, ["eq%d" % p, "xq%d" % tq])

        def values(p, r):
            unpack(r, p)
            act(T.fp[:, C * p:C * p + C], T["b%d" % (4 + p)][:, 0:C], [], ["b%d" % (4 + p), "fp%d" % p])

        def quant(i):
            a, b = CH[i]
            buf, keys = ("xt", [("xt%d" % p, a, b) for p in range(4)]) if t >= 0 else ("xin", [("xin", a, b)])
            quantize(T[xq1][:, a:b], T[xs1][:, a:b], T[buf][:, 4 * a:4 * b], keys, [(xq1, a, b)])
            if t == 2:
                return store(i)
            for n in range(2):
                mm(2 * i + n, "ua", "uas", 128 * n, xq1, xs1, a, b, ["ua", "uas", (xq1, a, b)])

        def signs(n, i):
            (a, b), nm = CH[i], ("sa", "sb")[n]
            act(T[nm][:, a:b], T["b%d" % (2 * i + n)][:, 0:b - a], [], ["b%d" % (2 * i + n), (nm, a, b)], sign, bias=-(2.0 ** -100))

        def store(i):
            a, b = CH[i]
            mm(i, "vq", "vs", 0, xq1, xs1, a, b, ["vq", (xq1, a, b)])
            dma("Y", T.oc[:, 4 * a:4 * b], codes(T[xq1], a, b), [(xq1, a, b)], ["ocout%d" % i])
            for k in range(4):
                dma("Y" if k < 2 or i == 0 else "S", T.osc[4 * k:4 * k + 4, a:b], T[xs1][32 * k:32 * k + 4, a:b], [(xq1, a, b)], ["oscout%d%d" % (i, k)])
            (act if i == 0 else cp)(T.yt[:, a:b], T["b%d" % i][:, 0:b - a], [], ["b%d" % i, ("yt", a, b)])
            dma("Y" if i == 0 else "S", T.y[:, a:b], T.yt[:, a:b], [("yt", a, b)], ["yout%d" % i])

        def pick(q0, out, okey, win, wkey, off, key, a=0, b=22):
            buf, lo = off
            (cp if q0 == "V" else act)(T[out[0]][:, out[1] + 16 * a:out[1] + 16 * b], win.indirect(T[buf][:, lo + a:lo + b]), [wkey, key], [(okey, out[1] + 16 * a, out[1] + 16 * b)])

        def both(name, *args):
            parts[name] = lambda: pick("S", *args)
            parts[name + "v"] = lambda: pick("V", *args)
            parts[name + "a"] = lambda: pick("V", *args, 0, 12)
            parts[name + "b"] = lambda: pick("S", *args, 12, 22)

        def kplus(q0, r):
            o, k = T.mra[:, C * r:C * r + C], T.pr16[:, 22 * r:22 * r + 22]
            if not W0:
                (cp if q0 == "V" else act)(o, T.idm[:, :].indirect(k), ["pr16", "idm"], ["mr%d" % r])
            elif q0 == "V":
                ts(o, T.idm[:, :].indirect(k), W0 + MID, None, [A.add], ["pr16", "idm"], ["mr%d" % r])
            else:
                act(o, T.idm[:, :].indirect(k), ["pr16", "idm"], ["mr%d" % r], F.Identity, bias=W0 + MID)

        def choose(n):
            a = 66 * n
            op("V", lambda q: q.tensor_tensor_scan(T.sz[:, a:a + 66], T.sE[:, 13:3 * C:16], T.dz[:, a:a + 66], 0.0, A.mult, A.add),
               ["sE", "sE0", "sE1", "dz0", ("D", n, n + 1), ("M", n, n + 1)], [("sz", a, a + 66)])

        def list_out():
            ts(f_, T.zf[:, 5:154:7], MID, None, [A.add], ["zf"], [f16])
            if hp:
                sends([f16], bits(topo, core, hp[0])[1], lambda: send_two(g, T, topo, core, [(c, T.hl[:, a:b], T[cpf][:, 44 + a:44 + b], "hla") for c, (a, b) in zip(hp, CUT)]))
            else:
                sends([f16], bits(topo, core, dst)[1], lambda: send(g, T, topo, core, dst, T[fs][:, 0:22], f_, "la%d" % t))

        def half_copy(q0, p, a, b):
            a, b = C * p + a, C * p + b
            (cp if q0 == "V" else act)(T.g2[:, a:b], T.gp[:, a:b], ["gp%d" % p], [("g2", a, b)])

        def mix(p, a, b):
            o = C * p
            tt(T.zt[:, 4 * a + p:4 * b:4], T.gp[:, o:o + C].indirect(T[cpf][:, 44 + a // 16:44 + b // 16]), T.g2[:, o + a:o + b], A.add,
               ["gp%d" % p, ("g2", o + a, o + b), f16], [("zt%d" % p, a, b)])

        def zquant(a, nm):
            quantize(T["%sq%d" % (nm, t)][:, :], T["%ss%d" % (nm, t)][:, :], T.zt[:, 4 * a:4 * (a + H)], [("zt%d" % p, a, a + H) for p in range(4)], ["%sq%d" % (nm, t)])

        def upper_out():
            zquant(H, "zu")
            zq, zs, za = "zuq%d" % t, "zus%d" % t, "za%d" % t
            if hp:
                k = bits(topo, core, hp[0])[1]
                sends([zq], k, lambda: send(g, T, topo, core, hp[0], codes(T.hq, 0, HQ), codes(T[zq], 0, HQ), "hca"))
                sends([zq], k, lambda: send_two(g, T, topo, core, [(hp[1], codes(T.hq, HQ, H), codes(T[zq], HQ, H), "hca"), (hp[1], T.hs[:, 0:H], T[zs][:, 0:H], "hca")]))
            else:
                k = bits(topo, core, dst)[1]
                sends([zq], k, lambda: send(g, T, topo, core, dst, codes(T["zrq%d" % t], 0, H), codes(T[zq], 0, H), za))
                sends([zq], k, lambda: send(g, T, topo, core, dst, T["zrs%d" % t][:, 0:H], T[zs][:, 0:H], za))

        def lower_quant():
            zquant(0, "zl")
            for p in range(4):
                mm(p, "wq", "wsp", 128 * p, "zlq%d" % t, "zls%d" % t, 0, H, ["wq", "wsp", "zlq%d" % t])

        def scaled(q0, bank, p, a):
            o, i_, wr = T.bp[:, C * p + a:C * p + a + H], T["b%d" % bank][:, 0:H], ["b%d" % bank, ("bp%d" % p, a, a + H)]
            if q0 == "S":
                act(o, i_, [], wr, scale=0.03125)
            else:
                ts(o, i_, 0.03125, None, [A.mult], [], wr)

        def their_half(q0, p):
            mm(p, "wq", "wsp", 128 * p, "zrq%d" % t, "zrs%d" % t, 0, H, ["wq", "wsp", "zr%d" % t])
            scaled(q0, p, p, H)

        def to_columns(src, key):
            cp(T.ew[:, :].indirect(p_), src, [key, oc], ["ew"])

        def places_out():
            for n, (off, key) in enumerate(((p_, oc), (f_, f16))):
                act(T.pfo[:, C * n:C * n + C], T.idm[:, :].indirect(off), [key, "idm"], [("pfo", C * n, C * n + C)], F.Identity, bias=MID)
            dma("Y", T.pf[:, :], T.pfo[0:128:16, :], ["pfo"], ["pf"])

        def new_x(how, p, i):
            a, b = (0, C) if i is None else CH[i]
            o, e = T.xt[:, 4 * a + p:4 * b:4], T.e16a[:, c0 + a // 16:c0 + b // 16]
            if how == "s":
                act(T.bg[:, C * p + a:C * p + b], T.bp[:, C * p:C * p + C].indirect(e), ["bp%d" % p, e16], [("bg%d" % p, a, b)])
            elif how == "a":
                tt(o, T["b%d" % (4 + p)][:, a:b], T.bg[:, C * p + a:C * p + b], A.add, [("bg%d" % p, a, b)], ["b%d" % (4 + p), ("xt%d" % p, a, b)])
            else:
                tt(o, T.bp[:, C * p:C * p + C].indirect(e), T.fp[:, C * p + a:C * p + b], A.add, ["bp%d" % p, e16, "fp%d" % p], [("xt%d" % p, a, b)])

        def differences():
            tt(T.qk[:, :], T.q16[:, :], T.pri[:, :], A.subtract, ["q16", "pri"], ["qk0"])

        def bounds(n):
            if n == 0:
                ts(T.r1[:, 3:264:4], T.qk[:, :], own, 0.5, [A.add, A.mult], ["qk0", "own"], ["qk"])
            else:
                ts(T.thr[:, 66 * n - 66:66 * n], T.qk[:, :], T.wt[:, 23 + n:24 + n], -0.5, [A.add, A.mult], ["qk0", "own"], [("thr", n, n + 1)])

        parts = {
            "p16": lambda: cp(p_, T.ppi[:, :], ["ppi"], [oc]), "k16": lambda: cp(T.pr16[:, :], T.pri[:, :], ["pri"], ["pr16"]),
            "uo": lambda: cp(T.uo[:, :], T.uoi[:, :], ["uoi"], ["uo"]), "uq": lambda: quantize(T.uq[:, :], T.us[:, :], T.ut[:, :], ["ut"], ["uq"]),
            "ua": lambda: cp(T.ua[:, 0:256].bitcast(dt.uint32), T.uq[:, 0:128].bitcast(dt.uint32).indirect(T.uo[:, 0:16]), ["uq", "uo"], ["ua"]),
            "us": lambda: act(T.uas[:, 0:256], T.us[:, 0:128].indirect(T.uo[:, 0:16]), ["uq", "uo"], ["uas"]),
            "usv": lambda: cp(T.uas[:, 0:256], T.us[:, 0:128].indirect(T.uo[:, 0:16]), ["uq", "uo"], ["uas"]),
            "qk": differences, "d0": lambda: bounds(0), "d1": lambda: bounds(1), "d2": lambda: bounds(2),
            "bw": lambda: tt(T.bw[:, :], T.sa[:, :].indirect(T.pka[:, c0:c0 + 22]), T.am[:, :], A.mult, ["sa", "pk16%d" % t, "am"], ["bw"]),
            "sE": lambda: scan(T.sE[:, 0:3 * C:3], "sE", T.bw[:, :], "bw"),
            "D": lambda: tt(T.dz[:, 0:198:3], T.x1[:, 3:264:4], T.ba[:, :], A.subtract, ["x1", "ba"], [("D", 0, 3)]),
            "M": lambda: tt(T.dz[:, 2:198:3], T.x1[:, 3:264:4], T.ba[:, :], A.add, ["x1", "ba"], [("M", 0, 3)]),
            "S0": lambda: choose(0), "S1": lambda: choose(1), "S2": lambda: choose(2),
            "oc": lambda: cp(T[cpf][:, 0:44], T.sz[:, 2:132:3], [("sz", 0, 132)], [oc]),
            "gb": lambda: act(T.gb[:, 0:C], T.sb[:, :].indirect(p_), ["sb", oc], ["gb"]),
            "Bp": lambda: act(T.gb[:, 0:C], T.sb[:, :].indirect(was), ["sb", wkey], [("gb", 0, C)]),
            "Bk": lambda: act(T.gb[:, C:2 * C], T.sb[:, :].indirect(T.pka[:, c0:c0 + 22]), ["sb", "pk16%d" % t], [("gb", C, 2 * C)]),
            "wp": lambda: scan(T.gsb[:, 0:C], ("gsb", 0, C), T.gb[:, 0:C], ("gb", 0, C)),
            "wk": lambda: scan(T.gsb[:, C:2 * C], ("gsb", C, 2 * C), T.gb[:, C:2 * C], ("gb", C, 2 * C)),
            "Db": lambda: tt(T.dz[:, 198:264:3], T.gsb[:, C + 15:2 * C:16], T.gsb[:, 15:C:16], A.subtract, ["gsb"], [("D", 3, 4)]),
            "Mb": lambda: tt(T.dz[:, 200:264:3], T.gsb[:, C + 15:2 * C:16], T.gsb[:, 15:C:16], A.add, ["gsb"], [("M", 3, 4)]),
            "S3": lambda: choose(3), "yc": lambda: ts(step(T.gs, 57, 5), T.sz[:, 200:264:3], 0.0, None, [A.is_gt], [("sz", 198, 264)], ["yb"]),
            "gm": lambda: ts(T.gm[:, :], T.bw[:, :].indirect(c_), 1.0, 0.5, [A.add, A.mult], ["bw", oc], ["gm"]),
            "gs": lambda: scan(T.gs[:, 0:7 * C:7], "gs", T.gm[:, :], "gm"), "gsb": lambda: scan(T.gsb[:, 0:C], "gsb", T.gb[:, 0:C], "gb"),
            "am": lambda: tt(T.am[:, :], T.sa[:, :].indirect(was), T.mra[:, C * t:C * t + C], A.mult, ["sa", wkey, "mr%d" % t], ["am"]),
            "gw": lambda: ts(T.kc[:, :], T.bw[:, :].indirect(c_), W0 + MID, -MID - 1, [A.subtract, A.max], ["bw", oc], ["kc"]),
            "ys": lambda: ts(step(T.gs, 57, 3), step(T.gk, 105, 0), down, -MID - 0.5, [A.mult, A.is_gt], ["gk", "down"], ["gs"]),
            "gk": lambda: scan(T.gk[:, 0:7 * C:7], "gk", T.kc[:, :], "kc"),
            "y0": lambda: ts(step(T.gk, 105, 1), T.sz[:, 2:66:3], MID, -1.0, [A.subtract, A.mult], [("sz", 0, 66)], ["y0"]),
            "y1": lambda: ts(step(T.gk, 105, 3), T.sz[:, 2:66:3], MID, None, [A.subtract], [("sz", 0, 66)], ["y1"]),
            "y2": lambda: ts(step(T.gk, 105, 4), T.sz[:, 134:198:3], MID, -1.0, [A.subtract, A.mult], [("sz", 132, 198)], ["y2"]),
            "y3": lambda: ts(step(T.gk, 105, 5), T.sz[:, 134:198:3], MID, None, [A.subtract], [("sz", 132, 198)], ["y3"]),
            "yb": lambda: ts(step(T.gs, 57, 5), T.gsb[:, 15:C:16], 0.0, None, [A.is_gt], ["gsb"], ["yb"]),
            "y": lambda: op("V", lambda q: q.tensor_tensor_scan(T.zf[:, :], T.gs[:, 57:57 + 7 * C:16], T.gk[:, 105:105 + 7 * C:16], 0.0, A.mult, A.add),
                            ["zc", "gs", "gk", "y0", "y1", "y2", "y3", "yb"], ["zf"]),
            "f16": list_out if t >= 0 else lambda: cp(f_, T.rfi[:, :], ["rfi"], [f16]),
            "zq": upper_out, "lq": lower_quant, "O": lambda: [scaled("S", p, p, 0) for p in range(4)],
            "h": lambda: to_columns(T.hr[:, :], "hr"), "g": lambda: to_columns(T[rep][:, C:2 * C], (rep, C, 2 * C)),
            "wh": lambda: scan(T.esc[:, :], "esc", T.ew[:, :], "ew"), "wg": lambda: scan(T.gsc[:, :], "gsc", T.ew[:, :], "ew"),
            "we": lambda: scan(T.esc[:, :], "esc", T.hr[:, :], "hr"),
            "g16": lambda: held(g_, g16, T.gsc[:, 15:C:16], "gsc", down, "down", MID, []),
            "e16": lambda: held(e_, e16, T.esc[:, 15:C:16], "esc", down, "down", MID, []),
            "K": lambda: kplus("S", n1), "Kv": lambda: kplus("V", n1), "J": lambda: kplus("S", n1 + 1), "Jv": lambda: kplus("V", n1 + 1),
            "I": lambda: kplus("S", t), "Iv": lambda: kplus("V", t),
            "w1": lambda: scan(T.sp[:, 0:C], ("sp", 0, C), T.pkf[:, 0:C], ("pkf", 0, C)),
            "w0": lambda: scan(T.sp[:, C:2 * C], ("sp", C, 2 * C), T.pkf[:, C:2 * C], ("pkf", C, 2 * C)),
            "hx": lambda: held(T.x1[:, 3:176:4], ("x1", 0, 44), T.sp[:, 15:2 * C:16], "sp", half_down, "half_down", MID / 2, []),
            "hf": lambda: held(T.x1[:, 3:88:4], ("x1", 0, 22), T.sp[:, 15:C:16], ("sp", 0, C), half_down, "half_down", MID / 2, []),
            "hk": lambda: held(T.x1[:, 91:176:4], ("x1", 22, 44), T.sp[:, C + 15:2 * C:16], ("sp", C, 2 * C), half_down, "half_down", MID / 2, []),
            "hp": lambda: held(T.pka[:, c1:c1 + 22], "pk16%d" % n1, T.sp[:, C + 15:2 * C:16], ("sp", C, 2 * C), down, "down", MID, []),
            "bc": lambda: ts(T.ba[:, 0:22], f_, 0.5, None, [A.mult], [f16], [("ba", 0, 22)]),
            "ba": lambda: ts(T.ba[:, 22:66], T[cpf][:, 22:66], 0.5, None, [A.mult], [oc, f16], [("ba", 22, 66)]),
            "v": lambda: quantize(T.vq[:, :], T.vs[:, :], T.vt[:, :], ["vt"], ["vq"]),
        }
        parts["r0"] = lambda: held(T.r1[:, 88 * n1 + 2:88 * n1 + 88:4], "rx", T.sp[:, 15:C:16], ("sp", 0, C), half_down, "half_down", MID / 2, [])
        parts["r1"] = lambda: tt(T.r0[:, 1:88:4], T.x1[:, 3:88:4], T.thr[:, 66 + c1:88 + c1], A.is_ge, [("x1", 0, 22), "thr"], ["rb"])
        parts["r2"] = lambda: tt(T.r0[:, 2:88:4], T.x1[:, 3:88:4], T.thr[:, c1:c1 + 22], A.is_ge, [("x1", 0, 22), "thr"], ["ra"])
        for nm, r in (("r", n1), ("n", t)):
            parts[nm + "3"] = lambda r=r: op("V", lambda q: q.tensor_tensor_scan(T.x1[:, 176:264], T.r0[:, :], T.r1[:, 88 * r:88 * r + 88], 0.0, A.mult, A.add),
                                             ["rc", "rx", "ra", "rb", "qk"], [("x1", 44, 66)])
        pb, fb = (cpf, 22), (cpf, 44)
        both("R", (rep, 0), rep, T.idm[:, :], "idm", pb, oc)
        both("Q", (rep, C), rep, T.idm[:, :], "idm", fb, f16)
        both("P", ("pkf", C), "pkf", T[rep][:, 0:C], (rep, 0, C), ("pr16", c1), "pr16")
        both("F", ("pkf", 0), "pkf", T[rep][:, C:2 * C], (rep, C, 2 * C), ("pr16", c1), "pr16")
        if t == 2:
            parts["R"] = places_out
        if t >= 0:
            both("A", ("am", 0), "am", T.sa[:, :], "sa", ("cpf%d" % t, 22), wkey)
            both("C", ("kc", 0), "kc", T.mra[:, C * t:C * t + C], "mr%d" % t, (cpf, 0), oc)
            both("T", ("fsr", 0), "fsr", T.idm[:, :], "idm", (fs, 0), fs)
            both("H", ("hr", 0), "hr", T.fsr[:, :], "fsr", fb, f16)
            both("E", ("hr", 0), "hr", T.fsr[:, :], "fsr", ("g16a", c0), g16)
        for p in range(4):
            parts["G%d" % p] = lambda p=p: act(T.gp[:, C * p:C * p + C], T.fp[:, C * p:C * p + C].indirect(p_), ["fp%d" % p, oc], ["gp%d" % p], scale=0.5)
            parts["e%d" % p] = lambda p=p: quantize(T.eq[:, 128 * p:128 * p + 128], T.es[:, 128 * p:128 * p + 128], T.et[:, 3 - p:515 - p], ["et"], ["eq%d" % p])
            parts["F%d" % p] = lambda p=p: values(p, n1)
            parts["f%d" % p] = lambda p=p: values(p, t)
            parts["U%d" % p] = lambda p=p: unpack(t, p)
            parts["Y%d" % p] = lambda p=p: dma("Y", T.g2[:, C * p:C * p + LOW], T.gp[:, C * p:C * p + LOW], ["gp%d" % p], [("g2", C * p, C * p + LOW)])
            for nm, a in (("fa", 0), ("fb", H)):
                parts["%s%d" % (nm, p)] = lambda p=p, a=a: cp(T.fp[:, C * p + a:C * p + a + H], T["b%d" % (4 + p)][:, a:a + H], [("b%d" % (4 + p), 0, 1)], [("fp%d" % p, a, a + H)])
            parts["c%d" % p] = lambda p=p: half_copy("V", p, 0, C)
            parts["u%d" % p] = lambda p=p: half_copy("V", p, LOW, C)
            parts["m%d" % p] = lambda p=p: half_copy("V", p, 0, LOW)
            parts["L%d" % p] = lambda p=p: half_copy("S", p, 0, LOW)
            parts["N%d" % p] = lambda p=p: half_copy("S", p, LOW, C)
            parts["W%d" % p] = lambda p=p: op("G", lambda q: q.affine_select(T.g2[:, C * p + LOW:C * p + C], T.gp[:, C * p + LOW:C * p + C], [[0, C - LOW]], A.is_ge, 0.0, 1, 0),
                                              ["gp%d" % p, "Gq"], [("g2", C * p + LOW, C * p + C)])
            lo, hi, n, v = ((2, 66, 1, -1.0), (2, 66, 3, 1.0), (134, 198, 4, -1.0), (134, 198, 5, 1.0))[p]
            parts["j%d" % p] = lambda p=p, lo=lo, hi=hi, n=n, v=v: act(step(T.gk, 105, n), T.sz[:, lo:hi:3], [("sz", lo - 2, hi)], ["y%d" % p], F.Identity, scale=v, bias=-v * MID)
            parts["z%d" % p] = lambda p=p: mix(p, LOW, C)
            parts["l%d" % p] = lambda p=p: mix(p, 0, LOW)
            parts["B%d" % p] = lambda p=p: their_half("S", p)
            parts["V%d" % p] = lambda p=p: their_half("V", p)
            parts["O%d" % p] = lambda p=p: scaled("S", p, p, 0)
            parts["o%d" % p] = lambda p=p: scaled("V", p, p, 0)
            for how in "sax":
                parts["%s%d" % (how, p)] = lambda how=how, p=p: new_x(how, p, None)
            for i in range(2):
                parts["q%d" % i] = lambda i=i: quant(i)
                parts["sa%d" % i] = lambda i=i: signs(0, i)
                parts["sb%d" % i] = lambda i=i: signs(1, i)
                for how in "sax":
                    parts["%s%d%d" % (how, p, i)] = lambda how=how, p=p, i=i: new_x(how, p, i)
        return parts

    for t, names in enumerate(ORDER):
        parts = parts_of(t - 1)
        for n in names.split():
            parts[n]()
    finish()
